import numpy as np
import ml_dtypes


def mxq(x, axis, fmt="e4m3"):
    dtype, down = {"e4m3": (ml_dtypes.float8_e4m3fn, 7), "e5m2": (ml_dtypes.float8_e5m2, 14)}[fmt]
    v = np.moveaxis(np.asarray(x, np.float32).astype(ml_dtypes.bfloat16).astype(np.float64), axis, -1)
    blocks = v.reshape(v.shape[:-1] + (-1, 32))
    amax = np.abs(blocks).max(-1, keepdims=True)
    byte = np.maximum(np.where(amax > 0, np.frexp(amax)[1] - 1 + 127, 0) - down, 1)
    scale = np.exp2(byte - 127.0)
    codes = (blocks / scale).astype(np.float32).astype(dtype).astype(np.float64)
    return np.moveaxis((codes * scale).reshape(v.shape), -1, axis)


WIDE = False


def mx_kscale(k):
    if not WIDE:
        return np.ones(k)
    levels = np.array([10, -10, 5, -5, 0])
    if k % 512:
        return np.exp2(np.random.permutation(np.resize(levels, k // 32))).repeat(32)
    a = np.empty((k // 512, 16))
    for p in range(k // 512):
        a[p, :8] = np.random.permutation(np.resize(levels, 8))
        for g in range(8):
            far = levels[np.abs(levels - a[p, g]) >= 10]
            a[p, g + 8] = far[np.random.randint(len(far))]
    return np.exp2(a.ravel()).repeat(32)


def f64(x):
    return np.asarray(x).astype(np.float64)


def striped(idx):
    return np.tile(idx.reshape(-1, 16).T, (8, 1)).astype(np.uint16)


def unstriped(offs):
    return offs[:16].T.reshape(-1).astype(np.int64)


E2M1 = np.array([0.0, 0.5, 1.0, 1.5, 2.0, 3.0, 4.0, 6.0, -0.0, -0.5, -1.0, -1.5, -2.0, -3.0, -4.0, -6.0])


def pack_weight(w, fmt):
    k, n = w.shape
    w = f64(np.asarray(w, np.float32).astype(ml_dtypes.bfloat16)).reshape(k // 32, 32, n)
    amax = np.abs(w).max(1)
    if fmt == "e4m3":
        byte = np.frexp(amax)[1] - 1 + 127 - 7
    else:
        mant, ex = np.frexp(amax / 6.0)
        byte = np.where(mant > 0.5, ex, ex - 1) + 127
    byte = np.clip(np.where(amax > 0, byte, 1), 1, 254)
    scaled = (w * np.exp2(127.0 - byte)[:, None, :]).reshape(k, n).astype(np.float32)
    by_word = np.ascontiguousarray(scaled.reshape(k // 512, 128, 4, n).transpose(0, 1, 3, 2))
    if fmt == "e4m3":
        words = by_word.astype(ml_dtypes.float8_e4m3fn).view(np.uint8)
    else:
        c = by_word.astype(ml_dtypes.float4_e2m1fn).view(np.uint8) & 0xF
        words = (c[..., 0::2] | (c[..., 1::2] << 4)).reshape(k // 512, 128, 2 * n)
    return np.ascontiguousarray(words), np.ascontiguousarray(byte.astype(np.uint8).reshape(k // 512, 16, n))


def unpack_weight(words, scales, fmt):
    g, _, n = scales.shape
    words = np.ascontiguousarray(words).reshape(g, 128, n, -1)
    if fmt == "e4m3":
        vals = words.view(ml_dtypes.float8_e4m3fn).astype(np.float64)
    else:
        nib = np.empty((g, 128, n, 4), np.uint8)
        nib[..., 0::2] = words & 0xF
        nib[..., 1::2] = words >> 4
        vals = E2M1[nib]
    vals = vals * np.repeat(np.exp2(scales.astype(np.float64) - 127.0), 8, axis=1)[..., None]
    return vals.transpose(0, 1, 3, 2).reshape(g * 512, n)


def gelu(v):
    return 0.5 * v * (1.0 + np.tanh(np.sqrt(2.0 / np.pi) * (v + 0.044715 * v**3)))


K, T, S, T2, S2, N = 1024, 4096, 1024, 2048, 1024, 512

def setup_inputs():
    n = np.random.standard_normal
    s = mx_kscale(K)[:, None]
    u = mx_kscale(S)[:, None]
    tab_words, tab_scales = pack_weight(n((K, T)) * s, "e4m3")
    tab2_words, tab2_scales = pack_weight(n((K, T2)) / s / np.sqrt(K), "e4m3")
    w4_words, w4_scales = pack_weight(n((S, N)) / np.sqrt(S) / u, "e2m1")
    return {
        "tab_words": tab_words, "tab_scales": tab_scales,
        "tab2_words": tab2_words, "tab2_scales": tab2_scales,
        "offs": striped(np.random.permutation(T)[:S]),
        "offs2": striped(np.random.permutation(T2)[:S2]),
        "idf": (2.0 * np.exp(0.3 * n(S)) * u[:, 0]).astype(np.float32),
        "w4_words": w4_words, "w4_scales": w4_scales,
        "wd": (0.5 * n((S, N)) / np.sqrt(S) / u).astype(np.float32),
    }

def reference(tab_words, tab_scales, tab2_words, tab2_scales, offs, offs2, idf, w4_words, w4_scales, wd):
    v = unpack_weight(tab_words, tab_scales, "e4m3")[:, unstriped(offs)]
    v2 = unpack_weight(tab2_words, tab2_scales, "e4m3")[:, unstriped(offs2)]
    w4 = unpack_weight(w4_words, w4_scales, "e2m1")
    wdq = mxq(f64(wd), 0, "e4m3")
    A = v.T @ v2
    z = np.log(1.0 + np.maximum(A, 0.0)) * f64(idf)[:, None]
    zq = mxq(z, 0, "e4m3")
    return w4.T @ zq + wdq.T @ zq

@@ -1,0 +1,274 @@
+from contextlib import ExitStack
+
+import concourse.mybir as mybir
+
+K, T, S, T2, S2, N = 1024, 4096, 1024, 2048, 1024, 512
+FLOPS = 2 * K * S * S2 + 2 * 2 * S * N * S2
+
+F32 = mybir.dt.float32
+BF16 = mybir.dt.bfloat16
+I32 = mybir.dt.int32
+U32 = mybir.dt.uint32
+U16 = mybir.dt.uint16
+U8 = mybir.dt.uint8
+FP8X4 = mybir.dt.float8_e4m3fn_x4
+FP4X4 = mybir.dt.float4_e2m1fn_x4
+ACT = mybir.ActivationFunctionType
+ALU = mybir.AluOpType
+
+P = 128
+PACK = 4
+PASS = P * PACK
+BANK = 512
+HALF = 256
+TERM_PLANE = (0, 4)
+QUERY_PLANE = (8, 12)
+
+
+def tile_list_term_query_topics_kernel(
+    tc, tab_words, tab_scales, tab2_words, tab2_scales, offs, offs2, idf, w4_words, w4_scales, wd, out
+):
+    nc = tc.nc
+    with ExitStack() as ctx:
+        keep = ctx.enter_context(tc.tile_pool(name="keep", bufs=1))
+        work = ctx.enter_context(tc.tile_pool(name="work", bufs=2))
+        stage = ctx.enter_context(tc.tile_pool(name="stage", bufs=4))
+        psum = ctx.enter_context(tc.psum_pool(name="psum", bufs=8))
+
+        term_list = keep.tile([P, S // 16], U16, name="term_list")
+        query_list = keep.tile([P, S2 // 16], U16, name="query_list")
+        term_table = [keep.tile([P, T], I32, name=f"term_table{a}", align_bytes=64) for a in range(2)]
+        query_table = [keep.tile([P, T2], I32, name=f"query_table{a}", align_bytes=64) for a in range(2)]
+        term_scale_table = keep.tile([P, T // 4], I32, name="term_scale_table", align_bytes=64)
+        query_scale_table = keep.tile([P, T2 // 4], I32, name="query_scale_table", align_bytes=64)
+        w4_codes = keep.tile([P, 2, 2 * N // 4], I32, name="w4_codes", align_bytes=64)
+        w4_planes = keep.tile([P, 2, N // 4], I32, name="w4_planes", align_bytes=64)
+        idf_sb = keep.tile([P, 2, PACK], F32, name="idf_sb", align_bytes=64)
+        wd_raw = [keep.tile([P, PACK, N], F32, name=f"wd_raw{b}", align_bytes=64) for b in range(2)]
+        one = keep.tile([P, 1], F32, name="one")
+        warm = keep.tile([P, 1], F32, name="warm")
+
+        nc.vector.memset(query_scale_table[:], 0)
+        nc.vector.memset(term_scale_table[:], 0)
+        nc.vector.memset(w4_planes[:], 0)
+        nc.vector.memset(one[:], 1.0)
+        nc.scalar.activation(out=warm[:], in_=one[:], func=ACT.Ln)
+
+        def words_of(table, a):
+            return table[a].rearrange("p n t -> p (n t)").bitcast(I32)
+
+        nc.sync.dma_start(query_list[:], offs2)
+        nc.sync.dma_start(out=query_table[0][:], in_=words_of(tab2_words, 0))
+        nc.sync.dma_start(term_list[:], offs)
+        for q in range(4):
+            lo = 32 * q + QUERY_PLANE[0]
+            nc.gpsimd.dma_start(out=query_scale_table[lo : lo + 8, :], in_=tab2_scales[:, 4 * q : 4 * q + 4, :].bitcast(I32))
+        for q in range(4):
+            lo = 32 * q + TERM_PLANE[0]
+            nc.gpsimd.dma_start(out=term_scale_table[lo : lo + 8, :], in_=tab_scales[:, 4 * q : 4 * q + 4, :].bitcast(I32))
+        nc.sync.dma_start(out=term_table[0][:], in_=words_of(tab_words, 0))
+        nc.sync.dma_start(out=term_table[1][:], in_=words_of(tab_words, 1))
+        nc.sync.dma_start(out=query_table[1][:], in_=words_of(tab2_words, 1))
+        nc.sync.dma_start(out=idf_sb[:], in_=idf.rearrange("(b p t) -> p b t", b=2, t=PACK))
+        nc.sync.dma_start(out=wd_raw[0][:], in_=wd[0:PASS, :].rearrange("(p t) n -> p t n", t=PACK))
+        nc.sync.dma_start(out=w4_codes[:], in_=w4_words.bitcast(I32).rearrange("b p c -> p b c"))
+        for q in range(4):
+            nc.sync.dma_start(
+                out=w4_planes[32 * q : 32 * q + 4, :, :],
+                in_=w4_scales[:, 4 * q : 4 * q + 4, :].bitcast(I32).rearrange("b r c -> r b c"),
+            )
+        nc.sync.dma_start(out=wd_raw[1][:], in_=wd[PASS : 2 * PASS, :].rearrange("(p t) n -> p t n", t=PACK))
+
+        term_codes = [keep.tile([P, 2, PACK, P], U32, name=f"term_codes{a}", align_bytes=64) for a in range(2)]
+        query_codes = [keep.tile([P, S2], U32, name=f"query_codes{a}", align_bytes=64) for a in range(2)]
+        term_planes_listed = keep.tile([P, S], U8, name="term_planes_listed", align_bytes=64)
+        term_planes = keep.tile([P, 2, PACK, P], U8, name="term_planes", align_bytes=64)
+        query_planes = keep.tile([P, S2], U8, name="query_planes", align_bytes=64)
+
+        def entries(lst, h):
+            return lst[:, 32 * h : 32 * (h + 1)]
+
+        def gather_query_words(a, h):
+            nc.vector.tensor_copy(
+                query_codes[a][:, BANK * h : BANK * (h + 1)], query_table[a][:].bitcast(U32).indirect(entries(query_list, h))
+            )
+
+        def gather_query_scales(h):
+            nc.vector.tensor_copy(
+                query_planes[:, BANK * h : BANK * (h + 1)], query_scale_table[:].bitcast(U8).indirect(entries(query_list, h))
+            )
+
+        def gather_term_words(a, b):
+            nc.vector.tensor_copy(
+                term_codes[a][:, b, :, :].rearrange("p t m -> p m t"), term_table[a][:].bitcast(U32).indirect(entries(term_list, b))
+            )
+
+        def gather_term_scales(b):
+            nc.vector.tensor_copy(
+                term_planes_listed[:, PASS * b : PASS * (b + 1)], term_scale_table[:].bitcast(U8).indirect(entries(term_list, b))
+            )
+
+        def permute_term_scales(b):
+            nc.vector.tensor_copy(
+                term_planes[:, b, :, :], term_planes_listed[:, PASS * b : PASS * (b + 1)].rearrange("p (m t) -> p t m", t=PACK)
+            )
+
+        wd_codes = [keep.tile([P, N], U32, name=f"wd_codes{b}", align_bytes=64) for b in range(2)]
+        wd_planes = [keep.tile([P, N], U8, name=f"wd_planes{b}", align_bytes=64) for b in range(2)]
+        wd_grouped = [keep.tile([P, N, PACK], BF16, name=f"wd_grouped{b}", align_bytes=64) for b in range(2)]
+
+        def round_wd(b):
+            nc.vector.tensor_copy(
+                wd_grouped[b][:].rearrange("p (c i) t -> p c t i", i=4), wd_raw[b][:].rearrange("p t (c i) -> p c t i", i=4)
+            )
+
+        def quantize_wd(b):
+            nc.vector.quantize_mx(
+                out=wd_codes[b][:].bitcast(FP8X4), scales=wd_planes[b][:], in_=wd_grouped[b][:].rearrange("p n t -> p (n t)")
+            )
+
+        z_codes = [keep.tile([P, S2], U32, name=f"z_codes{b}", align_bytes=64) for b in range(2)]
+        z_planes = [keep.tile([P, S2], U8, name=f"z_planes{b}", align_bytes=64) for b in range(2)]
+
+        def matches(b, h, order=(0, 1, 2, 3)):
+            cols = slice(BANK * h, BANK * (h + 1))
+            banks = {}
+            for t in order:
+                bank = psum.tile([P, BANK], F32, name="bank")
+                for a in range(2):
+                    nc.tensor.matmul_mx(
+                        out=bank[:],
+                        lhsT=term_codes[a][:, b, t, :].bitcast(FP8X4),
+                        lhsT_scale=term_planes[TERM_PLANE[a] :, b, t, :],
+                        rhs=query_codes[a][:, cols].bitcast(FP8X4),
+                        rhs_scale=query_planes[QUERY_PLANE[a] :, cols],
+                        start=(a == 0),
+                        stop=(a == 1),
+                    )
+                banks[t] = bank
+            return banks
+
+        def drop_negatives(banks, on_vector):
+            kept = work.tile([P, PACK, BANK], F32, name="kept", align_bytes=64)
+            for t in range(PACK):
+                if t in on_vector:
+                    nc.vector.tensor_scalar(out=kept[:, t, :], in0=banks[t][:], scalar1=0.0, scalar2=None, op0=ALU.max)
+                else:
+                    nc.scalar.activation(out=kept[:, t, :], in_=banks[t][:], func=ACT.Relu)
+            return kept
+
+        def saturate(kept, pieces):
+            logs = work.tile([P, 2, BANK, 2], F32, name="logs", align_bytes=64)
+            for lo, hi in pieces:
+                nc.scalar.activation(
+                    out=logs[:, :, lo:hi, :],
+                    in_=kept[:, :, lo:hi].rearrange("p (u e) j -> p u j e", e=2),
+                    func=ACT.Ln,
+                    bias=one[:],
+                )
+            return logs
+
+        def weigh(logs, b, lo, hi):
+            z = stage.tile([P, hi - lo, 2, 2], BF16, name="z", align_bytes=64)
+            weights = idf_sb[:, b, :].rearrange("p (u e) -> p u e", u=2).unsqueeze(1).to_broadcast([P, hi - lo, 2, 2])
+            nc.vector.tensor_tensor(out=z[:], in0=logs[:, :, lo:hi, :].rearrange("p u j e -> p j u e"), in1=weights, op=ALU.mult)
+            return z
+
+        def quantize_z(z, b, h, lo, hi):
+            cols = slice(BANK * h + lo, BANK * h + hi)
+            nc.vector.quantize_mx(
+                out=z_codes[b][:, cols].bitcast(FP8X4), scales=z_planes[b][:, cols], in_=z[:].rearrange("p j u e -> p (j u e)")
+            )
+
+        def weigh_and_quantize(logs, b, h):
+            z0 = weigh(logs, b, 0, HALF)
+            z1 = weigh(logs, b, HALF, BANK)
+            quantize_z(z0, b, h, 0, HALF)
+            quantize_z(z1, b, h, HALF, BANK)
+
+        def topic_passes(sums, b, h, lo, hi):
+            cols = slice(BANK * h + lo, BANK * h + hi)
+            for nt in range(N // P):
+                rows = slice(P * nt, P * (nt + 1))
+                nc.tensor.matmul_mx(
+                    out=sums[nt][:, lo:hi],
+                    lhsT=w4_codes[:, b, :].bitcast(U8)[:, 2 * P * nt : 2 * P * (nt + 1)].bitcast(FP4X4),
+                    lhsT_scale=w4_planes[:, b, :].bitcast(U8)[:, rows],
+                    rhs=z_codes[b][:, cols].bitcast(FP8X4),
+                    rhs_scale=z_planes[b][:, cols],
+                    start=(b == 0),
+                    stop=False,
+                )
+                nc.tensor.matmul_mx(
+                    out=sums[nt][:, lo:hi],
+                    lhsT=wd_codes[b][:, rows].bitcast(FP8X4),
+                    lhsT_scale=wd_planes[b][:, rows],
+                    rhs=z_codes[b][:, cols].bitcast(FP8X4),
+                    rhs_scale=z_planes[b][:, cols],
+                    start=False,
+                    stop=(b == 1),
+                )
+
+        def store(sums, h, on_vector):
+            for nt in range(N // P):
+                result = stage.tile([P, BANK], F32, name="result", align_bytes=64)
+                if nt in on_vector:
+                    nc.vector.tensor_copy(out=result[:], in_=sums[nt][:])
+                else:
+                    nc.scalar.copy(out=result[:], in_=sums[nt][:])
+                nc.sync.dma_start(out=out[P * nt : P * (nt + 1), BANK * h : BANK * (h + 1)], in_=result[:])
+
+        halves = ((0, HALF), (HALF, BANK))
+
+        gather_query_words(0, 0)
+        gather_query_words(0, 1)
+        gather_query_scales(0)
+        gather_term_words(0, 0)
+        gather_term_words(0, 1)
+        gather_term_scales(0)
+        gather_term_scales(1)
+        permute_term_scales(0)
+        permute_term_scales(1)
+        gather_term_words(1, 0)
+        gather_term_words(1, 1)
+        gather_query_words(1, 0)
+
+        banks00 = matches(0, 0, (0, 2, 1, 3))
+        banks10 = matches(1, 0)
+        kept00 = drop_negatives(banks00, (2, 3))
+        logs00 = saturate(kept00, halves)
+        gather_query_scales(1)
+        gather_query_words(1, 1)
+        banks01 = matches(0, 1)
+        kept10 = drop_negatives(banks10, ())
+        logs10 = saturate(kept10, halves)
+        banks11 = matches(1, 1)
+        weigh_and_quantize(logs00, 0, 0)
+        round_wd(0)
+        kept01 = drop_negatives(banks01, ())
+        logs01 = saturate(kept01, halves)
+        z10 = weigh(logs10, 1, 0, HALF)
+        quantize_wd(0)
+        sums0 = [psum.tile([P, BANK], F32, name="bank") for nt in range(N // P)]
+        topic_passes(sums0, 0, 0, 0, BANK)
+        z10b = weigh(logs10, 1, HALF, BANK)
+        quantize_z(z10, 1, 0, 0, HALF)
+        round_wd(1)
+        quantize_z(z10b, 1, 0, HALF, BANK)
+        kept11 = drop_negatives(banks11, ())
+        logs11 = saturate(kept11, halves)
+        z01 = weigh(logs01, 0, 0, HALF)
+        quantize_wd(1)
+        topic_passes(sums0, 1, 0, 0, BANK)
+        z01b = weigh(logs01, 0, HALF, BANK)
+        quantize_z(z01, 0, 1, 0, HALF)
+        z11 = weigh(logs11, 1, 0, HALF)
+        quantize_z(z01b, 0, 1, HALF, BANK)
+        sums1 = [psum.tile([P, BANK], F32, name="bank") for nt in range(N // P)]
+        topic_passes(sums1, 0, 1, 0, BANK)
+        store(sums0, 0, ())
+        z11b = weigh(logs11, 1, HALF, BANK)
+        quantize_z(z11, 1, 1, 0, HALF)
+        quantize_z(z11b, 1, 1, HALF, BANK)
+        topic_passes(sums1, 1, 1, 0, BANK)
+        store(sums1, 1, (1, 3))

@@ -50,7 +50,7 @@ def tile_list_term_query_topics_kernel(
 
         nc.vector.memset(query_scale_table[:], 0)
         nc.vector.memset(term_scale_table[:], 0)
-        nc.vector.memset(w4_planes[:], 0)
+        nc.gpsimd.memset(w4_planes[:], 0)
         nc.vector.memset(one[:], 1.0)
         nc.scalar.activation(out=warm[:], in_=one[:], func=ACT.Ln)
 
@@ -58,14 +58,15 @@ def tile_list_term_query_topics_kernel(
             return table[a].rearrange("p n t -> p (n t)").bitcast(I32)
 
         nc.sync.dma_start(query_list[:], offs2)
-        nc.sync.dma_start(out=query_table[0][:], in_=words_of(tab2_words, 0))
         nc.sync.dma_start(term_list[:], offs)
         for q in range(4):
             lo = 32 * q + QUERY_PLANE[0]
-            nc.gpsimd.dma_start(out=query_scale_table[lo : lo + 8, :], in_=tab2_scales[:, 4 * q : 4 * q + 4, :].bitcast(I32))
+            nc.sync.dma_start(out=query_scale_table[lo : lo + 8, :], in_=tab2_scales[:, 4 * q : 4 * q + 4, :].bitcast(I32))
         for q in range(4):
-            lo = 32 * q + TERM_PLANE[0]
-            nc.gpsimd.dma_start(out=term_scale_table[lo : lo + 8, :], in_=tab_scales[:, 4 * q : 4 * q + 4, :].bitcast(I32))
+            for a in range(2):
+                lo = 32 * q + TERM_PLANE[a]
+                nc.sync.dma_start(out=term_scale_table[lo : lo + 4, :], in_=tab_scales[a, 4 * q : 4 * q + 4, :].bitcast(I32))
+        nc.sync.dma_start(out=query_table[0][:], in_=words_of(tab2_words, 0))
         nc.sync.dma_start(out=term_table[0][:], in_=words_of(tab_words, 0))
         nc.sync.dma_start(out=term_table[1][:], in_=words_of(tab_words, 1))
         nc.sync.dma_start(out=query_table[1][:], in_=words_of(tab2_words, 1))
@@ -220,15 +221,16 @@ def tile_list_term_query_topics_kernel(
 
         halves = ((0, HALF), (HALF, BANK))
 
-        gather_query_words(0, 0)
-        gather_query_words(0, 1)
         gather_query_scales(0)
-        gather_term_words(0, 0)
-        gather_term_words(0, 1)
         gather_term_scales(0)
         gather_term_scales(1)
+        gather_query_scales(1)
         permute_term_scales(0)
         permute_term_scales(1)
+        gather_query_words(0, 0)
+        gather_query_words(0, 1)
+        gather_term_words(0, 0)
+        gather_term_words(0, 1)
         gather_term_words(1, 0)
         gather_term_words(1, 1)
         gather_query_words(1, 0)
@@ -237,7 +239,6 @@ def tile_list_term_query_topics_kernel(
         banks10 = matches(1, 0)
         kept00 = drop_negatives(banks00, (2, 3))
         logs00 = saturate(kept00, halves)
-        gather_query_scales(1)
         gather_query_words(1, 1)
         banks01 = matches(0, 1)
         kept10 = drop_negatives(banks10, ())

@@ -31,8 +31,9 @@ def tile_list_term_query_topics_kernel(
     nc = tc.nc
     with ExitStack() as ctx:
         keep = ctx.enter_context(tc.tile_pool(name="keep", bufs=1))
-        work = ctx.enter_context(tc.tile_pool(name="work", bufs=2))
-        stage = ctx.enter_context(tc.tile_pool(name="stage", bufs=4))
+        work = ctx.enter_context(tc.tile_pool(name="work", bufs=4))
+        stage = ctx.enter_context(tc.tile_pool(name="stage", bufs=8))
+        rounded = ctx.enter_context(tc.tile_pool(name="rounded", bufs=3))
         psum = ctx.enter_context(tc.psum_pool(name="psum", bufs=8))
 
         term_list = keep.tile([P, S // 16], U16, name="term_list")
@@ -58,15 +59,20 @@ def tile_list_term_query_topics_kernel(
             return table[a].rearrange("p n t -> p (n t)").bitcast(I32)
 
         nc.sync.dma_start(query_list[:], offs2)
-        nc.sync.dma_start(term_list[:], offs)
-        for q in range(4):
-            lo = 32 * q + QUERY_PLANE[0]
-            nc.sync.dma_start(out=query_scale_table[lo : lo + 8, :], in_=tab2_scales[:, 4 * q : 4 * q + 4, :].bitcast(I32))
-        for q in range(4):
-            for a in range(2):
-                lo = 32 * q + TERM_PLANE[a]
-                nc.sync.dma_start(out=term_scale_table[lo : lo + 4, :], in_=tab_scales[a, 4 * q : 4 * q + 4, :].bitcast(I32))
         nc.sync.dma_start(out=query_table[0][:], in_=words_of(tab2_words, 0))
+        nc.sync.dma_start(out=query_scale_table[32 * 0 + QUERY_PLANE[0] : 32 * 0 + QUERY_PLANE[0] + 8, :], in_=tab2_scales[:, 4 * 0 : 4 * 0 + 4, :].bitcast(I32))
+        nc.sync.dma_start(out=query_scale_table[32 * 1 + QUERY_PLANE[0] : 32 * 1 + QUERY_PLANE[0] + 8, :], in_=tab2_scales[:, 4 * 1 : 4 * 1 + 4, :].bitcast(I32))
+        nc.sync.dma_start(out=query_scale_table[32 * 2 + QUERY_PLANE[0] : 32 * 2 + QUERY_PLANE[0] + 8, :], in_=tab2_scales[:, 4 * 2 : 4 * 2 + 4, :].bitcast(I32))
+        nc.sync.dma_start(out=query_scale_table[32 * 3 + QUERY_PLANE[0] : 32 * 3 + QUERY_PLANE[0] + 8, :], in_=tab2_scales[:, 4 * 3 : 4 * 3 + 4, :].bitcast(I32))
+        nc.sync.dma_start(out=term_scale_table[32 * 0 + TERM_PLANE[0] : 32 * 0 + TERM_PLANE[0] + 4, :], in_=tab_scales[0, 4 * 0 : 4 * 0 + 4, :].bitcast(I32))
+        nc.sync.dma_start(out=term_scale_table[32 * 0 + TERM_PLANE[1] : 32 * 0 + TERM_PLANE[1] + 4, :], in_=tab_scales[1, 4 * 0 : 4 * 0 + 4, :].bitcast(I32))
+        nc.sync.dma_start(out=term_scale_table[32 * 1 + TERM_PLANE[0] : 32 * 1 + TERM_PLANE[0] + 4, :], in_=tab_scales[0, 4 * 1 : 4 * 1 + 4, :].bitcast(I32))
+        nc.sync.dma_start(out=term_scale_table[32 * 1 + TERM_PLANE[1] : 32 * 1 + TERM_PLANE[1] + 4, :], in_=tab_scales[1, 4 * 1 : 4 * 1 + 4, :].bitcast(I32))
+        nc.sync.dma_start(out=term_scale_table[32 * 2 + TERM_PLANE[0] : 32 * 2 + TERM_PLANE[0] + 4, :], in_=tab_scales[0, 4 * 2 : 4 * 2 + 4, :].bitcast(I32))
+        nc.sync.dma_start(out=term_scale_table[32 * 2 + TERM_PLANE[1] : 32 * 2 + TERM_PLANE[1] + 4, :], in_=tab_scales[1, 4 * 2 : 4 * 2 + 4, :].bitcast(I32))
+        nc.sync.dma_start(out=term_scale_table[32 * 3 + TERM_PLANE[0] : 32 * 3 + TERM_PLANE[0] + 4, :], in_=tab_scales[0, 4 * 3 : 4 * 3 + 4, :].bitcast(I32))
+        nc.sync.dma_start(out=term_scale_table[32 * 3 + TERM_PLANE[1] : 32 * 3 + TERM_PLANE[1] + 4, :], in_=tab_scales[1, 4 * 3 : 4 * 3 + 4, :].bitcast(I32))
+        nc.sync.dma_start(term_list[:], offs)
         nc.sync.dma_start(out=term_table[0][:], in_=words_of(tab_words, 0))
         nc.sync.dma_start(out=term_table[1][:], in_=words_of(tab_words, 1))
         nc.sync.dma_start(out=query_table[1][:], in_=words_of(tab2_words, 1))
@@ -116,160 +122,211 @@ def tile_list_term_query_topics_kernel(
 
         wd_codes = [keep.tile([P, N], U32, name=f"wd_codes{b}", align_bytes=64) for b in range(2)]
         wd_planes = [keep.tile([P, N], U8, name=f"wd_planes{b}", align_bytes=64) for b in range(2)]
-        wd_grouped = [keep.tile([P, N, PACK], BF16, name=f"wd_grouped{b}", align_bytes=64) for b in range(2)]
 
         def round_wd(b):
-            nc.vector.tensor_copy(
-                wd_grouped[b][:].rearrange("p (c i) t -> p c t i", i=4), wd_raw[b][:].rearrange("p t (c i) -> p c t i", i=4)
-            )
+            grouped = rounded.tile([P, N, PACK], BF16, name="grouped", align_bytes=64)
+            nc.vector.tensor_copy(grouped[:].rearrange("p (c i) t -> p c t i", i=4), wd_raw[b][:].rearrange("p t (c i) -> p c t i", i=4))
+            return grouped
 
-        def quantize_wd(b):
-            nc.vector.quantize_mx(
-                out=wd_codes[b][:].bitcast(FP8X4), scales=wd_planes[b][:], in_=wd_grouped[b][:].rearrange("p n t -> p (n t)")
-            )
+        def quantize_wd(grouped, b):
+            nc.vector.quantize_mx(out=wd_codes[b][:].bitcast(FP8X4), scales=wd_planes[b][:], in_=grouped[:].rearrange("p n t -> p (n t)"))
 
         z_codes = [keep.tile([P, S2], U32, name=f"z_codes{b}", align_bytes=64) for b in range(2)]
         z_planes = [keep.tile([P, S2], U8, name=f"z_planes{b}", align_bytes=64) for b in range(2)]
 
-        def matches(b, h, order=(0, 1, 2, 3)):
-            cols = slice(BANK * h, BANK * (h + 1))
-            banks = {}
-            for t in order:
-                bank = psum.tile([P, BANK], F32, name="bank")
-                for a in range(2):
-                    nc.tensor.matmul_mx(
-                        out=bank[:],
-                        lhsT=term_codes[a][:, b, t, :].bitcast(FP8X4),
-                        lhsT_scale=term_planes[TERM_PLANE[a] :, b, t, :],
-                        rhs=query_codes[a][:, cols].bitcast(FP8X4),
-                        rhs_scale=query_planes[QUERY_PLANE[a] :, cols],
-                        start=(a == 0),
-                        stop=(a == 1),
-                    )
-                banks[t] = bank
+        def matches(b, lo, hi):
+            width = hi - lo
+            per_bank = BANK // width
+            banks = []
+            for first in range(0, PACK, per_bank):
+                bank = psum.tile([P, per_bank, width], F32, name="bank")
+                for e in range(per_bank):
+                    for a in range(2):
+                        nc.tensor.matmul_mx(
+                            out=bank[:, e, :],
+                            lhsT=term_codes[a][:, b, first + e, :].bitcast(FP8X4),
+                            lhsT_scale=term_planes[TERM_PLANE[a] :, b, first + e, :],
+                            rhs=query_codes[a][:, lo:hi].bitcast(FP8X4),
+                            rhs_scale=query_planes[QUERY_PLANE[a] :, lo:hi],
+                            start=(a == 0),
+                            stop=(a == 1),
+                        )
+                banks.append(bank)
             return banks
 
         def drop_negatives(banks, on_vector):
-            kept = work.tile([P, PACK, BANK], F32, name="kept", align_bytes=64)
-            for t in range(PACK):
-                if t in on_vector:
-                    nc.vector.tensor_scalar(out=kept[:, t, :], in0=banks[t][:], scalar1=0.0, scalar2=None, op0=ALU.max)
+            per_bank, width = banks[0].shape[1:]
+            kept = work.tile([P, len(banks), width, per_bank], F32, name="kept", align_bytes=64)
+            for i, bank in enumerate(banks):
+                side_by_side = bank[:].rearrange("p e j -> p j e")
+                if i in on_vector:
+                    nc.vector.tensor_scalar(out=kept[:, i, :, :], in0=side_by_side, scalar1=0.0, scalar2=None, op0=ALU.max)
                 else:
-                    nc.scalar.activation(out=kept[:, t, :], in_=banks[t][:], func=ACT.Relu)
+                    nc.scalar.activation(out=kept[:, i, :, :], in_=side_by_side, func=ACT.Relu)
             return kept
 
-        def saturate(kept, pieces):
-            logs = work.tile([P, 2, BANK, 2], F32, name="logs", align_bytes=64)
-            for lo, hi in pieces:
-                nc.scalar.activation(
-                    out=logs[:, :, lo:hi, :],
-                    in_=kept[:, :, lo:hi].rearrange("p (u e) j -> p u j e", e=2),
-                    func=ACT.Ln,
-                    bias=one[:],
-                )
+        def saturate(kept, lo, hi):
+            runs = min(kept.shape[1], 2)
+            logs = work.tile([P, runs, hi - lo, PACK // runs], F32, name="logs", align_bytes=64)
+            if kept.shape[1] == PACK:
+                source = kept[:, :, lo:hi, 0].rearrange("p (u e) j -> p u j e", e=2)
+            else:
+                source = kept[:, :, lo:hi, :]
+            nc.scalar.activation(out=logs[:], in_=source, func=ACT.Ln, bias=one[:])
             return logs
 
-        def weigh(logs, b, lo, hi):
-            z = stage.tile([P, hi - lo, 2, 2], BF16, name="z", align_bytes=64)
-            weights = idf_sb[:, b, :].rearrange("p (u e) -> p u e", u=2).unsqueeze(1).to_broadcast([P, hi - lo, 2, 2])
-            nc.vector.tensor_tensor(out=z[:], in0=logs[:, :, lo:hi, :].rearrange("p u j e -> p j u e"), in1=weights, op=ALU.mult)
+        def weigh(logs, b):
+            runs, width, per_run = logs.shape[1:]
+            z = rounded.tile([P, width, runs, per_run], BF16, name="grouped", align_bytes=64)
+            weights = idf_sb[:, b, :].rearrange("p (u e) -> p u e", u=runs).unsqueeze(1).to_broadcast([P, width, runs, per_run])
+            nc.vector.tensor_tensor(out=z[:], in0=logs[:].rearrange("p u j e -> p j u e"), in1=weights, op=ALU.mult)
             return z
 
-        def quantize_z(z, b, h, lo, hi):
-            cols = slice(BANK * h + lo, BANK * h + hi)
+        def quantize_z(z, b, lo):
+            cols = slice(lo, lo + z.shape[1])
             nc.vector.quantize_mx(
                 out=z_codes[b][:, cols].bitcast(FP8X4), scales=z_planes[b][:, cols], in_=z[:].rearrange("p j u e -> p (j u e)")
             )
 
-        def weigh_and_quantize(logs, b, h):
-            z0 = weigh(logs, b, 0, HALF)
-            z1 = weigh(logs, b, HALF, BANK)
-            quantize_z(z0, b, h, 0, HALF)
-            quantize_z(z1, b, h, HALF, BANK)
+        def packed_pass(acc, nt, b, lo, hi):
+            nc.tensor.matmul_mx(
+                out=acc,
+                lhsT=w4_codes[:, b, :].bitcast(U8)[:, 2 * P * nt : 2 * P * (nt + 1)].bitcast(FP4X4),
+                lhsT_scale=w4_planes[:, b, :].bitcast(U8)[:, P * nt : P * (nt + 1)],
+                rhs=z_codes[b][:, lo:hi].bitcast(FP8X4),
+                rhs_scale=z_planes[b][:, lo:hi],
+                start=(b == 0),
+                stop=False,
+            )
 
-        def topic_passes(sums, b, h, lo, hi):
-            cols = slice(BANK * h + lo, BANK * h + hi)
+        def update_pass(acc, nt, b, lo, hi):
+            nc.tensor.matmul_mx(
+                out=acc,
+                lhsT=wd_codes[b][:, P * nt : P * (nt + 1)].bitcast(FP8X4),
+                lhsT_scale=wd_planes[b][:, P * nt : P * (nt + 1)],
+                rhs=z_codes[b][:, lo:hi].bitcast(FP8X4),
+                rhs_scale=z_planes[b][:, lo:hi],
+                start=False,
+                stop=(b == 1),
+            )
+
+        def open_sums(lo, hi):
+            sums = [psum.tile([P, 1, hi - lo], F32, name="bank") for nt in range(N // P)]
+            for one_pass in (packed_pass, update_pass):
+                for nt in range(N // P):
+                    one_pass(sums[nt][:, 0, :], nt, 0, lo, hi)
+            return sums
+
+        def close_sums(sums, lo, hi):
             for nt in range(N // P):
-                rows = slice(P * nt, P * (nt + 1))
-                nc.tensor.matmul_mx(
-                    out=sums[nt][:, lo:hi],
-                    lhsT=w4_codes[:, b, :].bitcast(U8)[:, 2 * P * nt : 2 * P * (nt + 1)].bitcast(FP4X4),
-                    lhsT_scale=w4_planes[:, b, :].bitcast(U8)[:, rows],
-                    rhs=z_codes[b][:, cols].bitcast(FP8X4),
-                    rhs_scale=z_planes[b][:, cols],
-                    start=(b == 0),
-                    stop=False,
-                )
-                nc.tensor.matmul_mx(
-                    out=sums[nt][:, lo:hi],
-                    lhsT=wd_codes[b][:, rows].bitcast(FP8X4),
-                    lhsT_scale=wd_planes[b][:, rows],
-                    rhs=z_codes[b][:, cols].bitcast(FP8X4),
-                    rhs_scale=z_planes[b][:, cols],
-                    start=False,
-                    stop=(b == 1),
-                )
+                packed_pass(sums[nt][:, 0, :], nt, 1, lo, hi)
+                update_pass(sums[nt][:, 0, :], nt, 1, lo, hi)
 
-        def store(sums, h, on_vector):
-            for nt in range(N // P):
-                result = stage.tile([P, BANK], F32, name="result", align_bytes=64)
-                if nt in on_vector:
-                    nc.vector.tensor_copy(out=result[:], in_=sums[nt][:])
-                else:
-                    nc.scalar.copy(out=result[:], in_=sums[nt][:])
-                nc.sync.dma_start(out=out[P * nt : P * (nt + 1), BANK * h : BANK * (h + 1)], in_=result[:])
+        def packed_sums(lo, hi):
+            tiles_per_bank = BANK // (hi - lo)
+            sums = []
+            for first in range(0, N // P, tiles_per_bank):
+                bank = psum.tile([P, tiles_per_bank, hi - lo], F32, name="bank")
+                for e in range(tiles_per_bank):
+                    for c in range(0, hi - lo, P):
+                        for b in range(2):
+                            packed_pass(bank[:, e, c : c + P], first + e, b, lo + c, lo + c + P)
+                            update_pass(bank[:, e, c : c + P], first + e, b, lo + c, lo + c + P)
+                sums.append(bank)
+            return sums
 
-        halves = ((0, HALF), (HALF, BANK))
+        def leave(result, bank, on_vector):
+            if on_vector:
+                nc.vector.tensor_copy(out=result, in_=bank[:])
+            else:
+                nc.scalar.copy(out=result, in_=bank[:])
 
+        def store(sums, lo, hi, on_vector):
+            for i, bank in enumerate(sums):
+                tiles = bank.shape[1]
+                result = stage.tile([P, tiles, hi - lo], F32, name="result", align_bytes=64)
+                leave(result[:], bank, i in on_vector)
+                rows = out[P * tiles * i : P * tiles * (i + 1), lo:hi]
+                nc.sync.dma_start(out=rows.rearrange("(e p) j -> p e j", p=P), in_=result[:])
+
+        def store_together(sums, lo, hi, on_vector):
+            result = stage.tile([P, len(sums), hi - lo], F32, name="result", align_bytes=64)
+            for i, bank in enumerate(sums):
+                leave(result[:, i : i + 1, :], bank, i in on_vector)
+            nc.sync.dma_start(out=out[:, lo:hi].rearrange("(e p) j -> p e j", p=P), in_=result[:])
+
+        gather_query_words(0, 0)
+        gather_query_words(0, 1)
         gather_query_scales(0)
         gather_term_scales(0)
         gather_term_scales(1)
         gather_query_scales(1)
         permute_term_scales(0)
         permute_term_scales(1)
-        gather_query_words(0, 0)
-        gather_query_words(0, 1)
         gather_term_words(0, 0)
         gather_term_words(0, 1)
         gather_term_words(1, 0)
         gather_term_words(1, 1)
         gather_query_words(1, 0)
 
-        banks00 = matches(0, 0, (0, 2, 1, 3))
-        banks10 = matches(1, 0)
-        kept00 = drop_negatives(banks00, (2, 3))
-        logs00 = saturate(kept00, halves)
+        m00 = matches(0, 0, 512)
+        m10 = matches(1, 0, 512)
+        k00 = drop_negatives(m00, ())
+        l00a = saturate(k00, 0, 256)
+        l00b = saturate(k00, 256, 512)
         gather_query_words(1, 1)
-        banks01 = matches(0, 1)
-        kept10 = drop_negatives(banks10, ())
-        logs10 = saturate(kept10, halves)
-        banks11 = matches(1, 1)
-        weigh_and_quantize(logs00, 0, 0)
-        round_wd(0)
-        kept01 = drop_negatives(banks01, ())
-        logs01 = saturate(kept01, halves)
-        z10 = weigh(logs10, 1, 0, HALF)
-        quantize_wd(0)
-        sums0 = [psum.tile([P, BANK], F32, name="bank") for nt in range(N // P)]
-        topic_passes(sums0, 0, 0, 0, BANK)
-        z10b = weigh(logs10, 1, HALF, BANK)
-        quantize_z(z10, 1, 0, 0, HALF)
-        round_wd(1)
-        quantize_z(z10b, 1, 0, HALF, BANK)
-        kept11 = drop_negatives(banks11, ())
-        logs11 = saturate(kept11, halves)
-        z01 = weigh(logs01, 0, 0, HALF)
-        quantize_wd(1)
-        topic_passes(sums0, 1, 0, 0, BANK)
-        z01b = weigh(logs01, 0, HALF, BANK)
-        quantize_z(z01, 0, 1, 0, HALF)
-        z11 = weigh(logs11, 1, 0, HALF)
-        quantize_z(z01b, 0, 1, HALF, BANK)
-        sums1 = [psum.tile([P, BANK], F32, name="bank") for nt in range(N // P)]
-        topic_passes(sums1, 0, 1, 0, BANK)
-        store(sums0, 0, ())
-        z11b = weigh(logs11, 1, HALF, BANK)
-        quantize_z(z11, 1, 1, 0, HALF)
-        quantize_z(z11b, 1, 1, HALF, BANK)
-        topic_passes(sums1, 1, 1, 0, BANK)
-        store(sums1, 1, (1, 3))
+        m01 = matches(0, 512, 768)
+        m11 = matches(1, 512, 768)
+        g0 = round_wd(0)
+        k10 = drop_negatives(m10, (0, 1))
+        l10a = saturate(k10, 0, 256)
+        l10b = saturate(k10, 256, 512)
+        m02 = matches(0, 768, 896)
+        m12 = matches(1, 768, 896)
+        quantize_wd(g0, 0)
+        z00a = weigh(l00a, 0)
+        z00b = weigh(l00b, 0)
+        quantize_z(z00a, 0, 0)
+        quantize_z(z00b, 0, 256)
+        k01 = drop_negatives(m01, ())
+        l01 = saturate(k01, 0, 256)
+        s0 = open_sums(0, 512)
+        z10a = weigh(l10a, 1)
+        z10b = weigh(l10b, 1)
+        g1 = round_wd(1)
+        quantize_z(z10a, 1, 0)
+        quantize_z(z10b, 1, 256)
+        quantize_wd(g1, 1)
+        k11 = drop_negatives(m11, ())
+        l11 = saturate(k11, 0, 256)
+        m03 = matches(0, 896, 1024)
+        m13 = matches(1, 896, 1024)
+        close_sums(s0, 0, 512)
+        z01 = weigh(l01, 0)
+        z11 = weigh(l11, 1)
+        quantize_z(z01, 0, 512)
+        quantize_z(z11, 1, 512)
+        k02 = drop_negatives(m02, ())
+        l02 = saturate(k02, 0, 128)
+        k12 = drop_negatives(m12, ())
+        l12 = saturate(k12, 0, 128)
+        store(s0, 0, 512, (1, 3))
+        s1 = packed_sums(512, 768)
+        z02 = weigh(l02, 0)
+        z12 = weigh(l12, 1)
+        quantize_z(z02, 0, 768)
+        quantize_z(z12, 1, 768)
+        k03 = drop_negatives(m03, ())
+        l03 = saturate(k03, 0, 128)
+        k13 = drop_negatives(m13, ())
+        l13 = saturate(k13, 0, 128)
+        s2 = packed_sums(768, 896)
+        z03 = weigh(l03, 0)
+        z13 = weigh(l13, 1)
+        quantize_z(z03, 0, 896)
+        s3 = open_sums(896, 1024)
+        quantize_z(z13, 1, 896)
+        close_sums(s3, 896, 1024)
+        store(s1, 512, 768, ())
+        store(s2, 768, 896, ())
+        store_together(s3, 896, 1024, (1, 3))

@@ -20,9 +20,9 @@ P = 128
 PACK = 4
 PASS = P * PACK
 BANK = 512
-HALF = 256
-TERM_PLANE = (0, 4)
-QUERY_PLANE = (8, 12)
+CHUNK = 256
+ROWS = 32
+KIB = 1024
 
 
 def tile_list_term_query_topics_kernel(
@@ -31,52 +31,72 @@ def tile_list_term_query_topics_kernel(
     nc = tc.nc
     with ExitStack() as ctx:
         keep = ctx.enter_context(tc.tile_pool(name="keep", bufs=1))
-        work = ctx.enter_context(tc.tile_pool(name="work", bufs=4))
+        shared = ctx.enter_context(tc.tile_pool(name="shared", bufs=1))
+        work = ctx.enter_context(tc.tile_pool(name="work", bufs=3))
         stage = ctx.enter_context(tc.tile_pool(name="stage", bufs=8))
         rounded = ctx.enter_context(tc.tile_pool(name="rounded", bufs=3))
-        psum = ctx.enter_context(tc.psum_pool(name="psum", bufs=8))
+        psum = ctx.enter_context(tc.psum_pool(name="psum", bufs=1))
 
         term_list = keep.tile([P, S // 16], U16, name="term_list")
         query_list = keep.tile([P, S2 // 16], U16, name="query_list")
-        term_table = [keep.tile([P, T], I32, name=f"term_table{a}", align_bytes=64) for a in range(2)]
-        query_table = [keep.tile([P, T2], I32, name=f"query_table{a}", align_bytes=64) for a in range(2)]
         term_scale_table = keep.tile([P, T // 4], I32, name="term_scale_table", align_bytes=64)
         query_scale_table = keep.tile([P, T2 // 4], I32, name="query_scale_table", align_bytes=64)
-        w4_codes = keep.tile([P, 2, 2 * N // 4], I32, name="w4_codes", align_bytes=64)
-        w4_planes = keep.tile([P, 2, N // 4], I32, name="w4_planes", align_bytes=64)
-        idf_sb = keep.tile([P, 2, PACK], F32, name="idf_sb", align_bytes=64)
-        wd_raw = [keep.tile([P, PACK, N], F32, name=f"wd_raw{b}", align_bytes=64) for b in range(2)]
+        planes = [keep.tile([P, (S + S2) // 4], I32, name=f"planes{a}", align_bytes=64) for a in range(2)]
         one = keep.tile([P, 1], F32, name="one")
         warm = keep.tile([P, 1], F32, name="warm")
+        query_table = shared.tile([P, 2, T2], I32, name="query_table", align_bytes=64, offset=0)
+        term_table = [shared.tile([P, T], I32, name=f"term_table{a}", align_bytes=64, offset=16 * KIB * (a + 1)) for a in range(2)]
 
-        nc.vector.memset(query_scale_table[:], 0)
-        nc.vector.memset(term_scale_table[:], 0)
-        nc.gpsimd.memset(w4_planes[:], 0)
         nc.vector.memset(one[:], 1.0)
         nc.scalar.activation(out=warm[:], in_=one[:], func=ACT.Ln)
-
-        def words_of(table, a):
-            return table[a].rearrange("p n t -> p (n t)").bitcast(I32)
+        for table in (query_scale_table, term_scale_table):
+            nc.vector.memset(table[32:64, :], 0)
+            nc.vector.memset(table[64:128, :], 0)
+        nc.gpsimd.memset(planes[1][:], 0)
 
         nc.sync.dma_start(query_list[:], offs2)
-        nc.sync.dma_start(out=query_table[0][:], in_=words_of(tab2_words, 0))
-        nc.sync.dma_start(out=query_scale_table[32 * 0 + QUERY_PLANE[0] : 32 * 0 + QUERY_PLANE[0] + 8, :], in_=tab2_scales[:, 4 * 0 : 4 * 0 + 4, :].bitcast(I32))
-        nc.sync.dma_start(out=query_scale_table[32 * 1 + QUERY_PLANE[0] : 32 * 1 + QUERY_PLANE[0] + 8, :], in_=tab2_scales[:, 4 * 1 : 4 * 1 + 4, :].bitcast(I32))
-        nc.sync.dma_start(out=query_scale_table[32 * 2 + QUERY_PLANE[0] : 32 * 2 + QUERY_PLANE[0] + 8, :], in_=tab2_scales[:, 4 * 2 : 4 * 2 + 4, :].bitcast(I32))
-        nc.sync.dma_start(out=query_scale_table[32 * 3 + QUERY_PLANE[0] : 32 * 3 + QUERY_PLANE[0] + 8, :], in_=tab2_scales[:, 4 * 3 : 4 * 3 + 4, :].bitcast(I32))
-        nc.sync.dma_start(out=term_scale_table[32 * 0 + TERM_PLANE[0] : 32 * 0 + TERM_PLANE[0] + 4, :], in_=tab_scales[0, 4 * 0 : 4 * 0 + 4, :].bitcast(I32))
-        nc.sync.dma_start(out=term_scale_table[32 * 0 + TERM_PLANE[1] : 32 * 0 + TERM_PLANE[1] + 4, :], in_=tab_scales[1, 4 * 0 : 4 * 0 + 4, :].bitcast(I32))
-        nc.sync.dma_start(out=term_scale_table[32 * 1 + TERM_PLANE[0] : 32 * 1 + TERM_PLANE[0] + 4, :], in_=tab_scales[0, 4 * 1 : 4 * 1 + 4, :].bitcast(I32))
-        nc.sync.dma_start(out=term_scale_table[32 * 1 + TERM_PLANE[1] : 32 * 1 + TERM_PLANE[1] + 4, :], in_=tab_scales[1, 4 * 1 : 4 * 1 + 4, :].bitcast(I32))
-        nc.sync.dma_start(out=term_scale_table[32 * 2 + TERM_PLANE[0] : 32 * 2 + TERM_PLANE[0] + 4, :], in_=tab_scales[0, 4 * 2 : 4 * 2 + 4, :].bitcast(I32))
-        nc.sync.dma_start(out=term_scale_table[32 * 2 + TERM_PLANE[1] : 32 * 2 + TERM_PLANE[1] + 4, :], in_=tab_scales[1, 4 * 2 : 4 * 2 + 4, :].bitcast(I32))
-        nc.sync.dma_start(out=term_scale_table[32 * 3 + TERM_PLANE[0] : 32 * 3 + TERM_PLANE[0] + 4, :], in_=tab_scales[0, 4 * 3 : 4 * 3 + 4, :].bitcast(I32))
-        nc.sync.dma_start(out=term_scale_table[32 * 3 + TERM_PLANE[1] : 32 * 3 + TERM_PLANE[1] + 4, :], in_=tab_scales[1, 4 * 3 : 4 * 3 + 4, :].bitcast(I32))
         nc.sync.dma_start(term_list[:], offs)
-        nc.sync.dma_start(out=term_table[0][:], in_=words_of(tab_words, 0))
-        nc.sync.dma_start(out=term_table[1][:], in_=words_of(tab_words, 1))
-        nc.sync.dma_start(out=query_table[1][:], in_=words_of(tab2_words, 1))
-        nc.sync.dma_start(out=idf_sb[:], in_=idf.rearrange("(b p t) -> p b t", b=2, t=PACK))
+        nc.sync.dma_start(out=query_scale_table[0:ROWS, :], in_=tab2_scales.rearrange("a q n -> (a q) n").bitcast(I32))
+        nc.sync.dma_start(out=term_scale_table[0:ROWS, :], in_=tab_scales.rearrange("a q n -> (a q) n").bitcast(I32))
+        nc.sync.dma_start(out=query_table[:], in_=tab2_words.rearrange("a p n t -> p a (n t)").bitcast(I32))
+        for a in range(2):
+            nc.sync.dma_start(out=term_table[a][:], in_=tab_words[a].rearrange("p n t -> p (n t)").bitcast(I32))
+
+        term_codes = [keep.tile([P, 2, PACK, P], U32, name=f"term_codes{a}", align_bytes=64) for a in range(2)]
+        query_codes = [keep.tile([P, S2], U32, name=f"query_codes{a}", align_bytes=64) for a in range(2)]
+        term_scales = shared.tile([P, S], U8, name="term_scales", align_bytes=64, offset=48 * KIB)
+        query_scales = keep.tile([P, S2], U8, name="query_scales", align_bytes=64)
+
+        nc.vector.tensor_copy(query_scales[:], query_scale_table[:].bitcast(U8).indirect(query_list[:]))
+        nc.vector.tensor_copy(term_scales[:], term_scale_table[:].bitcast(U8).indirect(term_list[:]))
+        nc.vector.tensor_copy(planes[0][:, S // 4 :], query_scales[:].bitcast(I32))
+        nc.vector.tensor_copy(
+            planes[0][:, 0 : S // 4].bitcast(U8).rearrange("p (b t m) -> p b t m", b=2, t=PACK),
+            term_scales[:].rearrange("p (b m t) -> p b t m", b=2, t=PACK),
+        )
+        for a in range(2):
+            for q in range(1 - a, 4):
+                first = 16 * a + 4 * q
+                nc.scalar.dma_start(out=planes[a][32 * q : 32 * q + 4, :], in_=planes[0][first : first + 4, :])
+        idf_sb = shared.tile([P, 2, PACK], F32, name="idf_sb", align_bytes=64, offset=48 * KIB)
+        nc.scalar.dma_start(out=idf_sb[:], in_=idf.rearrange("(b p t) -> p b t", b=2, t=PACK))
+
+        for a in range(2):
+            nc.vector.tensor_copy(query_codes[a][:], query_table[:, a, :].bitcast(U32).indirect(query_list[:]))
+
+        def gather_term_words(a, b):
+            nc.vector.tensor_copy(
+                term_codes[a][:, b, :, :].rearrange("p t m -> p m t"),
+                term_table[a][:].bitcast(U32).indirect(term_list[:, 32 * b : 32 * (b + 1)]),
+            )
+
+        gather_term_words(0, 0)
+        gather_term_words(0, 1)
+
+        wd_raw = [shared.tile([P, PACK, N], F32, name=f"wd_raw{b}", align_bytes=64, offset=16 * KIB * b) for b in range(2)]
+        w4_codes = shared.tile([P, 2, 2 * N // 4], I32, name="w4_codes", align_bytes=64, offset=24 * KIB)
+        w4_planes = shared.tile([P, 2, N // 4], I32, name="w4_planes", align_bytes=64, offset=26 * KIB)
+        nc.vector.memset(w4_planes[:], 0)
         nc.sync.dma_start(out=wd_raw[0][:], in_=wd[0:PASS, :].rearrange("(p t) n -> p t n", t=PACK))
         nc.sync.dma_start(out=w4_codes[:], in_=w4_words.bitcast(I32).rearrange("b p c -> p b c"))
         for q in range(4):
@@ -86,42 +106,13 @@ def tile_list_term_query_topics_kernel(
             )
         nc.sync.dma_start(out=wd_raw[1][:], in_=wd[PASS : 2 * PASS, :].rearrange("(p t) n -> p t n", t=PACK))
 
-        term_codes = [keep.tile([P, 2, PACK, P], U32, name=f"term_codes{a}", align_bytes=64) for a in range(2)]
-        query_codes = [keep.tile([P, S2], U32, name=f"query_codes{a}", align_bytes=64) for a in range(2)]
-        term_planes_listed = keep.tile([P, S], U8, name="term_planes_listed", align_bytes=64)
-        term_planes = keep.tile([P, 2, PACK, P], U8, name="term_planes", align_bytes=64)
-        query_planes = keep.tile([P, S2], U8, name="query_planes", align_bytes=64)
-
-        def entries(lst, h):
-            return lst[:, 32 * h : 32 * (h + 1)]
-
-        def gather_query_words(a, h):
-            nc.vector.tensor_copy(
-                query_codes[a][:, BANK * h : BANK * (h + 1)], query_table[a][:].bitcast(U32).indirect(entries(query_list, h))
-            )
-
-        def gather_query_scales(h):
-            nc.vector.tensor_copy(
-                query_planes[:, BANK * h : BANK * (h + 1)], query_scale_table[:].bitcast(U8).indirect(entries(query_list, h))
-            )
-
-        def gather_term_words(a, b):
-            nc.vector.tensor_copy(
-                term_codes[a][:, b, :, :].rearrange("p t m -> p m t"), term_table[a][:].bitcast(U32).indirect(entries(term_list, b))
-            )
-
-        def gather_term_scales(b):
-            nc.vector.tensor_copy(
-                term_planes_listed[:, PASS * b : PASS * (b + 1)], term_scale_table[:].bitcast(U8).indirect(entries(term_list, b))
-            )
-
-        def permute_term_scales(b):
-            nc.vector.tensor_copy(
-                term_planes[:, b, :, :], term_planes_listed[:, PASS * b : PASS * (b + 1)].rearrange("p (m t) -> p t m", t=PACK)
-            )
-
         wd_codes = [keep.tile([P, N], U32, name=f"wd_codes{b}", align_bytes=64) for b in range(2)]
         wd_planes = [keep.tile([P, N], U8, name=f"wd_planes{b}", align_bytes=64) for b in range(2)]
+        z_codes = [keep.tile([P, S2], U32, name=f"z_codes{b}", align_bytes=64) for b in range(2)]
+        z_planes = [keep.tile([P, S2], U8, name=f"z_planes{b}", align_bytes=64) for b in range(2)]
+
+        def bank_tile(number, parts):
+            return psum.tile([P, parts, BANK // parts], F32, name="bank", tag=f"bank{number}")
 
         def round_wd(b):
             grouped = rounded.tile([P, N, PACK], BF16, name="grouped", align_bytes=64)
@@ -131,75 +122,64 @@ def tile_list_term_query_topics_kernel(
         def quantize_wd(grouped, b):
             nc.vector.quantize_mx(out=wd_codes[b][:].bitcast(FP8X4), scales=wd_planes[b][:], in_=grouped[:].rearrange("p n t -> p (n t)"))
 
-        z_codes = [keep.tile([P, S2], U32, name=f"z_codes{b}", align_bytes=64) for b in range(2)]
-        z_planes = [keep.tile([P, S2], U8, name=f"z_planes{b}", align_bytes=64) for b in range(2)]
+        def match_pass(banks, a, b, lo):
+            plane = planes[a][:].bitcast(U8)
+            for t in range(PACK):
+                first = PASS * b + P * t
+                nc.tensor.matmul_mx(
+                    out=banks[t // 2][:, t % 2, :],
+                    lhsT=term_codes[a][:, b, t, :].bitcast(FP8X4),
+                    lhsT_scale=plane[:, first : first + P],
+                    rhs=query_codes[a][:, lo : lo + CHUNK].bitcast(FP8X4),
+                    rhs_scale=plane[:, S + lo : S + lo + CHUNK],
+                    start=(a == 0 and t % 2 == 0),
+                    stop=(a == 1 and t % 2 == 1),
+                )
 
-        def matches(b, lo, hi):
-            width = hi - lo
-            per_bank = BANK // width
-            banks = []
-            for first in range(0, PACK, per_bank):
-                bank = psum.tile([P, per_bank, width], F32, name="bank")
-                for e in range(per_bank):
-                    for a in range(2):
-                        nc.tensor.matmul_mx(
-                            out=bank[:, e, :],
-                            lhsT=term_codes[a][:, b, first + e, :].bitcast(FP8X4),
-                            lhsT_scale=term_planes[TERM_PLANE[a] :, b, first + e, :],
-                            rhs=query_codes[a][:, lo:hi].bitcast(FP8X4),
-                            rhs_scale=query_planes[QUERY_PLANE[a] :, lo:hi],
-                            start=(a == 0),
-                            stop=(a == 1),
-                        )
-                banks.append(bank)
+        def matches(first_bank, b, lo):
+            banks = [bank_tile(first_bank + u, 2) for u in range(2)]
+            match_pass(banks, 0, b, lo)
+            match_pass(banks, 1, b, lo)
             return banks
 
         def drop_negatives(banks, on_vector):
-            per_bank, width = banks[0].shape[1:]
-            kept = work.tile([P, len(banks), width, per_bank], F32, name="kept", align_bytes=64)
-            for i, bank in enumerate(banks):
+            kept = work.tile([P, 2, CHUNK, 2], F32, name="kept", align_bytes=64)
+            for u, bank in enumerate(banks):
                 side_by_side = bank[:].rearrange("p e j -> p j e")
-                if i in on_vector:
-                    nc.vector.tensor_scalar(out=kept[:, i, :, :], in0=side_by_side, scalar1=0.0, scalar2=None, op0=ALU.max)
+                if on_vector:
+                    nc.vector.tensor_scalar(out=kept[:, u, :, :], in0=side_by_side, scalar1=0.0, scalar2=None, op0=ALU.max)
                 else:
-                    nc.scalar.activation(out=kept[:, i, :, :], in_=side_by_side, func=ACT.Relu)
+                    nc.scalar.activation(out=kept[:, u, :, :], in_=side_by_side, func=ACT.Relu)
             return kept
 
         def saturate(kept, lo, hi):
-            runs = min(kept.shape[1], 2)
-            logs = work.tile([P, runs, hi - lo, PACK // runs], F32, name="logs", align_bytes=64)
-            if kept.shape[1] == PACK:
-                source = kept[:, :, lo:hi, 0].rearrange("p (u e) j -> p u j e", e=2)
-            else:
-                source = kept[:, :, lo:hi, :]
-            nc.scalar.activation(out=logs[:], in_=source, func=ACT.Ln, bias=one[:])
+            logs = work.tile([P, hi - lo, 2, 2], F32, name="logs", align_bytes=64)
+            nc.scalar.activation(out=logs[:], in_=kept[:, :, lo:hi, :].rearrange("p u j e -> p j u e"), func=ACT.Ln, bias=one[:])
             return logs
 
         def weigh(logs, b):
-            runs, width, per_run = logs.shape[1:]
-            z = rounded.tile([P, width, runs, per_run], BF16, name="grouped", align_bytes=64)
-            weights = idf_sb[:, b, :].rearrange("p (u e) -> p u e", u=runs).unsqueeze(1).to_broadcast([P, width, runs, per_run])
-            nc.vector.tensor_tensor(out=z[:], in0=logs[:].rearrange("p u j e -> p j u e"), in1=weights, op=ALU.mult)
+            width = logs.shape[1]
+            z = rounded.tile([P, width, PACK], BF16, name="grouped", align_bytes=64)
+            weights = idf_sb[:, b, :].unsqueeze(1).to_broadcast([P, width, PACK])
+            nc.vector.tensor_tensor(out=z[:], in0=logs[:].rearrange("p j u e -> p j (u e)"), in1=weights, op=ALU.mult)
             return z
 
         def quantize_z(z, b, lo):
             cols = slice(lo, lo + z.shape[1])
-            nc.vector.quantize_mx(
-                out=z_codes[b][:, cols].bitcast(FP8X4), scales=z_planes[b][:, cols], in_=z[:].rearrange("p j u e -> p (j u e)")
-            )
+            nc.vector.quantize_mx(out=z_codes[b][:, cols].bitcast(FP8X4), scales=z_planes[b][:, cols], in_=z[:].rearrange("p j t -> p (j t)"))
 
-        def packed_pass(acc, nt, b, lo, hi):
+        def packed_pass(acc, nt, b, lo, hi, start):
             nc.tensor.matmul_mx(
                 out=acc,
                 lhsT=w4_codes[:, b, :].bitcast(U8)[:, 2 * P * nt : 2 * P * (nt + 1)].bitcast(FP4X4),
                 lhsT_scale=w4_planes[:, b, :].bitcast(U8)[:, P * nt : P * (nt + 1)],
                 rhs=z_codes[b][:, lo:hi].bitcast(FP8X4),
                 rhs_scale=z_planes[b][:, lo:hi],
-                start=(b == 0),
+                start=start,
                 stop=False,
             )
 
-        def update_pass(acc, nt, b, lo, hi):
+        def update_pass(acc, nt, b, lo, hi, stop):
             nc.tensor.matmul_mx(
                 out=acc,
                 lhsT=wd_codes[b][:, P * nt : P * (nt + 1)].bitcast(FP8X4),
@@ -207,126 +187,94 @@ def tile_list_term_query_topics_kernel(
                 rhs=z_codes[b][:, lo:hi].bitcast(FP8X4),
                 rhs_scale=z_planes[b][:, lo:hi],
                 start=False,
-                stop=(b == 1),
+                stop=stop,
             )
 
-        def open_sums(lo, hi):
-            sums = [psum.tile([P, 1, hi - lo], F32, name="bank") for nt in range(N // P)]
-            for one_pass in (packed_pass, update_pass):
-                for nt in range(N // P):
-                    one_pass(sums[nt][:, 0, :], nt, 0, lo, hi)
-            return sums
-
-        def close_sums(sums, lo, hi):
-            for nt in range(N // P):
-                packed_pass(sums[nt][:, 0, :], nt, 1, lo, hi)
-                update_pass(sums[nt][:, 0, :], nt, 1, lo, hi)
-
-        def packed_sums(lo, hi):
-            tiles_per_bank = BANK // (hi - lo)
-            sums = []
-            for first in range(0, N // P, tiles_per_bank):
-                bank = psum.tile([P, tiles_per_bank, hi - lo], F32, name="bank")
-                for e in range(tiles_per_bank):
-                    for c in range(0, hi - lo, P):
-                        for b in range(2):
-                            packed_pass(bank[:, e, c : c + P], first + e, b, lo + c, lo + c + P)
-                            update_pass(bank[:, e, c : c + P], first + e, b, lo + c, lo + c + P)
-                sums.append(bank)
-            return sums
-
-        def leave(result, bank, on_vector):
-            if on_vector:
-                nc.vector.tensor_copy(out=result, in_=bank[:])
-            else:
-                nc.scalar.copy(out=result, in_=bank[:])
+        def topic_passes(sums, b, lo, hi):
+            width = hi - lo
+            step = width if width == BANK else P
+            for i, bank in enumerate(sums):
+                tiles = N // P // len(sums)
+                for e in range(tiles):
+                    for c in range(0, width, step):
+                        packed_pass(bank[:, e, c : c + step], tiles * i + e, b, lo + c, lo + c + step, b == 0 and e == 0 and c == 0)
+                    update_pass(bank[:, e, 0:width], tiles * i + e, b, lo, hi, b == 1 and e == tiles - 1)
 
         def store(sums, lo, hi, on_vector):
+            tiles = N // P // len(sums)
             for i, bank in enumerate(sums):
-                tiles = bank.shape[1]
                 result = stage.tile([P, tiles, hi - lo], F32, name="result", align_bytes=64)
-                leave(result[:], bank, i in on_vector)
+                if i in on_vector:
+                    nc.vector.tensor_copy(out=result[:], in_=bank[:, 0:tiles, 0 : hi - lo])
+                else:
+                    nc.scalar.copy(out=result[:], in_=bank[:, 0:tiles, 0 : hi - lo])
                 rows = out[P * tiles * i : P * tiles * (i + 1), lo:hi]
                 nc.sync.dma_start(out=rows.rearrange("(e p) j -> p e j", p=P), in_=result[:])
 
-        def store_together(sums, lo, hi, on_vector):
-            result = stage.tile([P, len(sums), hi - lo], F32, name="result", align_bytes=64)
-            for i, bank in enumerate(sums):
-                leave(result[:, i : i + 1, :], bank, i in on_vector)
-            nc.sync.dma_start(out=out[:, lo:hi].rearrange("(e p) j -> p e j", p=P), in_=result[:])
-
-        gather_query_words(0, 0)
-        gather_query_words(0, 1)
-        gather_query_scales(0)
-        gather_term_scales(0)
-        gather_term_scales(1)
-        gather_query_scales(1)
-        permute_term_scales(0)
-        permute_term_scales(1)
-        gather_term_words(0, 0)
-        gather_term_words(0, 1)
+        early = [[bank_tile(2 * n + u, 2) for u in range(2)] for n in range(4)]
+        for n in range(4):
+            match_pass(early[n], 0, n // 2, CHUNK * (n % 2))
         gather_term_words(1, 0)
         gather_term_words(1, 1)
-        gather_query_words(1, 0)
+        for n in range(4):
+            match_pass(early[n], 1, n // 2, CHUNK * (n % 2))
 
-        m00 = matches(0, 0, 512)
-        m10 = matches(1, 0, 512)
-        k00 = drop_negatives(m00, ())
-        l00a = saturate(k00, 0, 256)
-        l00b = saturate(k00, 256, 512)
-        gather_query_words(1, 1)
-        m01 = matches(0, 512, 768)
-        m11 = matches(1, 512, 768)
+        k0 = drop_negatives(early[0], False)
+        k1 = drop_negatives(early[1], True)
+        l0 = saturate(k0, 0, CHUNK)
+        l1 = saturate(k1, 0, CHUNK)
+        m4 = matches(0, 0, 512)
+        m5 = matches(2, 1, 512)
+        k2 = drop_negatives(early[2], False)
+        l2 = saturate(k2, 0, CHUNK)
+        z0 = weigh(l0, 0)
         g0 = round_wd(0)
-        k10 = drop_negatives(m10, (0, 1))
-        l10a = saturate(k10, 0, 256)
-        l10b = saturate(k10, 256, 512)
-        m02 = matches(0, 768, 896)
-        m12 = matches(1, 768, 896)
+        quantize_z(z0, 0, 0)
+        z1 = weigh(l1, 0)
         quantize_wd(g0, 0)
-        z00a = weigh(l00a, 0)
-        z00b = weigh(l00b, 0)
-        quantize_z(z00a, 0, 0)
-        quantize_z(z00b, 0, 256)
-        k01 = drop_negatives(m01, ())
-        l01 = saturate(k01, 0, 256)
-        s0 = open_sums(0, 512)
-        z10a = weigh(l10a, 1)
-        z10b = weigh(l10b, 1)
+        quantize_z(z1, 0, 256)
+        k3 = drop_negatives(early[3], False)
+        l3 = saturate(k3, 0, CHUNK)
+        s0 = [bank_tile(4 + nt, 1) for nt in range(4)]
+        topic_passes(s0, 0, 0, 512)
+        z2 = weigh(l2, 1)
         g1 = round_wd(1)
-        quantize_z(z10a, 1, 0)
-        quantize_z(z10b, 1, 256)
+        quantize_z(z2, 1, 0)
+        k4 = drop_negatives(m4, False)
+        l4 = saturate(k4, 0, CHUNK)
+        m6 = matches(0, 0, 768)
+        z3 = weigh(l3, 1)
         quantize_wd(g1, 1)
-        k11 = drop_negatives(m11, ())
-        l11 = saturate(k11, 0, 256)
-        m03 = matches(0, 896, 1024)
-        m13 = matches(1, 896, 1024)
-        close_sums(s0, 0, 512)
-        z01 = weigh(l01, 0)
-        z11 = weigh(l11, 1)
-        quantize_z(z01, 0, 512)
-        quantize_z(z11, 1, 512)
-        k02 = drop_negatives(m02, ())
-        l02 = saturate(k02, 0, 128)
-        k12 = drop_negatives(m12, ())
-        l12 = saturate(k12, 0, 128)
-        store(s0, 0, 512, (1, 3))
-        s1 = packed_sums(512, 768)
-        z02 = weigh(l02, 0)
-        z12 = weigh(l12, 1)
-        quantize_z(z02, 0, 768)
-        quantize_z(z12, 1, 768)
-        k03 = drop_negatives(m03, ())
-        l03 = saturate(k03, 0, 128)
-        k13 = drop_negatives(m13, ())
-        l13 = saturate(k13, 0, 128)
-        s2 = packed_sums(768, 896)
-        z03 = weigh(l03, 0)
-        z13 = weigh(l13, 1)
-        quantize_z(z03, 0, 896)
-        s3 = open_sums(896, 1024)
-        quantize_z(z13, 1, 896)
-        close_sums(s3, 896, 1024)
+        quantize_z(z3, 1, 256)
+        topic_passes(s0, 1, 0, 512)
+        k5 = drop_negatives(m5, False)
+        l5 = saturate(k5, 0, CHUNK)
+        m7 = matches(2, 1, 768)
+        z4 = weigh(l4, 0)
+        z5 = weigh(l5, 1)
+        quantize_z(z4, 0, 512)
+        store(s0, 0, 512, (2, 3))
+        k6 = drop_negatives(m6, False)
+        l6 = saturate(k6, 0, CHUNK)
+        quantize_z(z5, 1, 512)
+        k7 = drop_negatives(m7, False)
+        l7a = saturate(k7, 0, P)
+        l7b = saturate(k7, P, CHUNK)
+        s1 = [bank_tile(4 + i, 2) for i in range(2)]
+        topic_passes(s1, 0, 512, 768)
+        topic_passes(s1, 1, 512, 768)
+        z6 = weigh(l6, 0)
+        z7a = weigh(l7a, 1)
+        quantize_z(z6, 0, 768)
+        s2 = [bank_tile(6, 4)]
+        s3 = [bank_tile(i, 2) for i in range(2)]
+        topic_passes(s2, 0, 768, 896)
+        topic_passes(s3, 0, 896, 1024)
+        z7b = weigh(l7b, 1)
+        quantize_z(z7a, 1, 768)
+        topic_passes(s2, 1, 768, 896)
+        quantize_z(z7b, 1, 896)
+        topic_passes(s3, 1, 896, 1024)
         store(s1, 512, 768, ())
         store(s2, 768, 896, ())
-        store_together(s3, 896, 1024, (1, 3))
+        store(s3, 896, 1024, (1,))

@@ -21,7 +21,8 @@ PACK = 4
 PASS = P * PACK
 BANK = 512
 CHUNK = 256
-ROWS = 32
+ROW0 = 96
+PLANE = (12, 0)
 KIB = 1024
 
 
@@ -42,6 +43,7 @@ def tile_list_term_query_topics_kernel(
         term_scale_table = keep.tile([P, T // 4], I32, name="term_scale_table", align_bytes=64)
         query_scale_table = keep.tile([P, T2 // 4], I32, name="query_scale_table", align_bytes=64)
         planes = [keep.tile([P, (S + S2) // 4], I32, name=f"planes{a}", align_bytes=64) for a in range(2)]
+        idf_sb = keep.tile([P, 2, PACK], F32, name="idf_sb", align_bytes=64)
         one = keep.tile([P, 1], F32, name="one")
         warm = keep.tile([P, 1], F32, name="warm")
         query_table = shared.tile([P, 2, T2], I32, name="query_table", align_bytes=64, offset=0)
@@ -50,21 +52,24 @@ def tile_list_term_query_topics_kernel(
         nc.vector.memset(one[:], 1.0)
         nc.scalar.activation(out=warm[:], in_=one[:], func=ACT.Ln)
         for table in (query_scale_table, term_scale_table):
-            nc.vector.memset(table[32:64, :], 0)
-            nc.vector.memset(table[64:128, :], 0)
-        nc.gpsimd.memset(planes[1][:], 0)
+            nc.vector.memset(table[0:ROW0, :], 0)
+        nc.vector.memset(planes[1][:], 0)
 
         nc.sync.dma_start(query_list[:], offs2)
         nc.sync.dma_start(term_list[:], offs)
-        nc.sync.dma_start(out=query_scale_table[0:ROWS, :], in_=tab2_scales.rearrange("a q n -> (a q) n").bitcast(I32))
-        nc.sync.dma_start(out=term_scale_table[0:ROWS, :], in_=tab_scales.rearrange("a q n -> (a q) n").bitcast(I32))
+        nc.sync.dma_start(out=query_scale_table[ROW0:, :], in_=tab2_scales.rearrange("a q n -> (a q) n").bitcast(I32))
+        nc.sync.dma_start(out=term_scale_table[ROW0:, :], in_=tab_scales.rearrange("a q n -> (a q) n").bitcast(I32))
+        nc.sync.dma_start(out=idf_sb[:], in_=idf.rearrange("(b p t) -> p b t", b=2, t=PACK))
         nc.sync.dma_start(out=query_table[:], in_=tab2_words.rearrange("a p n t -> p a (n t)").bitcast(I32))
-        for a in range(2):
+
+        def load_term_words(a):
             nc.sync.dma_start(out=term_table[a][:], in_=tab_words[a].rearrange("p n t -> p (n t)").bitcast(I32))
 
+        load_term_words(0)
+
         term_codes = [keep.tile([P, 2, PACK, P], U32, name=f"term_codes{a}", align_bytes=64) for a in range(2)]
-        query_codes = [keep.tile([P, S2], U32, name=f"query_codes{a}", align_bytes=64) for a in range(2)]
-        term_scales = shared.tile([P, S], U8, name="term_scales", align_bytes=64, offset=48 * KIB)
+        query_codes = {(a, h): keep.tile([P, BANK], U32, name=f"query_codes{a}{h}", align_bytes=64) for a, h in ((0, 0), (0, 1), (1, 0))}
+        term_scales = keep.tile([P, S], U8, name="term_scales", align_bytes=64)
         query_scales = keep.tile([P, S2], U8, name="query_scales", align_bytes=64)
 
         nc.vector.tensor_copy(query_scales[:], query_scale_table[:].bitcast(U8).indirect(query_list[:]))
@@ -74,15 +79,19 @@ def tile_list_term_query_topics_kernel(
             planes[0][:, 0 : S // 4].bitcast(U8).rearrange("p (b t m) -> p b t m", b=2, t=PACK),
             term_scales[:].rearrange("p (b m t) -> p b t m", b=2, t=PACK),
         )
-        for a in range(2):
-            for q in range(1 - a, 4):
-                first = 16 * a + 4 * q
-                nc.scalar.dma_start(out=planes[a][32 * q : 32 * q + 4, :], in_=planes[0][first : first + 4, :])
-        idf_sb = shared.tile([P, 2, PACK], F32, name="idf_sb", align_bytes=64, offset=48 * KIB)
-        nc.scalar.dma_start(out=idf_sb[:], in_=idf.rearrange("(b p t) -> p b t", b=2, t=PACK))
 
-        for a in range(2):
-            nc.vector.tensor_copy(query_codes[a][:], query_table[:, a, :].bitcast(U32).indirect(query_list[:]))
+        def move_rows(a, q):
+            source, target = ROW0 + 16 * a + 4 * q, 32 * q + PLANE[a]
+            nc.sync.dma_start(out=planes[a][target : target + 4, :], in_=planes[0][source : source + 4, :])
+
+        for q in range(3):
+            move_rows(0, q)
+        load_term_words(1)
+        for q in range(4):
+            move_rows(1, q)
+
+        def gather_query_words(a, h):
+            nc.vector.tensor_copy(query_codes[a, h][:], query_table[:, a, :].bitcast(U32).indirect(query_list[:, 32 * h : 32 * (h + 1)]))
 
         def gather_term_words(a, b):
             nc.vector.tensor_copy(
@@ -90,10 +99,15 @@ def tile_list_term_query_topics_kernel(
                 term_table[a][:].bitcast(U32).indirect(term_list[:, 32 * b : 32 * (b + 1)]),
             )
 
+        gather_query_words(0, 0)
+        gather_query_words(0, 1)
+        gather_query_words(1, 0)
         gather_term_words(0, 0)
         gather_term_words(0, 1)
+        query_codes[1, 1] = shared.tile([P, BANK], U32, name="query_codes11", align_bytes=64, offset=28 * KIB)
+        gather_query_words(1, 1)
 
-        wd_raw = [shared.tile([P, PACK, N], F32, name=f"wd_raw{b}", align_bytes=64, offset=16 * KIB * b) for b in range(2)]
+        wd_raw = [shared.tile([P, PACK, N], F32, name=f"wd_raw{b}", align_bytes=64, offset=16 * KIB * (1 - b)) for b in range(2)]
         w4_codes = shared.tile([P, 2, 2 * N // 4], I32, name="w4_codes", align_bytes=64, offset=24 * KIB)
         w4_planes = shared.tile([P, 2, N // 4], I32, name="w4_planes", align_bytes=64, offset=26 * KIB)
         nc.vector.memset(w4_planes[:], 0)
@@ -123,14 +137,14 @@ def tile_list_term_query_topics_kernel(
             nc.vector.quantize_mx(out=wd_codes[b][:].bitcast(FP8X4), scales=wd_planes[b][:], in_=grouped[:].rearrange("p n t -> p (n t)"))
 
         def match_pass(banks, a, b, lo):
-            plane = planes[a][:].bitcast(U8)
+            plane = planes[a][PLANE[a] :, :].bitcast(U8)
             for t in range(PACK):
                 first = PASS * b + P * t
                 nc.tensor.matmul_mx(
                     out=banks[t // 2][:, t % 2, :],
                     lhsT=term_codes[a][:, b, t, :].bitcast(FP8X4),
                     lhsT_scale=plane[:, first : first + P],
-                    rhs=query_codes[a][:, lo : lo + CHUNK].bitcast(FP8X4),
+                    rhs=query_codes[a, lo // BANK][:, lo % BANK : lo % BANK + CHUNK].bitcast(FP8X4),
                     rhs_scale=plane[:, S + lo : S + lo + CHUNK],
                     start=(a == 0 and t % 2 == 0),
                     stop=(a == 1 and t % 2 == 1),
@@ -200,11 +214,10 @@ def tile_list_term_query_topics_kernel(
                         packed_pass(bank[:, e, c : c + step], tiles * i + e, b, lo + c, lo + c + step, b == 0 and e == 0 and c == 0)
                     update_pass(bank[:, e, 0:width], tiles * i + e, b, lo, hi, b == 1 and e == tiles - 1)
 
-        def store(sums, lo, hi, on_vector):
-            tiles = N // P // len(sums)
-            for i, bank in enumerate(sums):
+        def store(sums, first, lo, hi, tiles, on_vector):
+            for i, bank in enumerate(sums, first):
                 result = stage.tile([P, tiles, hi - lo], F32, name="result", align_bytes=64)
-                if i in on_vector:
+                if on_vector:
                     nc.vector.tensor_copy(out=result[:], in_=bank[:, 0:tiles, 0 : hi - lo])
                 else:
                     nc.scalar.copy(out=result[:], in_=bank[:, 0:tiles, 0 : hi - lo])
@@ -220,18 +233,18 @@ def tile_list_term_query_topics_kernel(
             match_pass(early[n], 1, n // 2, CHUNK * (n % 2))
 
         k0 = drop_negatives(early[0], False)
-        k1 = drop_negatives(early[1], True)
         l0 = saturate(k0, 0, CHUNK)
+        k1 = drop_negatives(early[1], True)
         l1 = saturate(k1, 0, CHUNK)
         m4 = matches(0, 0, 512)
         m5 = matches(2, 1, 512)
         k2 = drop_negatives(early[2], False)
         l2 = saturate(k2, 0, CHUNK)
-        z0 = weigh(l0, 0)
         g0 = round_wd(0)
-        quantize_z(z0, 0, 0)
-        z1 = weigh(l1, 0)
+        z0 = weigh(l0, 0)
         quantize_wd(g0, 0)
+        z1 = weigh(l1, 0)
+        quantize_z(z0, 0, 0)
         quantize_z(z1, 0, 256)
         k3 = drop_negatives(early[3], False)
         l3 = saturate(k3, 0, CHUNK)
@@ -253,21 +266,21 @@ def tile_list_term_query_topics_kernel(
         z4 = weigh(l4, 0)
         z5 = weigh(l5, 1)
         quantize_z(z4, 0, 512)
-        store(s0, 0, 512, (2, 3))
+        store(s0[0:3], 0, 0, 512, 1, True)
         k6 = drop_negatives(m6, False)
         l6 = saturate(k6, 0, CHUNK)
         quantize_z(z5, 1, 512)
         k7 = drop_negatives(m7, False)
         l7a = saturate(k7, 0, P)
         l7b = saturate(k7, P, CHUNK)
-        s1 = [bank_tile(4 + i, 2) for i in range(2)]
+        s1 = [bank_tile(i, 2) for i in range(2)]
         topic_passes(s1, 0, 512, 768)
         topic_passes(s1, 1, 512, 768)
         z6 = weigh(l6, 0)
         z7a = weigh(l7a, 1)
         quantize_z(z6, 0, 768)
-        s2 = [bank_tile(6, 4)]
-        s3 = [bank_tile(i, 2) for i in range(2)]
+        s2 = [bank_tile(4, 4)]
+        s3 = [bank_tile(5 + i, 2) for i in range(2)]
         topic_passes(s2, 0, 768, 896)
         topic_passes(s3, 0, 896, 1024)
         z7b = weigh(l7b, 1)
@@ -275,6 +288,8 @@ def tile_list_term_query_topics_kernel(
         topic_passes(s2, 1, 768, 896)
         quantize_z(z7b, 1, 896)
         topic_passes(s3, 1, 896, 1024)
-        store(s1, 512, 768, ())
-        store(s2, 768, 896, ())
-        store(s3, 896, 1024, (1,))
+        store(s0[3:4], 3, 0, 512, 1, False)
+        store(s1, 0, 512, 768, 2, False)
+        store(s2, 0, 768, 896, 4, False)
+        store(s3[0:1], 0, 896, 1024, 2, False)
+        store(s3[1:2], 1, 896, 1024, 2, True)

@@ -59,7 +59,6 @@ def tile_list_term_query_topics_kernel(
         nc.sync.dma_start(term_list[:], offs)
         nc.sync.dma_start(out=query_scale_table[ROW0:, :], in_=tab2_scales.rearrange("a q n -> (a q) n").bitcast(I32))
         nc.sync.dma_start(out=term_scale_table[ROW0:, :], in_=tab_scales.rearrange("a q n -> (a q) n").bitcast(I32))
-        nc.sync.dma_start(out=idf_sb[:], in_=idf.rearrange("(b p t) -> p b t", b=2, t=PACK))
         nc.sync.dma_start(out=query_table[:], in_=tab2_words.rearrange("a p n t -> p a (n t)").bitcast(I32))
 
         def load_term_words(a):
@@ -68,7 +67,9 @@ def tile_list_term_query_topics_kernel(
         load_term_words(0)
 
         term_codes = [keep.tile([P, 2, PACK, P], U32, name=f"term_codes{a}", align_bytes=64) for a in range(2)]
-        query_codes = {(a, h): keep.tile([P, BANK], U32, name=f"query_codes{a}{h}", align_bytes=64) for a, h in ((0, 0), (0, 1), (1, 0))}
+        first_pass = keep.tile([P, S2], U32, name="query_codes0", align_bytes=64)
+        query_codes = {(0, h): first_pass[:, BANK * h : BANK * (h + 1)] for h in range(2)}
+        query_codes[1, 0] = keep.tile([P, BANK], U32, name="query_codes10", align_bytes=64)
         term_scales = keep.tile([P, S], U8, name="term_scales", align_bytes=64)
         query_scales = keep.tile([P, S2], U8, name="query_scales", align_bytes=64)
 
@@ -90,8 +91,8 @@ def tile_list_term_query_topics_kernel(
         for q in range(4):
             move_rows(1, q)
 
-        def gather_query_words(a, h):
-            nc.vector.tensor_copy(query_codes[a, h][:], query_table[:, a, :].bitcast(U32).indirect(query_list[:, 32 * h : 32 * (h + 1)]))
+        def gather_query_words(h):
+            nc.vector.tensor_copy(query_codes[1, h][:], query_table[:, 1, :].bitcast(U32).indirect(query_list[:, 32 * h : 32 * (h + 1)]))
 
         def gather_term_words(a, b):
             nc.vector.tensor_copy(
@@ -99,19 +100,19 @@ def tile_list_term_query_topics_kernel(
                 term_table[a][:].bitcast(U32).indirect(term_list[:, 32 * b : 32 * (b + 1)]),
             )
 
-        gather_query_words(0, 0)
-        gather_query_words(0, 1)
-        gather_query_words(1, 0)
+        nc.vector.tensor_copy(first_pass[:], query_table[:, 0, :].bitcast(U32).indirect(query_list[:]))
+        gather_query_words(0)
         gather_term_words(0, 0)
         gather_term_words(0, 1)
         query_codes[1, 1] = shared.tile([P, BANK], U32, name="query_codes11", align_bytes=64, offset=28 * KIB)
-        gather_query_words(1, 1)
+        gather_query_words(1)
 
-        wd_raw = [shared.tile([P, PACK, N], F32, name=f"wd_raw{b}", align_bytes=64, offset=16 * KIB * (1 - b)) for b in range(2)]
-        w4_codes = shared.tile([P, 2, 2 * N // 4], I32, name="w4_codes", align_bytes=64, offset=24 * KIB)
-        w4_planes = shared.tile([P, 2, N // 4], I32, name="w4_planes", align_bytes=64, offset=26 * KIB)
+        wd_raw = [keep.tile([P, PACK, N], F32, name=f"wd_raw{b}", align_bytes=64) for b in range(2)]
+        w4_codes = keep.tile([P, 2, 2 * N // 4], I32, name="w4_codes", align_bytes=64)
+        w4_planes = keep.tile([P, 2, N // 4], I32, name="w4_planes", align_bytes=64)
         nc.vector.memset(w4_planes[:], 0)
         nc.sync.dma_start(out=wd_raw[0][:], in_=wd[0:PASS, :].rearrange("(p t) n -> p t n", t=PACK))
+        nc.sync.dma_start(out=idf_sb[:], in_=idf.rearrange("(b p t) -> p b t", b=2, t=PACK))
         nc.sync.dma_start(out=w4_codes[:], in_=w4_words.bitcast(I32).rearrange("b p c -> p b c"))
         for q in range(4):
             nc.sync.dma_start(
@@ -237,7 +238,7 @@ def tile_list_term_query_topics_kernel(
         k1 = drop_negatives(early[1], True)
         l1 = saturate(k1, 0, CHUNK)
         m4 = matches(0, 0, 512)
-        m5 = matches(2, 1, 512)
+        m5 = matches(2, 0, 768)
         k2 = drop_negatives(early[2], False)
         l2 = saturate(k2, 0, CHUNK)
         g0 = round_wd(0)
@@ -255,41 +256,43 @@ def tile_list_term_query_topics_kernel(
         quantize_z(z2, 1, 0)
         k4 = drop_negatives(m4, False)
         l4 = saturate(k4, 0, CHUNK)
-        m6 = matches(0, 0, 768)
+        m6 = matches(0, 1, 512)
         z3 = weigh(l3, 1)
         quantize_wd(g1, 1)
         quantize_z(z3, 1, 256)
-        topic_passes(s0, 1, 0, 512)
         k5 = drop_negatives(m5, False)
         l5 = saturate(k5, 0, CHUNK)
         m7 = matches(2, 1, 768)
+        topic_passes(s0, 1, 0, 512)
         z4 = weigh(l4, 0)
-        z5 = weigh(l5, 1)
+        z5 = weigh(l5, 0)
         quantize_z(z4, 0, 512)
-        store(s0[0:3], 0, 0, 512, 1, True)
+        quantize_z(z5, 0, 768)
         k6 = drop_negatives(m6, False)
         l6 = saturate(k6, 0, CHUNK)
-        quantize_z(z5, 1, 512)
+        s1 = [bank_tile(i, 2) for i in range(2)]
+        topic_passes(s1, 0, 512, 768)
+        store(s0[0:1], 0, 0, 512, 1, False)
         k7 = drop_negatives(m7, False)
         l7a = saturate(k7, 0, P)
         l7b = saturate(k7, P, CHUNK)
-        s1 = [bank_tile(i, 2) for i in range(2)]
-        topic_passes(s1, 0, 512, 768)
-        topic_passes(s1, 1, 512, 768)
-        z6 = weigh(l6, 0)
-        z7a = weigh(l7a, 1)
-        quantize_z(z6, 0, 768)
+        z6 = weigh(l6, 1)
+        store(s0[1:2], 1, 0, 512, 1, True)
+        quantize_z(z6, 1, 512)
         s2 = [bank_tile(4, 4)]
-        s3 = [bank_tile(5 + i, 2) for i in range(2)]
+        s3 = [bank_tile(2 + i, 2) for i in range(2)]
         topic_passes(s2, 0, 768, 896)
         topic_passes(s3, 0, 896, 1024)
+        topic_passes(s1, 1, 512, 768)
+        z7a = weigh(l7a, 1)
         z7b = weigh(l7b, 1)
         quantize_z(z7a, 1, 768)
         topic_passes(s2, 1, 768, 896)
         quantize_z(z7b, 1, 896)
         topic_passes(s3, 1, 896, 1024)
-        store(s0[3:4], 3, 0, 512, 1, False)
-        store(s1, 0, 512, 768, 2, False)
+        store(s0[2:4], 2, 0, 512, 1, False)
+        store(s1[0:1], 0, 512, 768, 2, False)
+        store(s1[1:2], 1, 512, 768, 2, True)
         store(s2, 0, 768, 896, 4, False)
         store(s3[0:1], 0, 896, 1024, 2, False)
         store(s3[1:2], 1, 896, 1024, 2, True)

@@ -91,7 +91,7 @@ def tile_list_term_query_topics_kernel(
         for q in range(4):
             move_rows(1, q)
 
-        def gather_query_words(h):
+        def gather_second_pass(h):
             nc.vector.tensor_copy(query_codes[1, h][:], query_table[:, 1, :].bitcast(U32).indirect(query_list[:, 32 * h : 32 * (h + 1)]))
 
         def gather_term_words(a, b):
@@ -101,11 +101,11 @@ def tile_list_term_query_topics_kernel(
             )
 
         nc.vector.tensor_copy(first_pass[:], query_table[:, 0, :].bitcast(U32).indirect(query_list[:]))
-        gather_query_words(0)
+        gather_second_pass(0)
         gather_term_words(0, 0)
         gather_term_words(0, 1)
         query_codes[1, 1] = shared.tile([P, BANK], U32, name="query_codes11", align_bytes=64, offset=28 * KIB)
-        gather_query_words(1)
+        gather_second_pass(1)
 
         wd_raw = [keep.tile([P, PACK, N], F32, name=f"wd_raw{b}", align_bytes=64) for b in range(2)]
         w4_codes = keep.tile([P, 2, 2 * N // 4], I32, name="w4_codes", align_bytes=64)
@@ -208,8 +208,8 @@ def tile_list_term_query_topics_kernel(
         def topic_passes(sums, b, lo, hi):
             width = hi - lo
             step = width if width == BANK else P
+            tiles = N // P // len(sums)
             for i, bank in enumerate(sums):
-                tiles = N // P // len(sums)
                 for e in range(tiles):
                     for c in range(0, width, step):
                         packed_pass(bank[:, e, c : c + step], tiles * i + e, b, lo + c, lo + c + step, b == 0 and e == 0 and c == 0)
@@ -233,66 +233,64 @@ def tile_list_term_query_topics_kernel(
         for n in range(4):
             match_pass(early[n], 1, n // 2, CHUNK * (n % 2))
 
-        k0 = drop_negatives(early[0], False)
-        l0 = saturate(k0, 0, CHUNK)
-        k1 = drop_negatives(early[1], True)
-        l1 = saturate(k1, 0, CHUNK)
-        m4 = matches(0, 0, 512)
-        m5 = matches(2, 0, 768)
-        k2 = drop_negatives(early[2], False)
-        l2 = saturate(k2, 0, CHUNK)
-        g0 = round_wd(0)
-        z0 = weigh(l0, 0)
-        quantize_wd(g0, 0)
-        z1 = weigh(l1, 0)
+        kept0 = drop_negatives(early[0], False)
+        logs0 = saturate(kept0, 0, CHUNK)
+        kept1 = drop_negatives(early[1], True)
+        logs1 = saturate(kept1, 0, CHUNK)
+        match4 = matches(0, 0, 512)
+        match5 = matches(2, 0, 768)
+        kept2 = drop_negatives(early[2], False)
+        logs2 = saturate(kept2, 0, CHUNK)
+        wd_rounded0 = round_wd(0)
+        z0 = weigh(logs0, 0)
+        quantize_wd(wd_rounded0, 0)
+        z1 = weigh(logs1, 0)
         quantize_z(z0, 0, 0)
         quantize_z(z1, 0, 256)
-        k3 = drop_negatives(early[3], False)
-        l3 = saturate(k3, 0, CHUNK)
-        s0 = [bank_tile(4 + nt, 1) for nt in range(4)]
-        topic_passes(s0, 0, 0, 512)
-        z2 = weigh(l2, 1)
-        g1 = round_wd(1)
+        kept3 = drop_negatives(early[3], False)
+        logs3 = saturate(kept3, 0, CHUNK)
+        sums_half = [bank_tile(4 + nt, 1) for nt in range(4)]
+        topic_passes(sums_half, 0, 0, 512)
+        z2 = weigh(logs2, 1)
+        wd_rounded1 = round_wd(1)
         quantize_z(z2, 1, 0)
-        k4 = drop_negatives(m4, False)
-        l4 = saturate(k4, 0, CHUNK)
-        m6 = matches(0, 1, 512)
-        z3 = weigh(l3, 1)
-        quantize_wd(g1, 1)
+        kept4 = drop_negatives(match4, False)
+        logs4 = saturate(kept4, 0, CHUNK)
+        match6 = matches(0, 1, 512)
+        z3 = weigh(logs3, 1)
+        quantize_wd(wd_rounded1, 1)
         quantize_z(z3, 1, 256)
-        k5 = drop_negatives(m5, False)
-        l5 = saturate(k5, 0, CHUNK)
-        m7 = matches(2, 1, 768)
-        topic_passes(s0, 1, 0, 512)
-        z4 = weigh(l4, 0)
-        z5 = weigh(l5, 0)
+        kept5 = drop_negatives(match5, False)
+        logs5 = saturate(kept5, 0, CHUNK)
+        match7 = matches(2, 1, 768)
+        topic_passes(sums_half, 1, 0, 512)
+        z4 = weigh(logs4, 0)
+        z5 = weigh(logs5, 0)
         quantize_z(z4, 0, 512)
         quantize_z(z5, 0, 768)
-        k6 = drop_negatives(m6, False)
-        l6 = saturate(k6, 0, CHUNK)
-        s1 = [bank_tile(i, 2) for i in range(2)]
-        topic_passes(s1, 0, 512, 768)
-        store(s0[0:1], 0, 0, 512, 1, False)
-        k7 = drop_negatives(m7, False)
-        l7a = saturate(k7, 0, P)
-        l7b = saturate(k7, P, CHUNK)
-        z6 = weigh(l6, 1)
-        store(s0[1:2], 1, 0, 512, 1, True)
+        kept6 = drop_negatives(match6, False)
+        logs6 = saturate(kept6, 0, CHUNK)
+        sums_quarter = [bank_tile(i, 2) for i in range(2)]
+        topic_passes(sums_quarter, 0, 512, 768)
+        kept7 = drop_negatives(match7, False)
+        logs7a = saturate(kept7, 0, P)
+        logs7b = saturate(kept7, P, CHUNK)
+        z6 = weigh(logs6, 1)
+        store(sums_half[0:1], 0, 0, 512, 1, True)
         quantize_z(z6, 1, 512)
-        s2 = [bank_tile(4, 4)]
-        s3 = [bank_tile(2 + i, 2) for i in range(2)]
-        topic_passes(s2, 0, 768, 896)
-        topic_passes(s3, 0, 896, 1024)
-        topic_passes(s1, 1, 512, 768)
-        z7a = weigh(l7a, 1)
-        z7b = weigh(l7b, 1)
+        sums_eighth = [bank_tile(4, 4)]
+        sums_last = [bank_tile(2 + i, 2) for i in range(2)]
+        topic_passes(sums_eighth, 0, 768, 896)
+        topic_passes(sums_last, 0, 896, 1024)
+        topic_passes(sums_quarter, 1, 512, 768)
+        z7a = weigh(logs7a, 1)
+        z7b = weigh(logs7b, 1)
         quantize_z(z7a, 1, 768)
-        topic_passes(s2, 1, 768, 896)
+        topic_passes(sums_eighth, 1, 768, 896)
         quantize_z(z7b, 1, 896)
-        topic_passes(s3, 1, 896, 1024)
-        store(s0[2:4], 2, 0, 512, 1, False)
-        store(s1[0:1], 0, 512, 768, 2, False)
-        store(s1[1:2], 1, 512, 768, 2, True)
-        store(s2, 0, 768, 896, 4, False)
-        store(s3[0:1], 0, 896, 1024, 2, False)
-        store(s3[1:2], 1, 896, 1024, 2, True)
+        topic_passes(sums_last, 1, 896, 1024)
+        store(sums_half[1:4], 1, 0, 512, 1, False)
+        store(sums_quarter, 0, 512, 768, 2, False)
+        store(sums_eighth, 0, 768, 896, 4, True)
+        store(sums_last[0:1], 0, 896, 1024, 2, False)
+        store(sums_last[1:2], 1, 896, 1024, 2, True)

@@ -33,7 +33,7 @@ def tile_list_term_query_topics_kernel(
     with ExitStack() as ctx:
         keep = ctx.enter_context(tc.tile_pool(name="keep", bufs=1))
         shared = ctx.enter_context(tc.tile_pool(name="shared", bufs=1))
-        work = ctx.enter_context(tc.tile_pool(name="work", bufs=3))
+        work = ctx.enter_context(tc.tile_pool(name="work", bufs=4))
         stage = ctx.enter_context(tc.tile_pool(name="stage", bufs=8))
         rounded = ctx.enter_context(tc.tile_pool(name="rounded", bufs=3))
         psum = ctx.enter_context(tc.psum_pool(name="psum", bufs=1))
@@ -157,15 +157,15 @@ def tile_list_term_query_topics_kernel(
             match_pass(banks, 1, b, lo)
             return banks
 
-        def drop_negatives(banks, on_vector):
-            kept = work.tile([P, 2, CHUNK, 2], F32, name="kept", align_bytes=64)
-            for u, bank in enumerate(banks):
-                side_by_side = bank[:].rearrange("p e j -> p j e")
-                if on_vector:
-                    nc.vector.tensor_scalar(out=kept[:, u, :, :], in0=side_by_side, scalar1=0.0, scalar2=None, op0=ALU.max)
-                else:
-                    nc.scalar.activation(out=kept[:, u, :, :], in_=side_by_side, func=ACT.Relu)
-            return kept
+        def new_kept():
+            return work.tile([P, 2, CHUNK, 2], F32, name="kept", align_bytes=64)
+
+        def drop_negatives(kept, banks, u, on_vector):
+            side_by_side = banks[u][:].rearrange("p e j -> p j e")
+            if on_vector:
+                nc.vector.tensor_scalar(out=kept[:, u, :, :], in0=side_by_side, scalar1=0.0, scalar2=None, op0=ALU.max)
+            else:
+                nc.scalar.activation(out=kept[:, u, :, :], in_=side_by_side, func=ACT.Relu)
 
         def saturate(kept, lo, hi):
             logs = work.tile([P, hi - lo, 2, 2], F32, name="logs", align_bytes=64)
@@ -233,50 +233,67 @@ def tile_list_term_query_topics_kernel(
         for n in range(4):
             match_pass(early[n], 1, n // 2, CHUNK * (n % 2))
 
-        kept0 = drop_negatives(early[0], False)
+        kept0 = new_kept()
+        drop_negatives(kept0, early[0], 0, False)
+        drop_negatives(kept0, early[0], 1, False)
+        kept1 = new_kept()
+        kept2 = new_kept()
+        drop_negatives(kept2, early[2], 0, False)
         logs0 = saturate(kept0, 0, CHUNK)
-        kept1 = drop_negatives(early[1], True)
+        drop_negatives(kept1, early[1], 0, True)
+        wd_rounded0 = round_wd(0)
+        drop_negatives(kept1, early[1], 1, True)
+        drop_negatives(kept2, early[2], 1, False)
         logs1 = saturate(kept1, 0, CHUNK)
         match4 = matches(0, 0, 512)
         match5 = matches(2, 0, 768)
-        kept2 = drop_negatives(early[2], False)
+        kept3 = new_kept()
+        drop_negatives(kept3, early[3], 0, False)
         logs2 = saturate(kept2, 0, CHUNK)
-        wd_rounded0 = round_wd(0)
-        z0 = weigh(logs0, 0)
         quantize_wd(wd_rounded0, 0)
+        z0 = weigh(logs0, 0)
         z1 = weigh(logs1, 0)
         quantize_z(z0, 0, 0)
         quantize_z(z1, 0, 256)
-        kept3 = drop_negatives(early[3], False)
+        drop_negatives(kept3, early[3], 1, False)
+        kept4 = new_kept()
+        drop_negatives(kept4, match4, 0, False)
         logs3 = saturate(kept3, 0, CHUNK)
+        drop_negatives(kept4, match4, 1, False)
         sums_half = [bank_tile(4 + nt, 1) for nt in range(4)]
         topic_passes(sums_half, 0, 0, 512)
+        match6 = matches(0, 1, 512)
         z2 = weigh(logs2, 1)
         wd_rounded1 = round_wd(1)
         quantize_z(z2, 1, 0)
-        kept4 = drop_negatives(match4, False)
+        kept5 = new_kept()
+        drop_negatives(kept5, match5, 0, False)
         logs4 = saturate(kept4, 0, CHUNK)
-        match6 = matches(0, 1, 512)
+        drop_negatives(kept5, match5, 1, False)
+        match7 = matches(2, 1, 768)
         z3 = weigh(logs3, 1)
         quantize_wd(wd_rounded1, 1)
         quantize_z(z3, 1, 256)
-        kept5 = drop_negatives(match5, False)
+        kept6 = new_kept()
+        drop_negatives(kept6, match6, 0, False)
         logs5 = saturate(kept5, 0, CHUNK)
-        match7 = matches(2, 1, 768)
+        drop_negatives(kept6, match6, 1, False)
         topic_passes(sums_half, 1, 0, 512)
         z4 = weigh(logs4, 0)
         z5 = weigh(logs5, 0)
         quantize_z(z4, 0, 512)
         quantize_z(z5, 0, 768)
-        kept6 = drop_negatives(match6, False)
+        kept7 = new_kept()
+        drop_negatives(kept7, match7, 0, False)
         logs6 = saturate(kept6, 0, CHUNK)
+        drop_negatives(kept7, match7, 1, False)
         sums_quarter = [bank_tile(i, 2) for i in range(2)]
         topic_passes(sums_quarter, 0, 512, 768)
-        kept7 = drop_negatives(match7, False)
+        store(sums_half[0:1], 0, 0, 512, 1, True)
+        store(sums_half[1:2], 1, 0, 512, 1, False)
         logs7a = saturate(kept7, 0, P)
         logs7b = saturate(kept7, P, CHUNK)
         z6 = weigh(logs6, 1)
-        store(sums_half[0:1], 0, 0, 512, 1, True)
         quantize_z(z6, 1, 512)
         sums_eighth = [bank_tile(4, 4)]
         sums_last = [bank_tile(2 + i, 2) for i in range(2)]
@@ -289,7 +306,7 @@ def tile_list_term_query_topics_kernel(
         topic_passes(sums_eighth, 1, 768, 896)
         quantize_z(z7b, 1, 896)
         topic_passes(sums_last, 1, 896, 1024)
-        store(sums_half[1:4], 1, 0, 512, 1, False)
+        store(sums_half[2:4], 2, 0, 512, 1, False)
         store(sums_quarter, 0, 512, 768, 2, False)
         store(sums_eighth, 0, 768, 896, 4, True)
         store(sums_last[0:1], 0, 896, 1024, 2, False)

@@ -35,7 +35,9 @@ def tile_list_term_query_topics_kernel(
         shared = ctx.enter_context(tc.tile_pool(name="shared", bufs=1))
         work = ctx.enter_context(tc.tile_pool(name="work", bufs=4))
         stage = ctx.enter_context(tc.tile_pool(name="stage", bufs=8))
-        rounded = ctx.enter_context(tc.tile_pool(name="rounded", bufs=3))
+        rounded = ctx.enter_context(tc.tile_pool(name="rounded", bufs=2))
+        gathered = ctx.enter_context(tc.tile_pool(name="gathered", bufs=5))
+        turn = ctx.enter_context(tc.tile_pool(name="turn", bufs=18))
         psum = ctx.enter_context(tc.psum_pool(name="psum", bufs=1))
 
         term_list = keep.tile([P, S // 16], U16, name="term_list")
@@ -51,14 +53,14 @@ def tile_list_term_query_topics_kernel(
 
         nc.vector.memset(one[:], 1.0)
         nc.scalar.activation(out=warm[:], in_=one[:], func=ACT.Ln)
-        for table in (query_scale_table, term_scale_table):
+        for table in (term_scale_table, query_scale_table):
             nc.vector.memset(table[0:ROW0, :], 0)
         nc.vector.memset(planes[1][:], 0)
 
-        nc.sync.dma_start(query_list[:], offs2)
         nc.sync.dma_start(term_list[:], offs)
-        nc.sync.dma_start(out=query_scale_table[ROW0:, :], in_=tab2_scales.rearrange("a q n -> (a q) n").bitcast(I32))
         nc.sync.dma_start(out=term_scale_table[ROW0:, :], in_=tab_scales.rearrange("a q n -> (a q) n").bitcast(I32))
+        nc.sync.dma_start(query_list[:], offs2)
+        nc.sync.dma_start(out=query_scale_table[ROW0:, :], in_=tab2_scales.rearrange("a q n -> (a q) n").bitcast(I32))
         nc.sync.dma_start(out=query_table[:], in_=tab2_words.rearrange("a p n t -> p a (n t)").bitcast(I32))
 
         def load_term_words(a):
@@ -66,20 +68,20 @@ def tile_list_term_query_topics_kernel(
 
         load_term_words(0)
 
-        term_codes = [keep.tile([P, 2, PACK, P], U32, name=f"term_codes{a}", align_bytes=64) for a in range(2)]
+        term_codes = {}
         first_pass = keep.tile([P, S2], U32, name="query_codes0", align_bytes=64)
         query_codes = {(0, h): first_pass[:, BANK * h : BANK * (h + 1)] for h in range(2)}
         query_codes[1, 0] = keep.tile([P, BANK], U32, name="query_codes10", align_bytes=64)
         term_scales = keep.tile([P, S], U8, name="term_scales", align_bytes=64)
         query_scales = keep.tile([P, S2], U8, name="query_scales", align_bytes=64)
 
-        nc.vector.tensor_copy(query_scales[:], query_scale_table[:].bitcast(U8).indirect(query_list[:]))
         nc.vector.tensor_copy(term_scales[:], term_scale_table[:].bitcast(U8).indirect(term_list[:]))
-        nc.vector.tensor_copy(planes[0][:, S // 4 :], query_scales[:].bitcast(I32))
+        nc.vector.tensor_copy(query_scales[:], query_scale_table[:].bitcast(U8).indirect(query_list[:]))
         nc.vector.tensor_copy(
             planes[0][:, 0 : S // 4].bitcast(U8).rearrange("p (b t m) -> p b t m", b=2, t=PACK),
             term_scales[:].rearrange("p (b m t) -> p b t m", b=2, t=PACK),
         )
+        nc.vector.tensor_copy(planes[0][:, S // 4 :], query_scales[:].bitcast(I32))
 
         def move_rows(a, q):
             source, target = ROW0 + 16 * a + 4 * q, 32 * q + PLANE[a]
@@ -95,8 +97,9 @@ def tile_list_term_query_topics_kernel(
             nc.vector.tensor_copy(query_codes[1, h][:], query_table[:, 1, :].bitcast(U32).indirect(query_list[:, 32 * h : 32 * (h + 1)]))
 
         def gather_term_words(a, b):
+            term_codes[a, b] = gathered.tile([P, PACK, P], U32, name="gathered", align_bytes=64)
             nc.vector.tensor_copy(
-                term_codes[a][:, b, :, :].rearrange("p t m -> p m t"),
+                term_codes[a, b][:].rearrange("p t m -> p m t"),
                 term_table[a][:].bitcast(U32).indirect(term_list[:, 32 * b : 32 * (b + 1)]),
             )
 
@@ -104,7 +107,7 @@ def tile_list_term_query_topics_kernel(
         gather_second_pass(0)
         gather_term_words(0, 0)
         gather_term_words(0, 1)
-        query_codes[1, 1] = shared.tile([P, BANK], U32, name="query_codes11", align_bytes=64, offset=28 * KIB)
+        query_codes[1, 1] = gathered.tile([P, BANK], U32, name="gathered", align_bytes=64)
         gather_second_pass(1)
 
         wd_raw = [keep.tile([P, PACK, N], F32, name=f"wd_raw{b}", align_bytes=64) for b in range(2)]
@@ -121,9 +124,17 @@ def tile_list_term_query_topics_kernel(
             )
         nc.sync.dma_start(out=wd_raw[1][:], in_=wd[PASS : 2 * PASS, :].rearrange("(p t) n -> p t n", t=PACK))
 
-        wd_codes = [keep.tile([P, N], U32, name=f"wd_codes{b}", align_bytes=64) for b in range(2)]
+        wd_codes = {}
         wd_planes = [keep.tile([P, N], U8, name=f"wd_planes{b}", align_bytes=64) for b in range(2)]
-        z_codes = [keep.tile([P, S2], U32, name=f"z_codes{b}", align_bytes=64) for b in range(2)]
+        z_tiles = {0: [], 1: []}
+
+        def new_z_codes(b, lo, hi):
+            z_tiles[b].append((lo, hi, turn.tile([P, hi - lo], U32, name="turn", align_bytes=64)))
+
+        def z_codes(b, lo, hi):
+            first, last, tile = [entry for entry in z_tiles[b] if entry[0] <= lo and hi <= entry[1]][0]
+            return tile[:, lo - first : hi - first].bitcast(FP8X4)
+
         z_planes = [keep.tile([P, S2], U8, name=f"z_planes{b}", align_bytes=64) for b in range(2)]
 
         def bank_tile(number, parts):
@@ -135,15 +146,16 @@ def tile_list_term_query_topics_kernel(
             return grouped
 
         def quantize_wd(grouped, b):
+            wd_codes[b] = turn.tile([P, N], U32, name="turn", align_bytes=64)
             nc.vector.quantize_mx(out=wd_codes[b][:].bitcast(FP8X4), scales=wd_planes[b][:], in_=grouped[:].rearrange("p n t -> p (n t)"))
 
-        def match_pass(banks, a, b, lo):
+        def match_pass(banks, a, b, lo, slots=range(PACK)):
             plane = planes[a][PLANE[a] :, :].bitcast(U8)
-            for t in range(PACK):
+            for t in slots:
                 first = PASS * b + P * t
                 nc.tensor.matmul_mx(
                     out=banks[t // 2][:, t % 2, :],
-                    lhsT=term_codes[a][:, b, t, :].bitcast(FP8X4),
+                    lhsT=term_codes[a, b][:, t, :].bitcast(FP8X4),
                     lhsT_scale=plane[:, first : first + P],
                     rhs=query_codes[a, lo // BANK][:, lo % BANK : lo % BANK + CHUNK].bitcast(FP8X4),
                     rhs_scale=plane[:, S + lo : S + lo + CHUNK],
@@ -153,8 +165,9 @@ def tile_list_term_query_topics_kernel(
 
         def matches(first_bank, b, lo):
             banks = [bank_tile(first_bank + u, 2) for u in range(2)]
-            match_pass(banks, 0, b, lo)
-            match_pass(banks, 1, b, lo)
+            for u in range(2):
+                for a in range(2):
+                    match_pass(banks, a, b, lo, range(2 * u, 2 * u + 2))
             return banks
 
         def new_kept():
@@ -174,21 +187,21 @@ def tile_list_term_query_topics_kernel(
 
         def weigh(logs, b):
             width = logs.shape[1]
-            z = rounded.tile([P, width, PACK], BF16, name="grouped", align_bytes=64)
+            z = turn.tile([P, width, PACK], BF16, name="turn", align_bytes=64)
             weights = idf_sb[:, b, :].unsqueeze(1).to_broadcast([P, width, PACK])
-            nc.vector.tensor_tensor(out=z[:], in0=logs[:].rearrange("p j u e -> p j (u e)"), in1=weights, op=ALU.mult)
+            nc.vector.tensor_tensor(out=z[:], in0=logs[:, :, :, :].rearrange("p j u e -> p j (u e)"), in1=weights, op=ALU.mult)
             return z
 
         def quantize_z(z, b, lo):
             cols = slice(lo, lo + z.shape[1])
-            nc.vector.quantize_mx(out=z_codes[b][:, cols].bitcast(FP8X4), scales=z_planes[b][:, cols], in_=z[:].rearrange("p j t -> p (j t)"))
+            nc.vector.quantize_mx(out=z_codes(b, lo, lo + z.shape[1]), scales=z_planes[b][:, cols], in_=z[:].rearrange("p j t -> p (j t)"))
 
         def packed_pass(acc, nt, b, lo, hi, start):
             nc.tensor.matmul_mx(
                 out=acc,
                 lhsT=w4_codes[:, b, :].bitcast(U8)[:, 2 * P * nt : 2 * P * (nt + 1)].bitcast(FP4X4),
                 lhsT_scale=w4_planes[:, b, :].bitcast(U8)[:, P * nt : P * (nt + 1)],
-                rhs=z_codes[b][:, lo:hi].bitcast(FP8X4),
+                rhs=z_codes(b, lo, hi),
                 rhs_scale=z_planes[b][:, lo:hi],
                 start=start,
                 stop=False,
@@ -199,7 +212,7 @@ def tile_list_term_query_topics_kernel(
                 out=acc,
                 lhsT=wd_codes[b][:, P * nt : P * (nt + 1)].bitcast(FP8X4),
                 lhsT_scale=wd_planes[b][:, P * nt : P * (nt + 1)],
-                rhs=z_codes[b][:, lo:hi].bitcast(FP8X4),
+                rhs=z_codes(b, lo, hi),
                 rhs_scale=z_planes[b][:, lo:hi],
                 start=False,
                 stop=stop,
@@ -215,9 +228,12 @@ def tile_list_term_query_topics_kernel(
                         packed_pass(bank[:, e, c : c + step], tiles * i + e, b, lo + c, lo + c + step, b == 0 and e == 0 and c == 0)
                     update_pass(bank[:, e, 0:width], tiles * i + e, b, lo, hi, b == 1 and e == tiles - 1)
 
-        def store(sums, first, lo, hi, tiles, on_vector):
+        def store(sums, first, lo, hi, tiles, on_vector, in_turn=False):
             for i, bank in enumerate(sums, first):
-                result = stage.tile([P, tiles, hi - lo], F32, name="result", align_bytes=64)
+                if in_turn:
+                    result = turn.tile([P, tiles, hi - lo], F32, name="turn", align_bytes=64)
+                else:
+                    result = stage.tile([P, tiles, hi - lo], F32, name="result", align_bytes=64)
                 if on_vector:
                     nc.vector.tensor_copy(out=result[:], in_=bank[:, 0:tiles, 0 : hi - lo])
                 else:
@@ -241,38 +257,40 @@ def tile_list_term_query_topics_kernel(
         drop_negatives(kept2, early[2], 0, False)
         logs0 = saturate(kept0, 0, CHUNK)
         drop_negatives(kept1, early[1], 0, True)
-        wd_rounded0 = round_wd(0)
         drop_negatives(kept1, early[1], 1, True)
+        wd_rounded0 = round_wd(0)
         drop_negatives(kept2, early[2], 1, False)
         logs1 = saturate(kept1, 0, CHUNK)
-        match4 = matches(0, 0, 512)
-        match5 = matches(2, 0, 768)
+        match4 = matches(4, 0, 512)
         kept3 = new_kept()
         drop_negatives(kept3, early[3], 0, False)
         logs2 = saturate(kept2, 0, CHUNK)
-        quantize_wd(wd_rounded0, 0)
         z0 = weigh(logs0, 0)
         z1 = weigh(logs1, 0)
+        quantize_wd(wd_rounded0, 0)
+        new_z_codes(0, 0, 512)
         quantize_z(z0, 0, 0)
         quantize_z(z1, 0, 256)
         drop_negatives(kept3, early[3], 1, False)
+        match5 = matches(6, 0, 768)
         kept4 = new_kept()
         drop_negatives(kept4, match4, 0, False)
         logs3 = saturate(kept3, 0, CHUNK)
         drop_negatives(kept4, match4, 1, False)
-        sums_half = [bank_tile(4 + nt, 1) for nt in range(4)]
+        sums_half = [bank_tile(nt, 1) for nt in range(4)]
         topic_passes(sums_half, 0, 0, 512)
-        match6 = matches(0, 1, 512)
+        match6 = matches(4, 1, 512)
         z2 = weigh(logs2, 1)
         wd_rounded1 = round_wd(1)
-        quantize_z(z2, 1, 0)
         kept5 = new_kept()
         drop_negatives(kept5, match5, 0, False)
         logs4 = saturate(kept4, 0, CHUNK)
         drop_negatives(kept5, match5, 1, False)
-        match7 = matches(2, 1, 768)
+        match7 = matches(6, 1, 768)
         z3 = weigh(logs3, 1)
         quantize_wd(wd_rounded1, 1)
+        new_z_codes(1, 0, 512)
+        quantize_z(z2, 1, 0)
         quantize_z(z3, 1, 256)
         kept6 = new_kept()
         drop_negatives(kept6, match6, 0, False)
@@ -281,27 +299,32 @@ def tile_list_term_query_topics_kernel(
         topic_passes(sums_half, 1, 0, 512)
         z4 = weigh(logs4, 0)
         z5 = weigh(logs5, 0)
+        new_z_codes(0, 512, 1024)
         quantize_z(z4, 0, 512)
         quantize_z(z5, 0, 768)
         kept7 = new_kept()
         drop_negatives(kept7, match7, 0, False)
         logs6 = saturate(kept6, 0, CHUNK)
         drop_negatives(kept7, match7, 1, False)
-        sums_quarter = [bank_tile(i, 2) for i in range(2)]
+        sums_quarter = [bank_tile(4 + i, 2) for i in range(2)]
         topic_passes(sums_quarter, 0, 512, 768)
-        store(sums_half[0:1], 0, 0, 512, 1, True)
+        store(sums_half[0:1], 0, 0, 512, 1, True, True)
         store(sums_half[1:2], 1, 0, 512, 1, False)
         logs7a = saturate(kept7, 0, P)
         logs7b = saturate(kept7, P, CHUNK)
-        z6 = weigh(logs6, 1)
-        quantize_z(z6, 1, 512)
-        sums_eighth = [bank_tile(4, 4)]
-        sums_last = [bank_tile(2 + i, 2) for i in range(2)]
-        topic_passes(sums_eighth, 0, 768, 896)
+        z6a = weigh(logs6[:, 0:P], 1)
+        z6b = weigh(logs6[:, P:CHUNK], 1)
+        new_z_codes(1, 512, 768)
+        quantize_z(z6a, 1, 512)
+        quantize_z(z6b, 1, 640)
+        sums_eighth = [bank_tile(0, 4)]
+        sums_last = [bank_tile(6 + i, 2) for i in range(2)]
         topic_passes(sums_last, 0, 896, 1024)
+        topic_passes(sums_eighth, 0, 768, 896)
         topic_passes(sums_quarter, 1, 512, 768)
         z7a = weigh(logs7a, 1)
         z7b = weigh(logs7b, 1)
+        new_z_codes(1, 768, 1024)
         quantize_z(z7a, 1, 768)
         topic_passes(sums_eighth, 1, 768, 896)
         quantize_z(z7b, 1, 896)

@@ -33,11 +33,11 @@ def tile_list_term_query_topics_kernel(
     with ExitStack() as ctx:
         keep = ctx.enter_context(tc.tile_pool(name="keep", bufs=1))
         shared = ctx.enter_context(tc.tile_pool(name="shared", bufs=1))
-        work = ctx.enter_context(tc.tile_pool(name="work", bufs=4))
-        stage = ctx.enter_context(tc.tile_pool(name="stage", bufs=8))
+        work = ctx.enter_context(tc.tile_pool(name="work", bufs=5))
+        stage = ctx.enter_context(tc.tile_pool(name="stage", bufs=9))
         rounded = ctx.enter_context(tc.tile_pool(name="rounded", bufs=2))
         gathered = ctx.enter_context(tc.tile_pool(name="gathered", bufs=5))
-        turn = ctx.enter_context(tc.tile_pool(name="turn", bufs=18))
+        turn = ctx.enter_context(tc.tile_pool(name="turn", bufs=27))
         psum = ctx.enter_context(tc.psum_pool(name="psum", bufs=1))
 
         term_list = keep.tile([P, S // 16], U16, name="term_list")
@@ -140,14 +140,24 @@ def tile_list_term_query_topics_kernel(
         def bank_tile(number, parts):
             return psum.tile([P, parts, BANK // parts], F32, name="bank", tag=f"bank{number}")
 
-        def round_wd(b):
-            grouped = rounded.tile([P, N, PACK], BF16, name="grouped", align_bytes=64)
-            nc.vector.tensor_copy(grouped[:].rearrange("p (c i) t -> p c t i", i=4), wd_raw[b][:].rearrange("p t (c i) -> p c t i", i=4))
-            return grouped
+        def round_wd(grouped, b, lo, hi):
+            nc.vector.tensor_copy(
+                grouped[:, lo:hi, :].rearrange("p (c i) t -> p c t i", i=4), wd_raw[b][:, :, lo:hi].rearrange("p t (c i) -> p c t i", i=4)
+            )
 
         def quantize_wd(grouped, b):
             wd_codes[b] = turn.tile([P, N], U32, name="turn", align_bytes=64)
             nc.vector.quantize_mx(out=wd_codes[b][:].bitcast(FP8X4), scales=wd_planes[b][:], in_=grouped[:].rearrange("p n t -> p (n t)"))
+
+        def round_wd_half(grouped, h):
+            nc.vector.tensor_copy(
+                grouped[:].rearrange("p (c i) t -> p c t i", i=4),
+                wd_raw[1][:, :, N // 2 * h : N // 2 * (h + 1)].rearrange("p t (c i) -> p c t i", i=4),
+            )
+
+        def quantize_wd_half(grouped, h):
+            cols = slice(N // 2 * h, N // 2 * (h + 1))
+            nc.vector.quantize_mx(out=wd_codes[1][:, cols].bitcast(FP8X4), scales=wd_planes[1][:, cols], in_=grouped[:].rearrange("p n t -> p (n t)"))
 
         def match_pass(banks, a, b, lo, slots=range(PACK)):
             plane = planes[a][PLANE[a] :, :].bitcast(U8)
@@ -181,7 +191,10 @@ def tile_list_term_query_topics_kernel(
                 nc.scalar.activation(out=kept[:, u, :, :], in_=side_by_side, func=ACT.Relu)
 
         def saturate(kept, lo, hi):
-            logs = work.tile([P, hi - lo, 2, 2], F32, name="logs", align_bytes=64)
+            if hi - lo == P:
+                logs = stage.tile([P, P, 2, 2], F32, name="result", align_bytes=64)
+            else:
+                logs = work.tile([P, CHUNK, 2, 2], F32, name="logs", align_bytes=64)
             nc.scalar.activation(out=logs[:], in_=kept[:, :, lo:hi, :].rearrange("p u j e -> p j u e"), func=ACT.Ln, bias=one[:])
             return logs
 
@@ -218,15 +231,18 @@ def tile_list_term_query_topics_kernel(
                 stop=stop,
             )
 
-        def topic_passes(sums, b, lo, hi):
+        def topic_passes(sums, b, lo, hi, origin=None, packed=True, update=True, closes=True):
+            origin = lo if origin is None else origin
             width = hi - lo
             step = width if width == BANK else P
             tiles = N // P // len(sums)
             for i, bank in enumerate(sums):
                 for e in range(tiles):
-                    for c in range(0, width, step):
-                        packed_pass(bank[:, e, c : c + step], tiles * i + e, b, lo + c, lo + c + step, b == 0 and e == 0 and c == 0)
-                    update_pass(bank[:, e, 0:width], tiles * i + e, b, lo, hi, b == 1 and e == tiles - 1)
+                    if packed:
+                        for c in range(lo, hi, step):
+                            packed_pass(bank[:, e, c - origin : c - origin + step], tiles * i + e, b, c, c + step, b == 0 and e == 0 and c == origin)
+                    if update:
+                        update_pass(bank[:, e, lo - origin : hi - origin], tiles * i + e, b, lo, hi, b == 1 and e == tiles - 1 and closes)
 
         def store(sums, first, lo, hi, tiles, on_vector, in_turn=False):
             for i, bank in enumerate(sums, first):
@@ -258,7 +274,8 @@ def tile_list_term_query_topics_kernel(
         logs0 = saturate(kept0, 0, CHUNK)
         drop_negatives(kept1, early[1], 0, True)
         drop_negatives(kept1, early[1], 1, True)
-        wd_rounded0 = round_wd(0)
+        wd_rounded0 = rounded.tile([P, N, PACK], BF16, name="grouped", align_bytes=64)
+        round_wd(wd_rounded0, 0, 0, N)
         drop_negatives(kept2, early[2], 1, False)
         logs1 = saturate(kept1, 0, CHUNK)
         match4 = matches(4, 0, 512)
@@ -281,56 +298,72 @@ def tile_list_term_query_topics_kernel(
         topic_passes(sums_half, 0, 0, 512)
         match6 = matches(4, 1, 512)
         z2 = weigh(logs2, 1)
-        wd_rounded1 = round_wd(1)
+        wd_halves = [turn.tile([P, N // 2, PACK], BF16, name="turn", align_bytes=64)]
+        round_wd_half(wd_halves[0], 0)
         kept5 = new_kept()
         drop_negatives(kept5, match5, 0, False)
         logs4 = saturate(kept4, 0, CHUNK)
         drop_negatives(kept5, match5, 1, False)
-        match7 = matches(6, 1, 768)
         z3 = weigh(logs3, 1)
-        quantize_wd(wd_rounded1, 1)
         new_z_codes(1, 0, 512)
         quantize_z(z2, 1, 0)
         quantize_z(z3, 1, 256)
+        topic_passes(sums_half, 1, 0, 512, update=False)
+        match7 = matches(6, 1, 768)
+        wd_halves.append(turn.tile([P, N // 2, PACK], BF16, name="turn", align_bytes=64))
+        round_wd_half(wd_halves[1], 1)
         kept6 = new_kept()
         drop_negatives(kept6, match6, 0, False)
         logs5 = saturate(kept5, 0, CHUNK)
         drop_negatives(kept6, match6, 1, False)
-        topic_passes(sums_half, 1, 0, 512)
+        wd_codes[1] = work.tile([P, N], U32, name="kept", align_bytes=64)
+        quantize_wd_half(wd_halves[0], 0)
         z4 = weigh(logs4, 0)
-        z5 = weigh(logs5, 0)
-        new_z_codes(0, 512, 1024)
+        new_z_codes(0, 512, 768)
+        quantize_wd_half(wd_halves[1], 1)
         quantize_z(z4, 0, 512)
-        quantize_z(z5, 0, 768)
+        topic_passes(sums_half, 1, 0, 512, packed=False)
+        z5 = weigh(logs5, 0)
         kept7 = new_kept()
         drop_negatives(kept7, match7, 0, False)
-        logs6 = saturate(kept6, 0, CHUNK)
+        logs6a = saturate(kept6, 0, P)
         drop_negatives(kept7, match7, 1, False)
+        logs6b = saturate(kept6, P, CHUNK)
         sums_quarter = [bank_tile(4 + i, 2) for i in range(2)]
         topic_passes(sums_quarter, 0, 512, 768)
         store(sums_half[0:1], 0, 0, 512, 1, True, True)
-        store(sums_half[1:2], 1, 0, 512, 1, False)
+        new_z_codes(0, 768, 1024)
+        quantize_z(z5, 0, 768)
+        shared_result = turn.tile([P, BANK], F32, name="turn", align_bytes=64)
+        nc.vector.tensor_copy(out=shared_result[:, 0:CHUNK], in_=sums_half[1][:, 0, 0:CHUNK])
+        nc.scalar.copy(out=shared_result[:, CHUNK:BANK], in_=sums_half[1][:, 0, CHUNK:BANK])
+        nc.sync.dma_start(out=out[P : 2 * P, 0:BANK], in_=shared_result[:])
         logs7a = saturate(kept7, 0, P)
+        store(sums_half[2:3], 2, 0, 512, 1, False)
         logs7b = saturate(kept7, P, CHUNK)
-        z6a = weigh(logs6[:, 0:P], 1)
-        z6b = weigh(logs6[:, P:CHUNK], 1)
-        new_z_codes(1, 512, 768)
-        quantize_z(z6a, 1, 512)
-        quantize_z(z6b, 1, 640)
         sums_eighth = [bank_tile(0, 4)]
         sums_last = [bank_tile(6 + i, 2) for i in range(2)]
-        topic_passes(sums_last, 0, 896, 1024)
         topic_passes(sums_eighth, 0, 768, 896)
-        topic_passes(sums_quarter, 1, 512, 768)
+        topic_passes(sums_last, 0, 896, 1024)
+        z6a = weigh(logs6a, 1)
+        z6b = weigh(logs6b, 1)
+        new_z_codes(1, 512, 640)
+        quantize_z(z6a, 1, 512)
+        topic_passes(sums_quarter, 1, 512, 640, closes=False)
         z7a = weigh(logs7a, 1)
-        z7b = weigh(logs7b, 1)
-        new_z_codes(1, 768, 1024)
+        new_z_codes(1, 640, 768)
+        quantize_z(z6b, 1, 640)
+        topic_passes(sums_quarter, 1, 640, 768, origin=512)
+        new_z_codes(1, 768, 896)
         quantize_z(z7a, 1, 768)
         topic_passes(sums_eighth, 1, 768, 896)
+        z7b = weigh(logs7b, 1)
+        new_z_codes(1, 896, 1024)
         quantize_z(z7b, 1, 896)
         topic_passes(sums_last, 1, 896, 1024)
-        store(sums_half[2:4], 2, 0, 512, 1, False)
-        store(sums_quarter, 0, 512, 768, 2, False)
-        store(sums_eighth, 0, 768, 896, 4, True)
+        store(sums_half[3:4], 3, 0, 512, 1, False)
+        store(sums_quarter[0:1], 0, 512, 768, 2, False)
+        store(sums_quarter[1:2], 1, 512, 768, 2, False)
+        store(sums_eighth, 0, 768, 896, 4, True, True)
         store(sums_last[0:1], 0, 896, 1024, 2, False)
-        store(sums_last[1:2], 1, 896, 1024, 2, True)
+        store(sums_last[1:2], 1, 896, 1024, 2, True, True)

@@ -36,7 +36,7 @@ def tile_list_term_query_topics_kernel(
         work = ctx.enter_context(tc.tile_pool(name="work", bufs=5))
         stage = ctx.enter_context(tc.tile_pool(name="stage", bufs=9))
         rounded = ctx.enter_context(tc.tile_pool(name="rounded", bufs=2))
-        gathered = ctx.enter_context(tc.tile_pool(name="gathered", bufs=5))
+        gathered = ctx.enter_context(tc.tile_pool(name="gathered", bufs=7))
         turn = ctx.enter_context(tc.tile_pool(name="turn", bufs=27))
         psum = ctx.enter_context(tc.psum_pool(name="psum", bufs=1))
 
@@ -48,8 +48,8 @@ def tile_list_term_query_topics_kernel(
         idf_sb = keep.tile([P, 2, PACK], F32, name="idf_sb", align_bytes=64)
         one = keep.tile([P, 1], F32, name="one")
         warm = keep.tile([P, 1], F32, name="warm")
-        query_table = shared.tile([P, 2, T2], I32, name="query_table", align_bytes=64, offset=0)
-        term_table = [shared.tile([P, T], I32, name=f"term_table{a}", align_bytes=64, offset=16 * KIB * (a + 1)) for a in range(2)]
+        query_table = [shared.tile([P, T2], I32, name=f"query_table{a}", align_bytes=64) for a in range(2)]
+        term_table = [shared.tile([P, T], I32, name=f"term_table{a}", align_bytes=64) for a in range(2)]
 
         nc.vector.memset(one[:], 1.0)
         nc.scalar.activation(out=warm[:], in_=one[:], func=ACT.Ln)
@@ -61,17 +61,20 @@ def tile_list_term_query_topics_kernel(
         nc.sync.dma_start(out=term_scale_table[ROW0:, :], in_=tab_scales.rearrange("a q n -> (a q) n").bitcast(I32))
         nc.sync.dma_start(query_list[:], offs2)
         nc.sync.dma_start(out=query_scale_table[ROW0:, :], in_=tab2_scales.rearrange("a q n -> (a q) n").bitcast(I32))
-        nc.sync.dma_start(out=query_table[:], in_=tab2_words.rearrange("a p n t -> p a (n t)").bitcast(I32))
+
+        def load_query_words(a):
+            nc.sync.dma_start(out=query_table[a][:], in_=tab2_words[a].rearrange("p n t -> p (n t)").bitcast(I32))
 
         def load_term_words(a):
             nc.sync.dma_start(out=term_table[a][:], in_=tab_words[a].rearrange("p n t -> p (n t)").bitcast(I32))
 
+        load_query_words(0)
         load_term_words(0)
+        load_term_words(1)
 
         term_codes = {}
         first_pass = keep.tile([P, S2], U32, name="query_codes0", align_bytes=64)
-        query_codes = {(0, h): first_pass[:, BANK * h : BANK * (h + 1)] for h in range(2)}
-        query_codes[1, 0] = keep.tile([P, BANK], U32, name="query_codes10", align_bytes=64)
+        query_codes = {(0, lo): first_pass[:, lo : lo + CHUNK] for lo in range(0, S2, CHUNK)}
         term_scales = keep.tile([P, S], U8, name="term_scales", align_bytes=64)
         query_scales = keep.tile([P, S2], U8, name="query_scales", align_bytes=64)
 
@@ -89,12 +92,16 @@ def tile_list_term_query_topics_kernel(
 
         for q in range(3):
             move_rows(0, q)
-        load_term_words(1)
-        for q in range(4):
+        for q in range(3):
             move_rows(1, q)
+        load_query_words(1)
+        move_rows(1, 3)
 
-        def gather_second_pass(h):
-            nc.vector.tensor_copy(query_codes[1, h][:], query_table[:, 1, :].bitcast(U32).indirect(query_list[:, 32 * h : 32 * (h + 1)]))
+        def gather_second_pass(lo, hi):
+            codes = gathered.tile([P, hi - lo], U32, name="gathered", align_bytes=64)
+            nc.vector.tensor_copy(codes[:], query_table[1][:].bitcast(U32).indirect(query_list[:, lo // 16 : hi // 16]))
+            for c in range(lo, hi, CHUNK):
+                query_codes[1, c] = codes[:, c - lo : c - lo + CHUNK]
 
         def gather_term_words(a, b):
             term_codes[a, b] = gathered.tile([P, PACK, P], U32, name="gathered", align_bytes=64)
@@ -103,12 +110,13 @@ def tile_list_term_query_topics_kernel(
                 term_table[a][:].bitcast(U32).indirect(term_list[:, 32 * b : 32 * (b + 1)]),
             )
 
-        nc.vector.tensor_copy(first_pass[:], query_table[:, 0, :].bitcast(U32).indirect(query_list[:]))
-        gather_second_pass(0)
-        gather_term_words(0, 0)
-        gather_term_words(0, 1)
-        query_codes[1, 1] = gathered.tile([P, BANK], U32, name="gathered", align_bytes=64)
-        gather_second_pass(1)
+        nc.vector.tensor_copy(first_pass[:], query_table[0][:].bitcast(U32).indirect(query_list[:]))
+        for a in range(2):
+            for b in range(2):
+                gather_term_words(a, b)
+        gather_second_pass(0, 256)
+        gather_second_pass(256, 512)
+        gather_second_pass(512, 1024)
 
         wd_raw = [keep.tile([P, PACK, N], F32, name=f"wd_raw{b}", align_bytes=64) for b in range(2)]
         w4_codes = keep.tile([P, 2, 2 * N // 4], I32, name="w4_codes", align_bytes=64)
@@ -159,7 +167,7 @@ def tile_list_term_query_topics_kernel(
             cols = slice(N // 2 * h, N // 2 * (h + 1))
             nc.vector.quantize_mx(out=wd_codes[1][:, cols].bitcast(FP8X4), scales=wd_planes[1][:, cols], in_=grouped[:].rearrange("p n t -> p (n t)"))
 
-        def match_pass(banks, a, b, lo, slots=range(PACK)):
+        def match_pass(banks, a, b, lo, slots=range(PACK), first_pass_number=0):
             plane = planes[a][PLANE[a] :, :].bitcast(U8)
             for t in slots:
                 first = PASS * b + P * t
@@ -167,10 +175,10 @@ def tile_list_term_query_topics_kernel(
                     out=banks[t // 2][:, t % 2, :],
                     lhsT=term_codes[a, b][:, t, :].bitcast(FP8X4),
                     lhsT_scale=plane[:, first : first + P],
-                    rhs=query_codes[a, lo // BANK][:, lo % BANK : lo % BANK + CHUNK].bitcast(FP8X4),
+                    rhs=query_codes[a, lo].bitcast(FP8X4),
                     rhs_scale=plane[:, S + lo : S + lo + CHUNK],
-                    start=(a == 0 and t % 2 == 0),
-                    stop=(a == 1 and t % 2 == 1),
+                    start=(a == first_pass_number and t % 2 == 0),
+                    stop=(a != first_pass_number and t % 2 == 1),
                 )
 
         def matches(first_bank, b, lo):
@@ -258,12 +266,13 @@ def tile_list_term_query_topics_kernel(
                 nc.sync.dma_start(out=rows.rearrange("(e p) j -> p e j", p=P), in_=result[:])
 
         early = [[bank_tile(2 * n + u, 2) for u in range(2)] for n in range(4)]
-        for n in range(4):
-            match_pass(early[n], 0, n // 2, CHUNK * (n % 2))
-        gather_term_words(1, 0)
-        gather_term_words(1, 1)
-        for n in range(4):
-            match_pass(early[n], 1, n // 2, CHUNK * (n % 2))
+        for a in range(2):
+            for n in (0, 2):
+                match_pass(early[n], a, n // 2, 0)
+        for n in (1, 3):
+            for u in range(2):
+                for a in (1, 0):
+                    match_pass(early[n], a, n // 2, CHUNK, range(2 * u, 2 * u + 2), first_pass_number=1)
 
         kept0 = new_kept()
         drop_negatives(kept0, early[0], 0, False)

@@ -1,6 +1,7 @@
 from contextlib import ExitStack
 
 import concourse.mybir as mybir
+from concourse.masks import make_identity
 
 K, T, S, T2, S2, N = 1024, 4096, 1024, 2048, 1024, 512
 FLOPS = 2 * K * S * S2 + 2 * 2 * S * N * S2
@@ -33,9 +34,7 @@ def tile_list_term_query_topics_kernel(
     with ExitStack() as ctx:
         keep = ctx.enter_context(tc.tile_pool(name="keep", bufs=1))
         shared = ctx.enter_context(tc.tile_pool(name="shared", bufs=1))
-        work = ctx.enter_context(tc.tile_pool(name="work", bufs=5))
-        stage = ctx.enter_context(tc.tile_pool(name="stage", bufs=9))
-        rounded = ctx.enter_context(tc.tile_pool(name="rounded", bufs=2))
+        work = ctx.enter_context(tc.tile_pool(name="work", bufs=14))
         gathered = ctx.enter_context(tc.tile_pool(name="gathered", bufs=7))
         turn = ctx.enter_context(tc.tile_pool(name="turn", bufs=27))
         psum = ctx.enter_context(tc.psum_pool(name="psum", bufs=1))
@@ -48,7 +47,7 @@ def tile_list_term_query_topics_kernel(
         idf_sb = keep.tile([P, 2, PACK], F32, name="idf_sb", align_bytes=64)
         one = keep.tile([P, 1], F32, name="one")
         warm = keep.tile([P, 1], F32, name="warm")
-        query_table = [shared.tile([P, T2], I32, name=f"query_table{a}", align_bytes=64) for a in range(2)]
+        query_table = [shared.tile([P, T2], I32, name=f"query_table{a}", tag=f"query_table{a}", align_bytes=64) for a in range(2)]
         term_table = [shared.tile([P, T], I32, name=f"term_table{a}", align_bytes=64) for a in range(2)]
 
         nc.vector.memset(one[:], 1.0)
@@ -56,6 +55,10 @@ def tile_list_term_query_topics_kernel(
         for table in (term_scale_table, query_scale_table):
             nc.vector.memset(table[0:ROW0, :], 0)
         nc.vector.memset(planes[1][:], 0)
+        idf_rows = keep.tile([P, PASS], F32, name="idf_rows", align_bytes=64)
+        identity = keep.tile([P, P], F32, name="identity", align_bytes=64)
+        nc.gpsimd.memset(idf_rows[:], 0.0)
+        make_identity(nc, identity[:])
 
         nc.sync.dma_start(term_list[:], offs)
         nc.sync.dma_start(out=term_scale_table[ROW0:, :], in_=tab_scales.rearrange("a q n -> (a q) n").bitcast(I32))
@@ -69,6 +72,7 @@ def tile_list_term_query_topics_kernel(
             nc.sync.dma_start(out=term_table[a][:], in_=tab_words[a].rearrange("p n t -> p (n t)").bitcast(I32))
 
         load_query_words(0)
+        nc.sync.dma_start(out=idf_rows[0:2, :], in_=idf.rearrange("(b i) -> b i", b=2))
         load_term_words(0)
         load_term_words(1)
 
@@ -123,14 +127,13 @@ def tile_list_term_query_topics_kernel(
         w4_planes = keep.tile([P, 2, N // 4], I32, name="w4_planes", align_bytes=64)
         nc.vector.memset(w4_planes[:], 0)
         nc.sync.dma_start(out=wd_raw[0][:], in_=wd[0:PASS, :].rearrange("(p t) n -> p t n", t=PACK))
-        nc.sync.dma_start(out=idf_sb[:], in_=idf.rearrange("(b p t) -> p b t", b=2, t=PACK))
+        nc.sync.dma_start(out=wd_raw[1][:], in_=wd[PASS : 2 * PASS, :].rearrange("(p t) n -> p t n", t=PACK))
         nc.sync.dma_start(out=w4_codes[:], in_=w4_words.bitcast(I32).rearrange("b p c -> p b c"))
         for q in range(4):
             nc.sync.dma_start(
                 out=w4_planes[32 * q : 32 * q + 4, :, :],
                 in_=w4_scales[:, 4 * q : 4 * q + 4, :].bitcast(I32).rearrange("b r c -> r b c"),
             )
-        nc.sync.dma_start(out=wd_raw[1][:], in_=wd[PASS : 2 * PASS, :].rearrange("(p t) n -> p t n", t=PACK))
 
         wd_codes = {}
         wd_planes = [keep.tile([P, N], U8, name=f"wd_planes{b}", align_bytes=64) for b in range(2)]
@@ -148,24 +151,22 @@ def tile_list_term_query_topics_kernel(
         def bank_tile(number, parts):
             return psum.tile([P, parts, BANK // parts], F32, name="bank", tag=f"bank{number}")
 
+        idf_bank = bank_tile(7, PACK)
+        for t in range(PACK):
+            nc.tensor.transpose(idf_bank[:, t, :], idf_rows[:, t:PASS:PACK], identity[:])
+        nc.scalar.copy(out=idf_sb[:].rearrange("p b t -> p t b"), in_=idf_bank[:, :, 0:2])
+
         def round_wd(grouped, b, lo, hi):
-            nc.vector.tensor_copy(
-                grouped[:, lo:hi, :].rearrange("p (c i) t -> p c t i", i=4), wd_raw[b][:, :, lo:hi].rearrange("p t (c i) -> p c t i", i=4)
+            nc.gpsimd.tensor_scalar(
+                out=grouped[:], in0=wd_raw[b][:, :, lo:hi].rearrange("p t n -> p n t"), scalar1=1.0, scalar2=0.0, op0=ALU.mult, op1=ALU.add
             )
 
-        def quantize_wd(grouped, b):
-            wd_codes[b] = turn.tile([P, N], U32, name="turn", align_bytes=64)
-            nc.vector.quantize_mx(out=wd_codes[b][:].bitcast(FP8X4), scales=wd_planes[b][:], in_=grouped[:].rearrange("p n t -> p (n t)"))
-
-        def round_wd_half(grouped, h):
-            nc.vector.tensor_copy(
-                grouped[:].rearrange("p (c i) t -> p c t i", i=4),
-                wd_raw[1][:, :, N // 2 * h : N // 2 * (h + 1)].rearrange("p t (c i) -> p c t i", i=4),
+        def quantize_wd(grouped, b, lo, hi):
+            if lo == 0:
+                wd_codes[b] = turn.tile([P, N], U32, name="turn", align_bytes=64)
+            nc.vector.quantize_mx(
+                out=wd_codes[b][:, lo:hi].bitcast(FP8X4), scales=wd_planes[b][:, lo:hi], in_=grouped[:].rearrange("p n t -> p (n t)")
             )
-
-        def quantize_wd_half(grouped, h):
-            cols = slice(N // 2 * h, N // 2 * (h + 1))
-            nc.vector.quantize_mx(out=wd_codes[1][:, cols].bitcast(FP8X4), scales=wd_planes[1][:, cols], in_=grouped[:].rearrange("p n t -> p (n t)"))
 
         def match_pass(banks, a, b, lo, slots=range(PACK), first_pass_number=0):
             plane = planes[a][PLANE[a] :, :].bitcast(U8)
@@ -181,15 +182,20 @@ def tile_list_term_query_topics_kernel(
                     stop=(a != first_pass_number and t % 2 == 1),
                 )
 
-        def matches(first_bank, b, lo):
-            banks = [bank_tile(first_bank + u, 2) for u in range(2)]
+        def match_bank(banks, u, b, lo):
+            for a in range(2):
+                match_pass(banks, a, b, lo, range(2 * u, 2 * u + 2))
+
+        def matches(numbers, b, lo):
+            banks = [bank_tile(number, 2) for number in numbers]
             for u in range(2):
-                for a in range(2):
-                    match_pass(banks, a, b, lo, range(2 * u, 2 * u + 2))
+                match_bank(banks, u, b, lo)
             return banks
 
-        def new_kept():
-            return work.tile([P, 2, CHUNK, 2], F32, name="kept", align_bytes=64)
+        def new_kept(on_vector=False):
+            if on_vector:
+                return shared.tile([P, 2, CHUNK, 2], F32, name="kept", tag="kept", bufs=2, align_bytes=64)
+            return work.tile([P, 2, CHUNK, 2], F32, name="work", align_bytes=64)
 
         def drop_negatives(kept, banks, u, on_vector):
             side_by_side = banks[u][:].rearrange("p e j -> p j e")
@@ -199,17 +205,15 @@ def tile_list_term_query_topics_kernel(
                 nc.scalar.activation(out=kept[:, u, :, :], in_=side_by_side, func=ACT.Relu)
 
         def saturate(kept, lo, hi):
-            if hi - lo == P:
-                logs = stage.tile([P, P, 2, 2], F32, name="result", align_bytes=64)
-            else:
-                logs = work.tile([P, CHUNK, 2, 2], F32, name="logs", align_bytes=64)
+            logs = work.tile([P, hi - lo, 2, 2], F32, name="work", align_bytes=64)
             nc.scalar.activation(out=logs[:], in_=kept[:, :, lo:hi, :].rearrange("p u j e -> p j u e"), func=ACT.Ln, bias=one[:])
             return logs
 
-        def weigh(logs, b):
+        def weigh(logs, b, from_psum=False):
             width = logs.shape[1]
             z = turn.tile([P, width, PACK], BF16, name="turn", align_bytes=64)
-            weights = idf_sb[:, b, :].unsqueeze(1).to_broadcast([P, width, PACK])
+            source = idf_bank[:, :, b] if from_psum else idf_sb[:, b, :]
+            weights = source.unsqueeze(1).to_broadcast([P, width, PACK])
             nc.vector.tensor_tensor(out=z[:], in0=logs[:, :, :, :].rearrange("p j u e -> p j (u e)"), in1=weights, op=ALU.mult)
             return z
 
@@ -252,12 +256,12 @@ def tile_list_term_query_topics_kernel(
                     if update:
                         update_pass(bank[:, e, lo - origin : hi - origin], tiles * i + e, b, lo, hi, b == 1 and e == tiles - 1 and closes)
 
-        def store(sums, first, lo, hi, tiles, on_vector, in_turn=False):
+        def store(sums, first, lo, hi, tiles, on_vector):
             for i, bank in enumerate(sums, first):
-                if in_turn:
+                if on_vector:
                     result = turn.tile([P, tiles, hi - lo], F32, name="turn", align_bytes=64)
                 else:
-                    result = stage.tile([P, tiles, hi - lo], F32, name="result", align_bytes=64)
+                    result = work.tile([P, tiles, hi - lo], F32, name="work", align_bytes=64)
                 if on_vector:
                     nc.vector.tensor_copy(out=result[:], in_=bank[:, 0:tiles, 0 : hi - lo])
                 else:
@@ -265,95 +269,110 @@ def tile_list_term_query_topics_kernel(
                 rows = out[P * tiles * i : P * tiles * (i + 1), lo:hi]
                 nc.sync.dma_start(out=rows.rearrange("(e p) j -> p e j", p=P), in_=result[:])
 
-        early = [[bank_tile(2 * n + u, 2) for u in range(2)] for n in range(4)]
+        def half_pass(kind, bank, nt, b):
+            if kind == "packed":
+                packed_pass(bank[:, 0, :], nt, b, 0, BANK, b == 0)
+            else:
+                update_pass(bank[:, 0, :], nt, b, 0, BANK, b == 1)
+
+        match0 = [bank_tile(u, 2) for u in range(2)]
+        match2 = [bank_tile(2 + u, 2) for u in range(2)]
         for a in range(2):
-            for n in (0, 2):
-                match_pass(early[n], a, n // 2, 0)
-        for n in (1, 3):
-            for u in range(2):
-                for a in (1, 0):
-                    match_pass(early[n], a, n // 2, CHUNK, range(2 * u, 2 * u + 2), first_pass_number=1)
+            match_pass(match0, a, 0, 0)
+            match_pass(match2, a, 1, 0)
+        match1 = [bank_tile(4 + u, 2) for u in range(2)]
+        for u in range(2):
+            for a in (1, 0):
+                match_pass(match1, a, 0, CHUNK, range(2 * u, 2 * u + 2), first_pass_number=1)
 
         kept0 = new_kept()
-        drop_negatives(kept0, early[0], 0, False)
-        drop_negatives(kept0, early[0], 1, False)
-        kept1 = new_kept()
+        drop_negatives(kept0, match0, 0, False)
+        match3 = [bank_tile(number, 2) for number in (6, 0)]
+        for u in range(2):
+            for a in (1, 0):
+                match_pass(match3, a, 1, CHUNK, range(2 * u, 2 * u + 2), first_pass_number=1)
+        drop_negatives(kept0, match0, 1, False)
         kept2 = new_kept()
-        drop_negatives(kept2, early[2], 0, False)
-        logs0 = saturate(kept0, 0, CHUNK)
-        drop_negatives(kept1, early[1], 0, True)
-        drop_negatives(kept1, early[1], 1, True)
-        wd_rounded0 = rounded.tile([P, N, PACK], BF16, name="grouped", align_bytes=64)
+        drop_negatives(kept2, match2, 0, False)
+        wd_rounded0 = shared.tile([P, N, PACK], BF16, name="wd_rounded0", tag="query_table1", align_bytes=64)
         round_wd(wd_rounded0, 0, 0, N)
-        drop_negatives(kept2, early[2], 1, False)
+        wd_rounded1a = keep.tile([P, N // 2, PACK], BF16, name="wd_rounded1a", align_bytes=64)
+        round_wd(wd_rounded1a, 1, 0, N // 2)
+        logs0 = saturate(kept0, 0, CHUNK)
+        kept1 = new_kept(True)
+        drop_negatives(kept1, match1, 0, True)
+        drop_negatives(kept1, match1, 1, True)
+        match4 = matches((1, 2), 0, 512)
+        drop_negatives(kept2, match2, 1, False)
+        kept3 = new_kept(True)
+        drop_negatives(kept3, match3, 0, True)
+        drop_negatives(kept3, match3, 1, True)
+        match5 = matches((3, 4), 0, 768)
+        match6 = matches((5, 6), 1, 512)
         logs1 = saturate(kept1, 0, CHUNK)
-        match4 = matches(4, 0, 512)
-        kept3 = new_kept()
-        drop_negatives(kept3, early[3], 0, False)
+        z0 = weigh(logs0, 0, True)
+        z1 = weigh(logs1, 0, True)
+        kept4 = new_kept()
+        drop_negatives(kept4, match4, 0, False)
         logs2 = saturate(kept2, 0, CHUNK)
-        z0 = weigh(logs0, 0)
-        z1 = weigh(logs1, 0)
-        quantize_wd(wd_rounded0, 0)
+        drop_negatives(kept4, match4, 1, False)
         new_z_codes(0, 0, 512)
         quantize_z(z0, 0, 0)
         quantize_z(z1, 0, 256)
-        drop_negatives(kept3, early[3], 1, False)
-        match5 = matches(6, 0, 768)
-        kept4 = new_kept()
-        drop_negatives(kept4, match4, 0, False)
+        quantize_wd(wd_rounded0, 0, 0, N)
+        wd_rounded1b = shared.tile([P, N // 2, PACK], BF16, name="wd_rounded1b", tag="query_table1", align_bytes=64)
+        round_wd(wd_rounded1b, 1, N // 2, N)
         logs3 = saturate(kept3, 0, CHUNK)
-        drop_negatives(kept4, match4, 1, False)
-        sums_half = [bank_tile(nt, 1) for nt in range(4)]
-        topic_passes(sums_half, 0, 0, 512)
-        match6 = matches(4, 1, 512)
-        z2 = weigh(logs2, 1)
-        wd_halves = [turn.tile([P, N // 2, PACK], BF16, name="turn", align_bytes=64)]
-        round_wd_half(wd_halves[0], 0)
         kept5 = new_kept()
         drop_negatives(kept5, match5, 0, False)
+        sums_half = [bank_tile(nt, 1) for nt in range(4)]
+        for kind in ("packed", "update"):
+            for nt in range(3):
+                half_pass(kind, sums_half[nt], nt, 0)
+        for kind in ("packed", "update"):
+            half_pass(kind, sums_half[3], 3, 0)
+        z2 = weigh(logs2, 1, True)
+        z3 = weigh(logs3, 1, True)
         logs4 = saturate(kept4, 0, CHUNK)
         drop_negatives(kept5, match5, 1, False)
-        z3 = weigh(logs3, 1)
+        match7 = [bank_tile(number, 2) for number in (7, 4)]
+        match_bank(match7, 0, 1, 768)
         new_z_codes(1, 0, 512)
         quantize_z(z2, 1, 0)
+        quantize_wd(wd_rounded1a, 1, 0, N // 2)
         quantize_z(z3, 1, 256)
-        topic_passes(sums_half, 1, 0, 512, update=False)
-        match7 = matches(6, 1, 768)
-        wd_halves.append(turn.tile([P, N // 2, PACK], BF16, name="turn", align_bytes=64))
-        round_wd_half(wd_halves[1], 1)
+        quantize_wd(wd_rounded1b, 1, N // 2, N)
+        for nt in range(4):
+            for kind in ("packed", "update"):
+                half_pass(kind, sums_half[nt], nt, 1)
+        match_bank(match7, 1, 1, 768)
         kept6 = new_kept()
         drop_negatives(kept6, match6, 0, False)
         logs5 = saturate(kept5, 0, CHUNK)
         drop_negatives(kept6, match6, 1, False)
-        wd_codes[1] = work.tile([P, N], U32, name="kept", align_bytes=64)
-        quantize_wd_half(wd_halves[0], 0)
         z4 = weigh(logs4, 0)
+        store(sums_half[0:1], 0, 0, 512, 1, True)
         new_z_codes(0, 512, 768)
-        quantize_wd_half(wd_halves[1], 1)
         quantize_z(z4, 0, 512)
-        topic_passes(sums_half, 1, 0, 512, packed=False)
+        sums_quarter = [bank_tile(5 + i, 2) for i in range(2)]
+        topic_passes(sums_quarter, 0, 512, 768)
         z5 = weigh(logs5, 0)
+        store(sums_half[1:2], 1, 0, 512, 1, True)
+        new_z_codes(0, 768, 1024)
+        quantize_z(z5, 0, 768)
         kept7 = new_kept()
         drop_negatives(kept7, match7, 0, False)
         logs6a = saturate(kept6, 0, P)
         drop_negatives(kept7, match7, 1, False)
         logs6b = saturate(kept6, P, CHUNK)
-        sums_quarter = [bank_tile(4 + i, 2) for i in range(2)]
-        topic_passes(sums_quarter, 0, 512, 768)
-        store(sums_half[0:1], 0, 0, 512, 1, True, True)
-        new_z_codes(0, 768, 1024)
-        quantize_z(z5, 0, 768)
-        shared_result = turn.tile([P, BANK], F32, name="turn", align_bytes=64)
-        nc.vector.tensor_copy(out=shared_result[:, 0:CHUNK], in_=sums_half[1][:, 0, 0:CHUNK])
-        nc.scalar.copy(out=shared_result[:, CHUNK:BANK], in_=sums_half[1][:, 0, CHUNK:BANK])
-        nc.sync.dma_start(out=out[P : 2 * P, 0:BANK], in_=shared_result[:])
+        sums_eighth = [bank_tile(0, 4)]
+        sums_last = [bank_tile(number, 2) for number in (7, 1)]
+        topic_passes(sums_eighth, 0, 768, 896)
+        topic_passes(sums_last, 0, 896, 1024)
         logs7a = saturate(kept7, 0, P)
         store(sums_half[2:3], 2, 0, 512, 1, False)
         logs7b = saturate(kept7, P, CHUNK)
-        sums_eighth = [bank_tile(0, 4)]
-        sums_last = [bank_tile(6 + i, 2) for i in range(2)]
-        topic_passes(sums_eighth, 0, 768, 896)
-        topic_passes(sums_last, 0, 896, 1024)
+        store(sums_half[3:4], 3, 0, 512, 1, False)
         z6a = weigh(logs6a, 1)
         z6b = weigh(logs6b, 1)
         new_z_codes(1, 512, 640)
@@ -370,9 +389,8 @@ def tile_list_term_query_topics_kernel(
         new_z_codes(1, 896, 1024)
         quantize_z(z7b, 1, 896)
         topic_passes(sums_last, 1, 896, 1024)
-        store(sums_half[3:4], 3, 0, 512, 1, False)
         store(sums_quarter[0:1], 0, 512, 768, 2, False)
         store(sums_quarter[1:2], 1, 512, 768, 2, False)
-        store(sums_eighth, 0, 768, 896, 4, True, True)
+        store(sums_eighth, 0, 768, 896, 4, True)
         store(sums_last[0:1], 0, 896, 1024, 2, False)
-        store(sums_last[1:2], 1, 896, 1024, 2, True, True)
+        store(sums_last[1:2], 1, 896, 1024, 2, True)

@@ -303,7 +303,7 @@ def tile_list_term_query_topics_kernel(
         drop_negatives(kept1, match1, 0, True)
         drop_negatives(kept1, match1, 1, True)
         match4 = matches((1, 2), 0, 512)
-        drop_negatives(kept2, match2, 1, False)
+        drop_negatives(kept2, match2, 1, True)
         kept3 = new_kept(True)
         drop_negatives(kept3, match3, 0, True)
         drop_negatives(kept3, match3, 1, True)
@@ -333,31 +333,32 @@ def tile_list_term_query_topics_kernel(
             half_pass(kind, sums_half[3], 3, 0)
         z2 = weigh(logs2, 1, True)
         z3 = weigh(logs3, 1, True)
-        logs4 = saturate(kept4, 0, CHUNK)
         drop_negatives(kept5, match5, 1, False)
-        match7 = [bank_tile(number, 2) for number in (7, 4)]
-        match_bank(match7, 0, 1, 768)
+        logs4 = saturate(kept4, 0, CHUNK)
+        match7 = matches((4, 7), 1, 768)
         new_z_codes(1, 0, 512)
         quantize_z(z2, 1, 0)
-        quantize_wd(wd_rounded1a, 1, 0, N // 2)
         quantize_z(z3, 1, 256)
+        quantize_wd(wd_rounded1a, 1, 0, N // 2)
         quantize_wd(wd_rounded1b, 1, N // 2, N)
-        for nt in range(4):
+        for pair in range(2):
             for kind in ("packed", "update"):
-                half_pass(kind, sums_half[nt], nt, 1)
-        match_bank(match7, 1, 1, 768)
+                for nt in (2 * pair, 2 * pair + 1):
+                    half_pass(kind, sums_half[nt], nt, 1)
         kept6 = new_kept()
         drop_negatives(kept6, match6, 0, False)
         logs5 = saturate(kept5, 0, CHUNK)
         drop_negatives(kept6, match6, 1, False)
         z4 = weigh(logs4, 0)
-        store(sums_half[0:1], 0, 0, 512, 1, True)
+        first_result = turn.tile([P, BANK], F32, name="turn", align_bytes=64)
+        nc.vector.tensor_copy(out=first_result[:, 0:CHUNK], in_=sums_half[0][:, 0, 0:CHUNK])
         new_z_codes(0, 512, 768)
         quantize_z(z4, 0, 512)
         sums_quarter = [bank_tile(5 + i, 2) for i in range(2)]
         topic_passes(sums_quarter, 0, 512, 768)
         z5 = weigh(logs5, 0)
-        store(sums_half[1:2], 1, 0, 512, 1, True)
+        nc.vector.tensor_copy(out=first_result[:, CHUNK:BANK], in_=sums_half[0][:, 0, CHUNK:BANK])
+        nc.sync.dma_start(out=out[0:P, 0:BANK], in_=first_result[:])
         new_z_codes(0, 768, 1024)
         quantize_z(z5, 0, 768)
         kept7 = new_kept()
@@ -365,10 +366,11 @@ def tile_list_term_query_topics_kernel(
         logs6a = saturate(kept6, 0, P)
         drop_negatives(kept7, match7, 1, False)
         logs6b = saturate(kept6, P, CHUNK)
-        sums_eighth = [bank_tile(0, 4)]
-        sums_last = [bank_tile(number, 2) for number in (7, 1)]
+        sums_eighth = [bank_tile(4, 4)]
+        sums_last = [bank_tile(number, 2) for number in (0, 7)]
         topic_passes(sums_eighth, 0, 768, 896)
         topic_passes(sums_last, 0, 896, 1024)
+        store(sums_half[1:2], 1, 0, 512, 1, False)
         logs7a = saturate(kept7, 0, P)
         store(sums_half[2:3], 2, 0, 512, 1, False)
         logs7b = saturate(kept7, P, CHUNK)

@@ -22,9 +22,10 @@ PACK = 4
 PASS = P * PACK
 BANK = 512
 CHUNK = 256
+TILES = N // P
 ROW0 = 96
 PLANE = (12, 0)
-KIB = 1024
+HALF, QUARTER, EIGHTH, LAST = (0, 512), (512, 768), (768, 896), (896, 1024)
 
 
 def tile_list_term_query_topics_kernel(
@@ -34,9 +35,9 @@ def tile_list_term_query_topics_kernel(
     with ExitStack() as ctx:
         keep = ctx.enter_context(tc.tile_pool(name="keep", bufs=1))
         shared = ctx.enter_context(tc.tile_pool(name="shared", bufs=1))
-        work = ctx.enter_context(tc.tile_pool(name="work", bufs=14))
+        scalar_out = ctx.enter_context(tc.tile_pool(name="scalar_out", bufs=14))
         gathered = ctx.enter_context(tc.tile_pool(name="gathered", bufs=7))
-        turn = ctx.enter_context(tc.tile_pool(name="turn", bufs=27))
+        vector_out = ctx.enter_context(tc.tile_pool(name="vector_out", bufs=24))
         psum = ctx.enter_context(tc.psum_pool(name="psum", bufs=1))
 
         term_list = keep.tile([P, S // 16], U16, name="term_list")
@@ -65,19 +66,16 @@ def tile_list_term_query_topics_kernel(
         nc.sync.dma_start(query_list[:], offs2)
         nc.sync.dma_start(out=query_scale_table[ROW0:, :], in_=tab2_scales.rearrange("a q n -> (a q) n").bitcast(I32))
 
-        def load_query_words(a):
-            nc.sync.dma_start(out=query_table[a][:], in_=tab2_words[a].rearrange("p n t -> p (n t)").bitcast(I32))
+        def load_words(table, words):
+            nc.sync.dma_start(out=table[:], in_=words.rearrange("p n t -> p (n t)").bitcast(I32))
 
-        def load_term_words(a):
-            nc.sync.dma_start(out=term_table[a][:], in_=tab_words[a].rearrange("p n t -> p (n t)").bitcast(I32))
-
-        load_query_words(0)
+        load_words(query_table[0], tab2_words[0])
         nc.sync.dma_start(out=idf_rows[0:2, :], in_=idf.rearrange("(b i) -> b i", b=2))
-        load_term_words(0)
-        load_term_words(1)
+        load_words(term_table[0], tab_words[0])
+        load_words(term_table[1], tab_words[1])
 
         term_codes = {}
-        first_pass = keep.tile([P, S2], U32, name="query_codes0", align_bytes=64)
+        first_pass = keep.tile([P, S2], U32, name="first_pass", align_bytes=64)
         query_codes = {(0, lo): first_pass[:, lo : lo + CHUNK] for lo in range(0, S2, CHUNK)}
         term_scales = keep.tile([P, S], U8, name="term_scales", align_bytes=64)
         query_scales = keep.tile([P, S2], U8, name="query_scales", align_bytes=64)
@@ -94,12 +92,18 @@ def tile_list_term_query_topics_kernel(
             source, target = ROW0 + 16 * a + 4 * q, 32 * q + PLANE[a]
             nc.sync.dma_start(out=planes[a][target : target + 4, :], in_=planes[0][source : source + 4, :])
 
-        for q in range(3):
-            move_rows(0, q)
-        for q in range(3):
-            move_rows(1, q)
-        load_query_words(1)
+        for a in range(2):
+            for q in range(3):
+                move_rows(a, q)
+        load_words(query_table[1], tab2_words[1])
         move_rows(1, 3)
+
+        def gather_term_words(a, b):
+            term_codes[a, b] = gathered.tile([P, PACK, P], U32, name="gathered", align_bytes=64)
+            nc.vector.tensor_copy(
+                term_codes[a, b][:].rearrange("p t m -> p m t"),
+                term_table[a][:].bitcast(U32).indirect(term_list[:, PASS // 16 * b : PASS // 16 * (b + 1)]),
+            )
 
         def gather_second_pass(lo, hi):
             codes = gathered.tile([P, hi - lo], U32, name="gathered", align_bytes=64)
@@ -107,27 +111,20 @@ def tile_list_term_query_topics_kernel(
             for c in range(lo, hi, CHUNK):
                 query_codes[1, c] = codes[:, c - lo : c - lo + CHUNK]
 
-        def gather_term_words(a, b):
-            term_codes[a, b] = gathered.tile([P, PACK, P], U32, name="gathered", align_bytes=64)
-            nc.vector.tensor_copy(
-                term_codes[a, b][:].rearrange("p t m -> p m t"),
-                term_table[a][:].bitcast(U32).indirect(term_list[:, 32 * b : 32 * (b + 1)]),
-            )
-
         nc.vector.tensor_copy(first_pass[:], query_table[0][:].bitcast(U32).indirect(query_list[:]))
         for a in range(2):
             for b in range(2):
                 gather_term_words(a, b)
-        gather_second_pass(0, 256)
-        gather_second_pass(256, 512)
-        gather_second_pass(512, 1024)
+        gather_second_pass(0, CHUNK)
+        gather_second_pass(CHUNK, 2 * CHUNK)
+        gather_second_pass(2 * CHUNK, S2)
 
         wd_raw = [keep.tile([P, PACK, N], F32, name=f"wd_raw{b}", align_bytes=64) for b in range(2)]
         w4_codes = keep.tile([P, 2, 2 * N // 4], I32, name="w4_codes", align_bytes=64)
         w4_planes = keep.tile([P, 2, N // 4], I32, name="w4_planes", align_bytes=64)
         nc.vector.memset(w4_planes[:], 0)
-        nc.sync.dma_start(out=wd_raw[0][:], in_=wd[0:PASS, :].rearrange("(p t) n -> p t n", t=PACK))
-        nc.sync.dma_start(out=wd_raw[1][:], in_=wd[PASS : 2 * PASS, :].rearrange("(p t) n -> p t n", t=PACK))
+        for b in range(2):
+            nc.sync.dma_start(out=wd_raw[b][:], in_=wd[PASS * b : PASS * (b + 1), :].rearrange("(p t) n -> p t n", t=PACK))
         nc.sync.dma_start(out=w4_codes[:], in_=w4_words.bitcast(I32).rearrange("b p c -> p b c"))
         for q in range(4):
             nc.sync.dma_start(
@@ -137,19 +134,16 @@ def tile_list_term_query_topics_kernel(
 
         wd_codes = {}
         wd_planes = [keep.tile([P, N], U8, name=f"wd_planes{b}", align_bytes=64) for b in range(2)]
-        z_tiles = {0: [], 1: []}
-
-        def new_z_codes(b, lo, hi):
-            z_tiles[b].append((lo, hi, turn.tile([P, hi - lo], U32, name="turn", align_bytes=64)))
-
-        def z_codes(b, lo, hi):
-            first, last, tile = [entry for entry in z_tiles[b] if entry[0] <= lo and hi <= entry[1]][0]
-            return tile[:, lo - first : hi - first].bitcast(FP8X4)
-
+        z_codes = {}
         z_planes = [keep.tile([P, S2], U8, name=f"z_planes{b}", align_bytes=64) for b in range(2)]
 
         def bank_tile(number, parts):
             return psum.tile([P, parts, BANK // parts], F32, name="bank", tag=f"bank{number}")
+
+        def result_tile(shape, on_vector):
+            if on_vector:
+                return vector_out.tile(shape, F32, name="vector_out", align_bytes=64)
+            return scalar_out.tile(shape, F32, name="scalar_out", align_bytes=64)
 
         idf_bank = bank_tile(7, PACK)
         for t in range(PACK):
@@ -163,12 +157,12 @@ def tile_list_term_query_topics_kernel(
 
         def quantize_wd(grouped, b, lo, hi):
             if lo == 0:
-                wd_codes[b] = turn.tile([P, N], U32, name="turn", align_bytes=64)
+                wd_codes[b] = vector_out.tile([P, N], U32, name="vector_out", align_bytes=64)
             nc.vector.quantize_mx(
                 out=wd_codes[b][:, lo:hi].bitcast(FP8X4), scales=wd_planes[b][:, lo:hi], in_=grouped[:].rearrange("p n t -> p (n t)")
             )
 
-        def match_pass(banks, a, b, lo, slots=range(PACK), first_pass_number=0):
+        def match_pass(banks, a, b, lo, slots, opening_pass):
             plane = planes[a][PLANE[a] :, :].bitcast(U8)
             for t in slots:
                 first = PASS * b + P * t
@@ -178,24 +172,21 @@ def tile_list_term_query_topics_kernel(
                     lhsT_scale=plane[:, first : first + P],
                     rhs=query_codes[a, lo].bitcast(FP8X4),
                     rhs_scale=plane[:, S + lo : S + lo + CHUNK],
-                    start=(a == first_pass_number and t % 2 == 0),
-                    stop=(a != first_pass_number and t % 2 == 1),
+                    start=(a == opening_pass and t % 2 == 0),
+                    stop=(a != opening_pass and t % 2 == 1),
                 )
 
-        def match_bank(banks, u, b, lo):
-            for a in range(2):
-                match_pass(banks, a, b, lo, range(2 * u, 2 * u + 2))
-
-        def matches(numbers, b, lo):
+        def matches(numbers, b, lo, opening_pass=0):
             banks = [bank_tile(number, 2) for number in numbers]
             for u in range(2):
-                match_bank(banks, u, b, lo)
+                for a in (opening_pass, 1 - opening_pass):
+                    match_pass(banks, a, b, lo, (2 * u, 2 * u + 1), opening_pass)
             return banks
 
-        def new_kept(on_vector=False):
+        def new_kept(on_vector):
             if on_vector:
                 return shared.tile([P, 2, CHUNK, 2], F32, name="kept", tag="kept", bufs=2, align_bytes=64)
-            return work.tile([P, 2, CHUNK, 2], F32, name="work", align_bytes=64)
+            return scalar_out.tile([P, 2, CHUNK, 2], F32, name="scalar_out", align_bytes=64)
 
         def drop_negatives(kept, banks, u, on_vector):
             side_by_side = banks[u][:].rearrange("p e j -> p j e")
@@ -205,194 +196,188 @@ def tile_list_term_query_topics_kernel(
                 nc.scalar.activation(out=kept[:, u, :, :], in_=side_by_side, func=ACT.Relu)
 
         def saturate(kept, lo, hi):
-            logs = work.tile([P, hi - lo, 2, 2], F32, name="work", align_bytes=64)
+            logs = scalar_out.tile([P, hi - lo, 2, 2], F32, name="scalar_out", align_bytes=64)
             nc.scalar.activation(out=logs[:], in_=kept[:, :, lo:hi, :].rearrange("p u j e -> p j u e"), func=ACT.Ln, bias=one[:])
             return logs
 
-        def weigh(logs, b, from_psum=False):
+        def weigh(logs, weights):
             width = logs.shape[1]
-            z = turn.tile([P, width, PACK], BF16, name="turn", align_bytes=64)
-            source = idf_bank[:, :, b] if from_psum else idf_sb[:, b, :]
-            weights = source.unsqueeze(1).to_broadcast([P, width, PACK])
-            nc.vector.tensor_tensor(out=z[:], in0=logs[:, :, :, :].rearrange("p j u e -> p j (u e)"), in1=weights, op=ALU.mult)
+            z = vector_out.tile([P, width, PACK], BF16, name="vector_out", align_bytes=64)
+            nc.vector.tensor_tensor(
+                out=z[:], in0=logs[:].rearrange("p j u e -> p j (u e)"), in1=weights.unsqueeze(1).to_broadcast([P, width, PACK]), op=ALU.mult
+            )
             return z
 
-        def quantize_z(z, b, lo):
-            cols = slice(lo, lo + z.shape[1])
-            nc.vector.quantize_mx(out=z_codes(b, lo, lo + z.shape[1]), scales=z_planes[b][:, cols], in_=z[:].rearrange("p j t -> p (j t)"))
-
-        def packed_pass(acc, nt, b, lo, hi, start):
-            nc.tensor.matmul_mx(
-                out=acc,
-                lhsT=w4_codes[:, b, :].bitcast(U8)[:, 2 * P * nt : 2 * P * (nt + 1)].bitcast(FP4X4),
-                lhsT_scale=w4_planes[:, b, :].bitcast(U8)[:, P * nt : P * (nt + 1)],
-                rhs=z_codes(b, lo, hi),
-                rhs_scale=z_planes[b][:, lo:hi],
-                start=start,
-                stop=False,
+        def quantize_z(z, b, columns, lo):
+            hi = lo + z.shape[1]
+            if lo == columns[0]:
+                z_codes[b, columns] = vector_out.tile([P, columns[1] - columns[0]], U32, name="vector_out", align_bytes=64)
+            nc.vector.quantize_mx(
+                out=z_codes[b, columns][:, lo - columns[0] : hi - columns[0]].bitcast(FP8X4),
+                scales=z_planes[b][:, lo:hi],
+                in_=z[:].rearrange("p j t -> p (j t)"),
             )
 
-        def update_pass(acc, nt, b, lo, hi, stop):
+        def packed_pass(acc, nt, b, columns, opens):
+            lo, hi = columns
+            step = BANK if hi - lo == BANK else P
+            for c in range(0, hi - lo, step):
+                nc.tensor.matmul_mx(
+                    out=acc[:, c : c + step],
+                    lhsT=w4_codes[:, b, :].bitcast(U8)[:, 2 * P * nt : 2 * P * (nt + 1)].bitcast(FP4X4),
+                    lhsT_scale=w4_planes[:, b, :].bitcast(U8)[:, P * nt : P * (nt + 1)],
+                    rhs=z_codes[b, columns][:, c : c + step].bitcast(FP8X4),
+                    rhs_scale=z_planes[b][:, lo + c : lo + c + step],
+                    start=(opens and c == 0),
+                    stop=False,
+                )
+
+        def update_pass(acc, nt, b, columns, closes):
+            lo, hi = columns
             nc.tensor.matmul_mx(
-                out=acc,
+                out=acc[:, 0 : hi - lo],
                 lhsT=wd_codes[b][:, P * nt : P * (nt + 1)].bitcast(FP8X4),
                 lhsT_scale=wd_planes[b][:, P * nt : P * (nt + 1)],
-                rhs=z_codes(b, lo, hi),
+                rhs=z_codes[b, columns][:].bitcast(FP8X4),
                 rhs_scale=z_planes[b][:, lo:hi],
                 start=False,
-                stop=stop,
+                stop=closes,
             )
 
-        def topic_passes(sums, b, lo, hi, origin=None, packed=True, update=True, closes=True):
-            origin = lo if origin is None else origin
-            width = hi - lo
-            step = width if width == BANK else P
-            tiles = N // P // len(sums)
+        def half_passes(sums, b, tiles):
+            for nt in tiles:
+                packed_pass(sums[nt][:, 0, :], nt, b, HALF, b == 0)
+            for nt in tiles:
+                update_pass(sums[nt][:, 0, :], nt, b, HALF, b == 1)
+
+        def narrow_passes(sums, b, columns):
+            per_bank = TILES // len(sums)
             for i, bank in enumerate(sums):
-                for e in range(tiles):
-                    if packed:
-                        for c in range(lo, hi, step):
-                            packed_pass(bank[:, e, c - origin : c - origin + step], tiles * i + e, b, c, c + step, b == 0 and e == 0 and c == origin)
-                    if update:
-                        update_pass(bank[:, e, lo - origin : hi - origin], tiles * i + e, b, lo, hi, b == 1 and e == tiles - 1 and closes)
+                for e in range(per_bank):
+                    packed_pass(bank[:, e, :], per_bank * i + e, b, columns, b == 0 and e == 0)
+                    update_pass(bank[:, e, :], per_bank * i + e, b, columns, b == 1 and e == per_bank - 1)
 
-        def store(sums, first, lo, hi, tiles, on_vector):
-            for i, bank in enumerate(sums, first):
-                if on_vector:
-                    result = turn.tile([P, tiles, hi - lo], F32, name="turn", align_bytes=64)
-                else:
-                    result = work.tile([P, tiles, hi - lo], F32, name="work", align_bytes=64)
-                if on_vector:
-                    nc.vector.tensor_copy(out=result[:], in_=bank[:, 0:tiles, 0 : hi - lo])
-                else:
-                    nc.scalar.copy(out=result[:], in_=bank[:, 0:tiles, 0 : hi - lo])
-                rows = out[P * tiles * i : P * tiles * (i + 1), lo:hi]
-                nc.sync.dma_start(out=rows.rearrange("(e p) j -> p e j", p=P), in_=result[:])
-
-        def half_pass(kind, bank, nt, b):
-            if kind == "packed":
-                packed_pass(bank[:, 0, :], nt, b, 0, BANK, b == 0)
+        def empty(result, sums, on_vector):
+            if on_vector:
+                nc.vector.tensor_copy(out=result, in_=sums)
             else:
-                update_pass(bank[:, 0, :], nt, b, 0, BANK, b == 1)
+                nc.scalar.copy(out=result, in_=sums)
 
-        match0 = [bank_tile(u, 2) for u in range(2)]
-        match2 = [bank_tile(2 + u, 2) for u in range(2)]
+        def send(result, nt, columns):
+            rows = out[P * nt : P * (nt + result.shape[1]), columns[0] : columns[1]]
+            nc.sync.dma_start(out=rows.rearrange("(e p) j -> p e j", p=P), in_=result[:])
+
+        def store(sums, nt, columns, on_vector):
+            result = result_tile([P, sums.shape[1], columns[1] - columns[0]], on_vector)
+            empty(result[:], sums, on_vector)
+            send(result, nt, columns)
+
+        match0 = [bank_tile(number, 2) for number in (0, 1)]
+        match2 = [bank_tile(number, 2) for number in (2, 3)]
+        match1 = [bank_tile(number, 2) for number in (4, 5)]
         for a in range(2):
-            match_pass(match0, a, 0, 0)
-            match_pass(match2, a, 1, 0)
-        match1 = [bank_tile(4 + u, 2) for u in range(2)]
-        for u in range(2):
-            for a in (1, 0):
-                match_pass(match1, a, 0, CHUNK, range(2 * u, 2 * u + 2), first_pass_number=1)
+            match_pass(match0, a, 0, 0, range(PACK), 0)
+            match_pass(match2, a, 1, 0, range(PACK), 0)
+            match_pass(match1, a, 0, CHUNK, range(PACK), 0)
 
-        kept0 = new_kept()
+        kept0 = new_kept(False)
         drop_negatives(kept0, match0, 0, False)
-        match3 = [bank_tile(number, 2) for number in (6, 0)]
-        for u in range(2):
-            for a in (1, 0):
-                match_pass(match3, a, 1, CHUNK, range(2 * u, 2 * u + 2), first_pass_number=1)
+        match3 = matches((6, 0), 1, CHUNK, opening_pass=1)
         drop_negatives(kept0, match0, 1, False)
-        kept2 = new_kept()
+        kept2 = new_kept(False)
         drop_negatives(kept2, match2, 0, False)
-        wd_rounded0 = shared.tile([P, N, PACK], BF16, name="wd_rounded0", tag="query_table1", align_bytes=64)
-        round_wd(wd_rounded0, 0, 0, N)
-        wd_rounded1a = keep.tile([P, N // 2, PACK], BF16, name="wd_rounded1a", align_bytes=64)
-        round_wd(wd_rounded1a, 1, 0, N // 2)
+
+        wd_first = shared.tile([P, N, PACK], BF16, name="wd_first", tag="query_table1", align_bytes=64)
+        round_wd(wd_first, 0, 0, N)
+        wd_second_left = keep.tile([P, N // 2, PACK], BF16, name="wd_second_left", align_bytes=64)
+        round_wd(wd_second_left, 1, 0, N // 2)
         logs0 = saturate(kept0, 0, CHUNK)
         kept1 = new_kept(True)
         drop_negatives(kept1, match1, 0, True)
         drop_negatives(kept1, match1, 1, True)
-        match4 = matches((1, 2), 0, 512)
+        match4 = matches((1, 2), 0, QUARTER[0])
         drop_negatives(kept2, match2, 1, True)
         kept3 = new_kept(True)
         drop_negatives(kept3, match3, 0, True)
         drop_negatives(kept3, match3, 1, True)
-        match5 = matches((3, 4), 0, 768)
-        match6 = matches((5, 6), 1, 512)
+        match5 = matches((3, 4), 1, QUARTER[0])
+        match6 = matches((5, 6), 0, EIGHTH[0])
         logs1 = saturate(kept1, 0, CHUNK)
-        z0 = weigh(logs0, 0, True)
-        z1 = weigh(logs1, 0, True)
-        kept4 = new_kept()
+        z0 = weigh(logs0, idf_bank[:, :, 0])
+        z1 = weigh(logs1, idf_bank[:, :, 0])
+        kept4 = new_kept(False)
         drop_negatives(kept4, match4, 0, False)
         logs2 = saturate(kept2, 0, CHUNK)
         drop_negatives(kept4, match4, 1, False)
-        new_z_codes(0, 0, 512)
-        quantize_z(z0, 0, 0)
-        quantize_z(z1, 0, 256)
-        quantize_wd(wd_rounded0, 0, 0, N)
-        wd_rounded1b = shared.tile([P, N // 2, PACK], BF16, name="wd_rounded1b", tag="query_table1", align_bytes=64)
-        round_wd(wd_rounded1b, 1, N // 2, N)
+        quantize_z(z0, 0, HALF, 0)
+        quantize_z(z1, 0, HALF, CHUNK)
+        quantize_wd(wd_first, 0, 0, N)
+
+        wd_second_right = shared.tile([P, N // 2, PACK], BF16, name="wd_second_right", tag="query_table1", align_bytes=64)
+        round_wd(wd_second_right, 1, N // 2, N)
         logs3 = saturate(kept3, 0, CHUNK)
-        kept5 = new_kept()
+        kept5 = new_kept(False)
         drop_negatives(kept5, match5, 0, False)
-        sums_half = [bank_tile(nt, 1) for nt in range(4)]
-        for kind in ("packed", "update"):
-            for nt in range(3):
-                half_pass(kind, sums_half[nt], nt, 0)
-        for kind in ("packed", "update"):
-            half_pass(kind, sums_half[3], 3, 0)
-        z2 = weigh(logs2, 1, True)
-        z3 = weigh(logs3, 1, True)
+        sums_half = [bank_tile(nt, 1) for nt in range(TILES)]
+        half_passes(sums_half, 0, (0, 1, 2))
+        half_passes(sums_half, 0, (3,))
+        z2 = weigh(logs2, idf_bank[:, :, 1])
+        z3 = weigh(logs3, idf_bank[:, :, 1])
         drop_negatives(kept5, match5, 1, False)
         logs4 = saturate(kept4, 0, CHUNK)
-        match7 = matches((4, 7), 1, 768)
-        new_z_codes(1, 0, 512)
-        quantize_z(z2, 1, 0)
-        quantize_z(z3, 1, 256)
-        quantize_wd(wd_rounded1a, 1, 0, N // 2)
-        quantize_wd(wd_rounded1b, 1, N // 2, N)
-        for pair in range(2):
-            for kind in ("packed", "update"):
-                for nt in (2 * pair, 2 * pair + 1):
-                    half_pass(kind, sums_half[nt], nt, 1)
-        kept6 = new_kept()
+        match7 = matches((4, 7), 1, EIGHTH[0])
+        quantize_z(z2, 1, HALF, 0)
+        quantize_z(z3, 1, HALF, CHUNK)
+        quantize_wd(wd_second_left, 1, 0, N // 2)
+        quantize_wd(wd_second_right, 1, N // 2, N)
+        half_passes(sums_half, 1, (0, 1))
+        half_passes(sums_half, 1, (2, 3))
+
+        kept6 = new_kept(False)
         drop_negatives(kept6, match6, 0, False)
         logs5 = saturate(kept5, 0, CHUNK)
         drop_negatives(kept6, match6, 1, False)
-        z4 = weigh(logs4, 0)
-        first_result = turn.tile([P, BANK], F32, name="turn", align_bytes=64)
-        nc.vector.tensor_copy(out=first_result[:, 0:CHUNK], in_=sums_half[0][:, 0, 0:CHUNK])
-        new_z_codes(0, 512, 768)
-        quantize_z(z4, 0, 512)
-        sums_quarter = [bank_tile(5 + i, 2) for i in range(2)]
-        topic_passes(sums_quarter, 0, 512, 768)
-        z5 = weigh(logs5, 0)
-        nc.vector.tensor_copy(out=first_result[:, CHUNK:BANK], in_=sums_half[0][:, 0, CHUNK:BANK])
-        nc.sync.dma_start(out=out[0:P, 0:BANK], in_=first_result[:])
-        new_z_codes(0, 768, 1024)
-        quantize_z(z5, 0, 768)
-        kept7 = new_kept()
+        z4 = weigh(logs4, idf_sb[:, 0, :])
+        first_result = result_tile([P, 1, BANK], True)
+        empty(first_result[:, 0, 0:CHUNK], sums_half[0][:, 0, 0:CHUNK], True)
+        quantize_z(z4, 0, QUARTER, QUARTER[0])
+        sums_quarter = [bank_tile(number, 2) for number in (5, 6)]
+        narrow_passes(sums_quarter, 0, QUARTER)
+        z5 = weigh(logs5, idf_sb[:, 1, :])
+        empty(first_result[:, 0, CHUNK:BANK], sums_half[0][:, 0, CHUNK:BANK], True)
+        send(first_result, 0, HALF)
+        quantize_z(z5, 1, QUARTER, QUARTER[0])
+        narrow_passes(sums_quarter, 1, QUARTER)
+
+        kept7 = new_kept(False)
         drop_negatives(kept7, match7, 0, False)
-        logs6a = saturate(kept6, 0, P)
+        logs6_eighth = saturate(kept6, 0, P)
         drop_negatives(kept7, match7, 1, False)
-        logs6b = saturate(kept6, P, CHUNK)
-        sums_eighth = [bank_tile(4, 4)]
+        logs6_last = saturate(kept6, P, CHUNK)
+        sums_eighth = [bank_tile(4, TILES)]
         sums_last = [bank_tile(number, 2) for number in (0, 7)]
-        topic_passes(sums_eighth, 0, 768, 896)
-        topic_passes(sums_last, 0, 896, 1024)
-        store(sums_half[1:2], 1, 0, 512, 1, False)
-        logs7a = saturate(kept7, 0, P)
-        store(sums_half[2:3], 2, 0, 512, 1, False)
-        logs7b = saturate(kept7, P, CHUNK)
-        store(sums_half[3:4], 3, 0, 512, 1, False)
-        z6a = weigh(logs6a, 1)
-        z6b = weigh(logs6b, 1)
-        new_z_codes(1, 512, 640)
-        quantize_z(z6a, 1, 512)
-        topic_passes(sums_quarter, 1, 512, 640, closes=False)
-        z7a = weigh(logs7a, 1)
-        new_z_codes(1, 640, 768)
-        quantize_z(z6b, 1, 640)
-        topic_passes(sums_quarter, 1, 640, 768, origin=512)
-        new_z_codes(1, 768, 896)
-        quantize_z(z7a, 1, 768)
-        topic_passes(sums_eighth, 1, 768, 896)
-        z7b = weigh(logs7b, 1)
-        new_z_codes(1, 896, 1024)
-        quantize_z(z7b, 1, 896)
-        topic_passes(sums_last, 1, 896, 1024)
-        store(sums_quarter[0:1], 0, 512, 768, 2, False)
-        store(sums_quarter[1:2], 1, 512, 768, 2, False)
-        store(sums_eighth, 0, 768, 896, 4, True)
-        store(sums_last[0:1], 0, 896, 1024, 2, False)
-        store(sums_last[1:2], 1, 896, 1024, 2, True)
+        store(sums_half[1][:], 1, HALF, False)
+        logs7_eighth = saturate(kept7, 0, P)
+        store(sums_half[2][:], 2, HALF, False)
+        logs7_last = saturate(kept7, P, CHUNK)
+        store(sums_half[3][:], 3, HALF, False)
+        store(sums_quarter[0][:], 0, QUARTER, False)
+        z6_eighth = weigh(logs6_eighth, idf_sb[:, 0, :])
+        z6_last = weigh(logs6_last, idf_sb[:, 0, :])
+        quantize_z(z6_eighth, 0, EIGHTH, EIGHTH[0])
+        narrow_passes(sums_eighth, 0, EIGHTH)
+        z7_eighth = weigh(logs7_eighth, idf_sb[:, 1, :])
+        quantize_z(z6_last, 0, LAST, LAST[0])
+        narrow_passes(sums_last, 0, LAST)
+        quantize_z(z7_eighth, 1, EIGHTH, EIGHTH[0])
+        narrow_passes(sums_eighth, 1, EIGHTH)
+        z7_last = weigh(logs7_last, idf_sb[:, 1, :])
+        store(sums_quarter[1][:, 1:2, :], 3, QUARTER, True)
+        store(sums_quarter[1][:, 0:1, :], 2, QUARTER, False)
+        quantize_z(z7_last, 1, LAST, LAST[0])
+        narrow_passes(sums_last, 1, LAST)
+        store(sums_eighth[0][:], 0, EIGHTH, True)
+        last_result = result_tile([P, TILES, P], True)
+        empty(last_result[:, 0:2, :], sums_last[0][:, :, 0:P], False)
+        empty(last_result[:, 2:4, :], sums_last[1][:, :, 0:P], True)
+        send(last_result, 0, LAST)

from contextlib import ExitStack

import concourse.mybir as mybir
from concourse.masks import make_identity

K, T, S, T2, S2, N = 1024, 4096, 1024, 2048, 1024, 512
FLOPS = 2 * K * S * S2 + 2 * 2 * S * N * S2

F32 = mybir.dt.float32
BF16 = mybir.dt.bfloat16
I32 = mybir.dt.int32
U32 = mybir.dt.uint32
U16 = mybir.dt.uint16
U8 = mybir.dt.uint8
FP8X4 = mybir.dt.float8_e4m3fn_x4
FP4X4 = mybir.dt.float4_e2m1fn_x4
ACT = mybir.ActivationFunctionType
ALU = mybir.AluOpType

P = 128
PACK = 4
PASS = P * PACK
BANK = 512
CHUNK = 256
TILES = N // P
ROW0 = 96
PLANE = (12, 0)
HALF, QUARTER, EIGHTH, LAST = (0, 512), (512, 768), (768, 896), (896, 1024)


def tile_list_term_query_topics_kernel(
    tc, tab_words, tab_scales, tab2_words, tab2_scales, offs, offs2, idf, w4_words, w4_scales, wd, out
):
    nc = tc.nc
    with ExitStack() as ctx:
        keep = ctx.enter_context(tc.tile_pool(name="keep", bufs=1))
        shared = ctx.enter_context(tc.tile_pool(name="shared", bufs=1))
        scalar_out = ctx.enter_context(tc.tile_pool(name="scalar_out", bufs=14))
        gathered = ctx.enter_context(tc.tile_pool(name="gathered", bufs=7))
        vector_out = ctx.enter_context(tc.tile_pool(name="vector_out", bufs=24))
        psum = ctx.enter_context(tc.psum_pool(name="psum", bufs=1))

        term_list = keep.tile([P, S // 16], U16, name="term_list")
        query_list = keep.tile([P, S2 // 16], U16, name="query_list")
        term_scale_table = keep.tile([P, T // 4], I32, name="term_scale_table", align_bytes=64)
        query_scale_table = keep.tile([P, T2 // 4], I32, name="query_scale_table", align_bytes=64)
        planes = [keep.tile([P, (S + S2) // 4], I32, name=f"planes{a}", align_bytes=64) for a in range(2)]
        idf_sb = keep.tile([P, 2, PACK], F32, name="idf_sb", align_bytes=64)
        one = keep.tile([P, 1], F32, name="one")
        warm = keep.tile([P, 1], F32, name="warm")
        query_table = [shared.tile([P, T2], I32, name=f"query_table{a}", tag=f"query_table{a}", align_bytes=64) for a in range(2)]
        term_table = [shared.tile([P, T], I32, name=f"term_table{a}", align_bytes=64) for a in range(2)]

        nc.vector.memset(one[:], 1.0)
        nc.scalar.activation(out=warm[:], in_=one[:], func=ACT.Ln)
        for table in (term_scale_table, query_scale_table):
            nc.vector.memset(table[0:ROW0, :], 0)
        nc.vector.memset(planes[1][:], 0)
        idf_rows = keep.tile([P, PASS], F32, name="idf_rows", align_bytes=64)
        identity = keep.tile([P, P], F32, name="identity", align_bytes=64)
        nc.gpsimd.memset(idf_rows[:], 0.0)
        make_identity(nc, identity[:])

        nc.sync.dma_start(term_list[:], offs)
        nc.sync.dma_start(out=term_scale_table[ROW0:, :], in_=tab_scales.rearrange("a q n -> (a q) n").bitcast(I32))
        nc.sync.dma_start(query_list[:], offs2)
        nc.sync.dma_start(out=query_scale_table[ROW0:, :], in_=tab2_scales.rearrange("a q n -> (a q) n").bitcast(I32))

        def load_words(table, words):
            nc.sync.dma_start(out=table[:], in_=words.rearrange("p n t -> p (n t)").bitcast(I32))

        load_words(query_table[0], tab2_words[0])
        nc.sync.dma_start(out=idf_rows[0:2, :], in_=idf.rearrange("(b i) -> b i", b=2))
        load_words(term_table[0], tab_words[0])
        load_words(term_table[1], tab_words[1])

        term_codes = {}
        first_pass = keep.tile([P, S2], U32, name="first_pass", align_bytes=64)
        query_codes = {(0, lo): first_pass[:, lo : lo + CHUNK] for lo in range(0, S2, CHUNK)}
        term_scales = keep.tile([P, S], U8, name="term_scales", align_bytes=64)
        query_scales = keep.tile([P, S2], U8, name="query_scales", align_bytes=64)

        nc.vector.tensor_copy(term_scales[:], term_scale_table[:].bitcast(U8).indirect(term_list[:]))
        nc.vector.tensor_copy(query_scales[:], query_scale_table[:].bitcast(U8).indirect(query_list[:]))
        nc.vector.tensor_copy(
            planes[0][:, 0 : S // 4].bitcast(U8).rearrange("p (b t m) -> p b t m", b=2, t=PACK),
            term_scales[:].rearrange("p (b m t) -> p b t m", b=2, t=PACK),
        )
        nc.vector.tensor_copy(planes[0][:, S // 4 :], query_scales[:].bitcast(I32))

        def move_rows(a, q):
            source, target = ROW0 + 16 * a + 4 * q, 32 * q + PLANE[a]
            nc.sync.dma_start(out=planes[a][target : target + 4, :], in_=planes[0][source : source + 4, :])

        for a in range(2):
            for q in range(3):
                move_rows(a, q)
        load_words(query_table[1], tab2_words[1])
        move_rows(1, 3)

        def gather_term_words(a, b):
            term_codes[a, b] = gathered.tile([P, PACK, P], U32, name="gathered", align_bytes=64)
            nc.vector.tensor_copy(
                term_codes[a, b][:].rearrange("p t m -> p m t"),
                term_table[a][:].bitcast(U32).indirect(term_list[:, PASS // 16 * b : PASS // 16 * (b + 1)]),
            )

        def gather_second_pass(lo, hi):
            codes = gathered.tile([P, hi - lo], U32, name="gathered", align_bytes=64)
            nc.vector.tensor_copy(codes[:], query_table[1][:].bitcast(U32).indirect(query_list[:, lo // 16 : hi // 16]))
            for c in range(lo, hi, CHUNK):
                query_codes[1, c] = codes[:, c - lo : c - lo + CHUNK]

        nc.vector.tensor_copy(first_pass[:], query_table[0][:].bitcast(U32).indirect(query_list[:]))
        for a in range(2):
            for b in range(2):
                gather_term_words(a, b)
        gather_second_pass(0, CHUNK)
        gather_second_pass(CHUNK, 2 * CHUNK)
        gather_second_pass(2 * CHUNK, S2)

        wd_raw = [keep.tile([P, PACK, N], F32, name=f"wd_raw{b}", align_bytes=64) for b in range(2)]
        w4_codes = keep.tile([P, 2, 2 * N // 4], I32, name="w4_codes", align_bytes=64)
        w4_planes = keep.tile([P, 2, N // 4], I32, name="w4_planes", align_bytes=64)
        nc.vector.memset(w4_planes[:], 0)
        for b in range(2):
            nc.sync.dma_start(out=wd_raw[b][:], in_=wd[PASS * b : PASS * (b + 1), :].rearrange("(p t) n -> p t n", t=PACK))
        nc.sync.dma_start(out=w4_codes[:], in_=w4_words.bitcast(I32).rearrange("b p c -> p b c"))
        for q in range(4):
            nc.sync.dma_start(
                out=w4_planes[32 * q : 32 * q + 4, :, :],
                in_=w4_scales[:, 4 * q : 4 * q + 4, :].bitcast(I32).rearrange("b r c -> r b c"),
            )

        wd_codes = {}
        wd_planes = [keep.tile([P, N], U8, name=f"wd_planes{b}", align_bytes=64) for b in range(2)]
        z_codes = {}
        z_planes = [keep.tile([P, S2], U8, name=f"z_planes{b}", align_bytes=64) for b in range(2)]

        def bank_tile(number, parts):
            return psum.tile([P, parts, BANK // parts], F32, name="bank", tag=f"bank{number}")

        def result_tile(shape, on_vector):
            if on_vector:
                return vector_out.tile(shape, F32, name="vector_out", align_bytes=64)
            return scalar_out.tile(shape, F32, name="scalar_out", align_bytes=64)

        idf_bank = bank_tile(7, PACK)
        for t in range(PACK):
            nc.tensor.transpose(idf_bank[:, t, :], idf_rows[:, t:PASS:PACK], identity[:])
        nc.scalar.copy(out=idf_sb[:].rearrange("p b t -> p t b"), in_=idf_bank[:, :, 0:2])

        def round_wd(grouped, b, lo, hi):
            nc.gpsimd.tensor_scalar(
                out=grouped[:], in0=wd_raw[b][:, :, lo:hi].rearrange("p t n -> p n t"), scalar1=1.0, scalar2=0.0, op0=ALU.mult, op1=ALU.add
            )

        def quantize_wd(grouped, b, lo, hi):
            if lo == 0:
                wd_codes[b] = vector_out.tile([P, N], U32, name="vector_out", align_bytes=64)
            nc.vector.quantize_mx(
                out=wd_codes[b][:, lo:hi].bitcast(FP8X4), scales=wd_planes[b][:, lo:hi], in_=grouped[:].rearrange("p n t -> p (n t)")
            )

        def match_pass(banks, a, b, lo, slots, opening_pass):
            plane = planes[a][PLANE[a] :, :].bitcast(U8)
            for t in slots:
                first = PASS * b + P * t
                nc.tensor.matmul_mx(
                    out=banks[t // 2][:, t % 2, :],
                    lhsT=term_codes[a, b][:, t, :].bitcast(FP8X4),
                    lhsT_scale=plane[:, first : first + P],
                    rhs=query_codes[a, lo].bitcast(FP8X4),
                    rhs_scale=plane[:, S + lo : S + lo + CHUNK],
                    start=(a == opening_pass and t % 2 == 0),
                    stop=(a != opening_pass and t % 2 == 1),
                )

        def matches(numbers, b, lo, opening_pass=0):
            banks = [bank_tile(number, 2) for number in numbers]
            for u in range(2):
                for a in (opening_pass, 1 - opening_pass):
                    match_pass(banks, a, b, lo, (2 * u, 2 * u + 1), opening_pass)
            return banks

        def new_kept(on_vector):
            if on_vector:
                return shared.tile([P, 2, CHUNK, 2], F32, name="kept", tag="kept", bufs=2, align_bytes=64)
            return scalar_out.tile([P, 2, CHUNK, 2], F32, name="scalar_out", align_bytes=64)

        def drop_negatives(kept, banks, u, on_vector):
            side_by_side = banks[u][:].rearrange("p e j -> p j e")
            if on_vector:
                nc.vector.tensor_scalar(out=kept[:, u, :, :], in0=side_by_side, scalar1=0.0, scalar2=None, op0=ALU.max)
            else:
                nc.scalar.activation(out=kept[:, u, :, :], in_=side_by_side, func=ACT.Relu)

        def saturate(kept, lo, hi):
            logs = scalar_out.tile([P, hi - lo, 2, 2], F32, name="scalar_out", align_bytes=64)
            nc.scalar.activation(out=logs[:], in_=kept[:, :, lo:hi, :].rearrange("p u j e -> p j u e"), func=ACT.Ln, bias=one[:])
            return logs

        def weigh(logs, weights):
            width = logs.shape[1]
            z = vector_out.tile([P, width, PACK], BF16, name="vector_out", align_bytes=64)
            nc.vector.tensor_tensor(
                out=z[:], in0=logs[:].rearrange("p j u e -> p j (u e)"), in1=weights.unsqueeze(1).to_broadcast([P, width, PACK]), op=ALU.mult
            )
            return z

        def quantize_z(z, b, columns, lo):
            hi = lo + z.shape[1]
            if lo == columns[0]:
                z_codes[b, columns] = vector_out.tile([P, columns[1] - columns[0]], U32, name="vector_out", align_bytes=64)
            nc.vector.quantize_mx(
                out=z_codes[b, columns][:, lo - columns[0] : hi - columns[0]].bitcast(FP8X4),
                scales=z_planes[b][:, lo:hi],
                in_=z[:].rearrange("p j t -> p (j t)"),
            )

        def packed_pass(acc, nt, b, columns, opens):
            lo, hi = columns
            step = BANK if hi - lo == BANK else P
            for c in range(0, hi - lo, step):
                nc.tensor.matmul_mx(
                    out=acc[:, c : c + step],
                    lhsT=w4_codes[:, b, :].bitcast(U8)[:, 2 * P * nt : 2 * P * (nt + 1)].bitcast(FP4X4),
                    lhsT_scale=w4_planes[:, b, :].bitcast(U8)[:, P * nt : P * (nt + 1)],
                    rhs=z_codes[b, columns][:, c : c + step].bitcast(FP8X4),
                    rhs_scale=z_planes[b][:, lo + c : lo + c + step],
                    start=(opens and c == 0),
                    stop=False,
                )

        def update_pass(acc, nt, b, columns, closes):
            lo, hi = columns
            nc.tensor.matmul_mx(
                out=acc[:, 0 : hi - lo],
                lhsT=wd_codes[b][:, P * nt : P * (nt + 1)].bitcast(FP8X4),
                lhsT_scale=wd_planes[b][:, P * nt : P * (nt + 1)],
                rhs=z_codes[b, columns][:].bitcast(FP8X4),
                rhs_scale=z_planes[b][:, lo:hi],
                start=False,
                stop=closes,
            )

        def half_passes(sums, b, tiles):
            for nt in tiles:
                packed_pass(sums[nt][:, 0, :], nt, b, HALF, b == 0)
            for nt in tiles:
                update_pass(sums[nt][:, 0, :], nt, b, HALF, b == 1)

        def narrow_passes(sums, b, columns):
            per_bank = TILES // len(sums)
            for i, bank in enumerate(sums):
                for e in range(per_bank):
                    packed_pass(bank[:, e, :], per_bank * i + e, b, columns, b == 0 and e == 0)
                    update_pass(bank[:, e, :], per_bank * i + e, b, columns, b == 1 and e == per_bank - 1)

        def empty(result, sums, on_vector):
            if on_vector:
                nc.vector.tensor_copy(out=result, in_=sums)
            else:
                nc.scalar.copy(out=result, in_=sums)

        def send(result, nt, columns):
            rows = out[P * nt : P * (nt + result.shape[1]), columns[0] : columns[1]]
            nc.sync.dma_start(out=rows.rearrange("(e p) j -> p e j", p=P), in_=result[:])

        def store(sums, nt, columns, on_vector):
            result = result_tile([P, sums.shape[1], columns[1] - columns[0]], on_vector)
            empty(result[:], sums, on_vector)
            send(result, nt, columns)

        match0 = [bank_tile(number, 2) for number in (0, 1)]
        match2 = [bank_tile(number, 2) for number in (2, 3)]
        match1 = [bank_tile(number, 2) for number in (4, 5)]
        for a in range(2):
            match_pass(match0, a, 0, 0, range(PACK), 0)
            match_pass(match2, a, 1, 0, range(PACK), 0)
            match_pass(match1, a, 0, CHUNK, range(PACK), 0)

        kept0 = new_kept(False)
        drop_negatives(kept0, match0, 0, False)
        match3 = matches((6, 0), 1, CHUNK, opening_pass=1)
        drop_negatives(kept0, match0, 1, False)
        kept2 = new_kept(False)
        drop_negatives(kept2, match2, 0, False)

        wd_first = shared.tile([P, N, PACK], BF16, name="wd_first", tag="query_table1", align_bytes=64)
        round_wd(wd_first, 0, 0, N)
        wd_second_left = keep.tile([P, N // 2, PACK], BF16, name="wd_second_left", align_bytes=64)
        round_wd(wd_second_left, 1, 0, N // 2)
        logs0 = saturate(kept0, 0, CHUNK)
        kept1 = new_kept(True)
        drop_negatives(kept1, match1, 0, True)
        drop_negatives(kept1, match1, 1, True)
        match4 = matches((1, 2), 0, QUARTER[0])
        drop_negatives(kept2, match2, 1, True)
        kept3 = new_kept(True)
        drop_negatives(kept3, match3, 0, True)
        drop_negatives(kept3, match3, 1, True)
        match5 = matches((3, 4), 1, QUARTER[0])
        match6 = matches((5, 6), 0, EIGHTH[0])
        logs1 = saturate(kept1, 0, CHUNK)
        z0 = weigh(logs0, idf_bank[:, :, 0])
        z1 = weigh(logs1, idf_bank[:, :, 0])
        kept4 = new_kept(False)
        drop_negatives(kept4, match4, 0, False)
        logs2 = saturate(kept2, 0, CHUNK)
        drop_negatives(kept4, match4, 1, False)
        quantize_z(z0, 0, HALF, 0)
        quantize_z(z1, 0, HALF, CHUNK)
        quantize_wd(wd_first, 0, 0, N)

        wd_second_right = shared.tile([P, N // 2, PACK], BF16, name="wd_second_right", tag="query_table1", align_bytes=64)
        round_wd(wd_second_right, 1, N // 2, N)
        logs3 = saturate(kept3, 0, CHUNK)
        kept5 = new_kept(False)
        drop_negatives(kept5, match5, 0, False)
        sums_half = [bank_tile(nt, 1) for nt in range(TILES)]
        half_passes(sums_half, 0, (0, 1, 2))
        half_passes(sums_half, 0, (3,))
        z2 = weigh(logs2, idf_bank[:, :, 1])
        z3 = weigh(logs3, idf_bank[:, :, 1])
        drop_negatives(kept5, match5, 1, False)
        logs4 = saturate(kept4, 0, CHUNK)
        match7 = matches((4, 7), 1, EIGHTH[0])
        quantize_z(z2, 1, HALF, 0)
        quantize_z(z3, 1, HALF, CHUNK)
        quantize_wd(wd_second_left, 1, 0, N // 2)
        quantize_wd(wd_second_right, 1, N // 2, N)
        half_passes(sums_half, 1, (0, 1))
        half_passes(sums_half, 1, (2, 3))

        kept6 = new_kept(False)
        drop_negatives(kept6, match6, 0, False)
        logs5 = saturate(kept5, 0, CHUNK)
        drop_negatives(kept6, match6, 1, False)
        z4 = weigh(logs4, idf_sb[:, 0, :])
        first_result = result_tile([P, 1, BANK], True)
        empty(first_result[:, 0, 0:CHUNK], sums_half[0][:, 0, 0:CHUNK], True)
        quantize_z(z4, 0, QUARTER, QUARTER[0])
        sums_quarter = [bank_tile(number, 2) for number in (5, 6)]
        narrow_passes(sums_quarter, 0, QUARTER)
        z5 = weigh(logs5, idf_sb[:, 1, :])
        empty(first_result[:, 0, CHUNK:BANK], sums_half[0][:, 0, CHUNK:BANK], True)
        send(first_result, 0, HALF)
        quantize_z(z5, 1, QUARTER, QUARTER[0])
        narrow_passes(sums_quarter, 1, QUARTER)

        kept7 = new_kept(False)
        drop_negatives(kept7, match7, 0, False)
        logs6_eighth = saturate(kept6, 0, P)
        drop_negatives(kept7, match7, 1, False)
        logs6_last = saturate(kept6, P, CHUNK)
        sums_eighth = [bank_tile(4, TILES)]
        sums_last = [bank_tile(number, 2) for number in (0, 7)]
        store(sums_half[1][:], 1, HALF, False)
        logs7_eighth = saturate(kept7, 0, P)
        store(sums_half[2][:], 2, HALF, False)
        logs7_last = saturate(kept7, P, CHUNK)
        store(sums_half[3][:], 3, HALF, False)
        store(sums_quarter[0][:], 0, QUARTER, False)
        z6_eighth = weigh(logs6_eighth, idf_sb[:, 0, :])
        z6_last = weigh(logs6_last, idf_sb[:, 0, :])
        quantize_z(z6_eighth, 0, EIGHTH, EIGHTH[0])
        narrow_passes(sums_eighth, 0, EIGHTH)
        z7_eighth = weigh(logs7_eighth, idf_sb[:, 1, :])
        quantize_z(z6_last, 0, LAST, LAST[0])
        narrow_passes(sums_last, 0, LAST)
        quantize_z(z7_eighth, 1, EIGHTH, EIGHTH[0])
        narrow_passes(sums_eighth, 1, EIGHTH)
        z7_last = weigh(logs7_last, idf_sb[:, 1, :])
        store(sums_quarter[1][:, 1:2, :], 3, QUARTER, True)
        store(sums_quarter[1][:, 0:1, :], 2, QUARTER, False)
        quantize_z(z7_last, 1, LAST, LAST[0])
        narrow_passes(sums_last, 1, LAST)
        store(sums_eighth[0][:], 0, EIGHTH, True)
        last_result = result_tile([P, TILES, P], True)
        empty(last_result[:, 0:2, :], sums_last[0][:, :, 0:P], False)
        empty(last_result[:, 2:4, :], sums_last[1][:, :, 0:P], True)
        send(last_result, 0, LAST)
